import numpy as np
import ml_dtypes


def mxq(x, axis, fmt="e4m3"):
    dtype, down = {"e4m3": (ml_dtypes.float8_e4m3fn, 7), "e5m2": (ml_dtypes.float8_e5m2, 14)}[fmt]
    v = np.moveaxis(np.asarray(x, np.float32).astype(ml_dtypes.bfloat16).astype(np.float64), axis, -1)
    blocks = v.reshape(v.shape[:-1] + (-1, 32))
    amax = np.abs(blocks).max(-1, keepdims=True)
    byte = np.maximum(np.where(amax > 0, np.frexp(amax)[1] - 1 + 127, 0) - down, 1)
    scale = np.exp2(byte - 127.0)
    codes = (blocks / scale).astype(np.float32).astype(dtype).astype(np.float64)
    return np.moveaxis((codes * scale).reshape(v.shape), -1, axis)


WIDE = False


def mx_kscale(k):
    if not WIDE:
        return np.ones(k)
    levels = np.array([10, -10, 5, -5, 0])
    if k % 512:
        return np.exp2(np.random.permutation(np.resize(levels, k // 32))).repeat(32)
    a = np.empty((k // 512, 16))
    for p in range(k // 512):
        a[p, :8] = np.random.permutation(np.resize(levels, 8))
        for g in range(8):
            far = levels[np.abs(levels - a[p, g]) >= 10]
            a[p, g + 8] = far[np.random.randint(len(far))]
    return np.exp2(a.ravel()).repeat(32)


BF16 = ml_dtypes.bfloat16


def bf(x):
    return np.asarray(x, np.float32).astype(BF16)


def f64(x):
    return np.asarray(x).astype(np.float64)


E2M1 = np.array([0.0, 0.5, 1.0, 1.5, 2.0, 3.0, 4.0, 6.0, -0.0, -0.5, -1.0, -1.5, -2.0, -3.0, -4.0, -6.0])


def pack_weight(w, fmt):
    k, n = w.shape
    w = f64(bf(w)).reshape(k // 32, 32, n)
    amax = np.abs(w).max(1)
    if fmt == "e4m3":
        byte = np.frexp(amax)[1] - 1 + 127 - 7
    else:
        mant, ex = np.frexp(amax / 6.0)
        byte = np.where(mant > 0.5, ex, ex - 1) + 127
    byte = np.clip(np.where(amax > 0, byte, 1), 1, 254)
    scaled = (w * np.exp2(127.0 - byte)[:, None, :]).reshape(k, n).astype(np.float32)
    by_word = np.ascontiguousarray(scaled.reshape(k // 512, 128, 4, n).transpose(0, 1, 3, 2))
    if fmt == "e4m3":
        words = by_word.astype(ml_dtypes.float8_e4m3fn).view(np.uint8)
    else:
        c = by_word.astype(ml_dtypes.float4_e2m1fn).view(np.uint8) & 0xF
        words = c[..., 0::2] | (c[..., 1::2] << 4)
    return np.ascontiguousarray(words), np.ascontiguousarray(byte.astype(np.uint8).reshape(k // 512, 16, n))


def unpack_weight(words, scales, fmt):
    g, p, n, _ = words.shape
    if fmt == "e4m3":
        vals = np.ascontiguousarray(words).view(ml_dtypes.float8_e4m3fn).astype(np.float64)
    else:
        nib = np.empty((g, p, n, 4), np.uint8)
        nib[..., 0::2] = words & 0xF
        nib[..., 1::2] = words >> 4
        vals = E2M1[nib]
    vals = vals * np.repeat(np.exp2(scales.astype(np.float64) - 127.0), 8, axis=1)[..., None]
    return vals.transpose(0, 1, 3, 2).reshape(g * 512, n)
def pack4(w):
    words, scales = pack_weight(w, "e2m1")
    return words.reshape(words.shape[0], 128, -1), scales


def unpack4(words, scales):
    return unpack_weight(words.reshape(words.shape[0], 128, -1, 2), scales, "e2m1")


T, DX, DZ, DG, E, L = 1024, 1024, 1024, 1024, 1024, 3


def modulator(z, gates, wh_words, wh_scales, bh):
    c = np.sum(f64(gates).T[:, :, None] * f64(z), axis=0)
    return (mxq(c, 1, "e4m3") @ unpack4(wh_words, wh_scales)) + f64(bh)[None, :]


def draw0():
    a, b, u = mx_kscale(DZ), mx_kscale(DG), mx_kscale(T)
    x = bf(np.random.standard_normal((T, DX)) * u[:, None])
    z = bf(np.random.standard_normal((L, T, DZ)) * a)
    gates = bf(np.random.standard_normal((T, L)) * 0.6)
    wh_words, wh_scales = pack4(np.random.standard_normal((DZ, E)) / np.sqrt(DZ) / a[:, None])
    bh = bf(np.random.standard_normal(E) * 0.4)
    wp_words, wp_scales = pack4((np.random.standard_normal((E, DG)) / np.sqrt(DG) / b[None, :]).T)
    g = bf(np.random.standard_normal((T, DG)) * b[None, :] / u[:, None])
    return {
        "x": x,
        "z": z,
        "gates": gates,
        "wh_words": wh_words,
        "wh_scales": wh_scales,
        "bh": bh,
        "wp_words": wp_words,
        "wp_scales": wp_scales,
        "g": g,
    }


def core(x, z, gates, wh_words, wh_scales, bh, wp_words, wp_scales, g):
    m = modulator(z, gates, wh_words, wh_scales, bh)
    p = mxq(f64(g), 1, "e4m3") @ unpack4(wp_words, wp_scales)
    s = p * m
    root_t = np.sqrt(x.shape[0])
    dwq = (mxq(f64(x), 0, "e4m3").T @ mxq(s, 0, "e4m3")) / root_t
    return dwq


def e4m3fn_bytes(y):
    return np.clip(np.asarray(y, np.float64), -448.0, 448.0).astype(np.float32).astype(ml_dtypes.float8_e4m3fn).view(np.uint8)


def e4m3fn_values(b):
    return np.asarray(b, np.uint8).view(ml_dtypes.float8_e4m3fn).astype(np.float64)


def setup_inputs():
    d = draw0()
    x0 = np.asarray(d['x']).astype(np.float64)
    s = (np.max(np.abs(x0), axis=(1,), keepdims=True) / 448.0).astype(np.float32)
    out = {}
    for k, v in d.items():
        if k == 'x':
            out['x_bytes'] = e4m3fn_bytes(x0 / s.astype(np.float64))
            out['x_scale'] = s
        else:
            out[k] = v
    return out


def reference(x_bytes, x_scale, z, gates, wh_words, wh_scales, bh, wp_words, wp_scales, g):
    return core(e4m3fn_values(x_bytes) * x_scale.astype(np.float64), z, gates, wh_words, wh_scales, bh, wp_words, wp_scales, g)

@@ -1,0 +1,365 @@
+from contextlib import ExitStack
+
+import concourse.mybir as mybir
+from concourse.masks import make_identity
+
+F32 = mybir.dt.float32
+BF16 = mybir.dt.bfloat16
+U32 = mybir.dt.uint32
+I32 = mybir.dt.int32
+U8 = mybir.dt.uint8
+FP8 = mybir.dt.float8_e4m3fn
+FP8X4 = mybir.dt.float8_e4m3fn_x4
+FP4X4 = mybir.dt.float4_e2m1fn_x4
+MULT = mybir.AluOpType.mult
+ADD = mybir.AluOpType.add
+COPY = mybir.ActivationFunctionType.Copy
+
+T = 1024
+D = 1024
+L = 3
+P = 128
+J = 4
+H = 2
+A = 2
+EB = 128
+NEB = D // EB
+
+FLOPS = 3 * 2 * T * D * D + 2 * L * T * D + 2 * T * D
+
+
+def tile_focalmodulationqueryweightgrad_w4_kernel(
+    tc, x_bytes, x_scale, z, gates, wh_words, wh_scales, bh, wp_words, wp_scales, g, out
+):
+    nc = tc.nc
+    with ExitStack() as ctx:
+        keep = ctx.enter_context(tc.tile_pool(name="keep", bufs=1))
+        work = ctx.enter_context(tc.tile_pool(name="work", bufs=2))
+        psum = ctx.enter_context(tc.psum_pool(name="psum", bufs=1))
+
+        gate_sb = keep.tile([P, H, J * L], BF16, name="gate_sb")
+        nc.scalar.dma_start(out=gate_sb[:], in_=gates.rearrange("(h m j) l -> m h (j l)", h=H, j=J))
+        xs_sb = keep.tile([P, H, J], F32, name="xs_sb")
+        nc.scalar.dma_start(out=xs_sb[:], in_=x_scale.rearrange("(h m j) o -> m h (j o)", h=H, j=J))
+
+        ident = keep.tile([P, P], F32, name="ident")
+        make_identity(nc, ident[:])
+        bh_row = keep.tile([P, D], BF16, name="bh_row")
+        nc.vector.memset(bh_row[:], 0.0)
+        w_sc = keep.tile([P, 4, D], U8, name="w_sc", align_bytes=64)
+        nc.vector.memset(w_sc[:].rearrange("p s n -> p (s n)").bitcast(I32), 0)
+        ident_bf = keep.tile([P, P], BF16, name="ident_bf")
+        nc.vector.tensor_copy(out=ident_bf[:], in_=ident[:])
+
+        def load_bias():
+            nc.sync.dma_start(out=bh_row[0:1, :], in_=bh.rearrange("(o n) -> o n", o=1))
+
+        ones = keep.tile([P, P], BF16, name="ones")
+        nc.vector.memset(ones[:], 1.0)
+
+        g_view = g.rearrange("(h m j) k -> h m (j k)", h=H, j=J)
+        z_view = z.rearrange("l (h m j) d -> h m l (j d)", h=H, j=J)
+        x_view = x_bytes.rearrange("(h m j) n -> h m (j n)", h=H, j=J)
+        g_sb = {}
+        z_sb = {}
+        x_sb = {}
+
+        def load_g(h):
+            for q in range(2):
+                t = keep.tile([P, 2, D], BF16, name=f"g_sb{h}{q}", align_bytes=64)
+                nc.sync.dma_start(out=t[:].rearrange("p j k -> p (j k)"), in_=g_view[h][:, 2048 * q : 2048 * (q + 1)])
+                g_sb[h, q] = t
+
+        def load_z(h, j):
+            t = keep.tile([P, L, D], BF16, name=f"z_sb{h}{j}", align_bytes=64)
+            nc.sync.dma_start(out=t[:], in_=z_view[h][:, :, D * j : D * (j + 1)])
+            z_sb[h, j] = t
+
+        def load_x(h):
+            t = keep.tile([P, J * D], U8, name=f"x_sb{h}", align_bytes=64)
+            nc.sync.dma_start(out=t[:], in_=x_view[h])
+            x_sb[h] = t
+
+        w_sb = {}
+
+        def load_w(key, words, scales, slot):
+            t = keep.tile([P, A, 2 * D], U8, name=f"w_{key}", align_bytes=64)
+            nc.sync.dma_start(out=t[:].bitcast(I32), in_=words.bitcast(I32).rearrange("a p n -> p a n"))
+            sv = scales.bitcast(I32).rearrange("a (q r) n -> r q a n", r=4)
+            for r in range(4):
+                nc.sync.dma_start(out=w_sc[r:P:32, slot : slot + A, :].bitcast(I32), in_=sv[r])
+            w_sb[key] = (t, slot)
+
+        for j in range(J):
+            load_z(0, j)
+        load_w("h", wh_words, wh_scales, 2)
+        load_bias()
+        load_g(0)
+        load_w("p", wp_words, wp_scales, 0)
+        load_x(0)
+        for j in range(J):
+            load_z(1, j)
+        load_g(1)
+        load_x(1)
+
+        def pe_levels(h, j):
+            return 3 if (h, j) in () else 2
+
+        diag = {}
+
+        def make_diag(h, j):
+            for l in range(pe_levels(h, j)):
+                t = keep.tile([P, P], BF16, name=f"diag{h}{j}{l}")
+                c = j * L + l
+                (nc.vector if (h, j) in ((0, 0), (0, 1), (0, 2), (0, 3)) else nc.gpsimd).tensor_scalar(
+                    out=t[:], in0=ident_bf[:], scalar1=gate_sb[:, h, c : c + 1], scalar2=0.0, op0=MULT, op1=ADD
+                )
+                diag[h, j, l] = t
+
+        for h in range(H):
+            for j in range(J):
+                make_diag(h, j)
+
+        bh_bc = keep.tile([P, D], F32, name="bh_bc")
+
+        def spread_bias():
+            for e in range(2):
+                b = psum.tile([P, 512], F32, name=f"bias{e}", tag="mp", bufs=4)
+                nc.tensor.matmul(b[:], lhsT=ones[:], rhs=bh_row[:, 512 * e : 512 * (e + 1)], start=True, stop=True)
+                nc.scalar.copy(out=bh_bc[:, 512 * e : 512 * (e + 1)], in_=b[:])
+
+        codes = {}
+        kin = {}
+        for key in ("g", "c"):
+            for h in range(H):
+                q = keep.tile([P, 2, A, 256], U32, name=f"{key}q{h}", align_bytes=64)
+                s = keep.tile([P, 2, A, 256], U8, name=f"{key}s{h}", align_bytes=64)
+                codes[key, h] = (q, s)
+        for key in ("x", "s"):
+            for h in range(H):
+                q = keep.tile([P, D], U32, name=f"{key}q{h}", align_bytes=64)
+                s = keep.tile([P, D], U8, name=f"{key}s{h}", align_bytes=64)
+                codes[key, h] = (q, s)
+
+        def transpose_tile(key, h, j, src):
+            if j % 2 == 0:
+                kin[key, h, j // 2] = work.tile([P, A, 256, 4], BF16, name=f"kin_{key}{h}{j}", tag="kin", bufs=3, align_bytes=64)
+            dst = kin[key, h, j // 2]
+            words = src.bitcast(F32)
+            bank = psum.tile([P, A, 2, P], F32, name=f"tp_{key}{h}{j}", tag="tp", bufs=2)
+            for a in range(A):
+                for u in range(2):
+                    if key == "c":
+                        cols = words[:, 256 * a + P * u : 256 * a + P * (u + 1)]
+                    else:
+                        cols = words[:, 256 * a + u : 256 * (a + 1) : 2]
+                    nc.tensor.transpose(bank[:, a, u, :], cols, ident[:])
+            jj = j % 2
+            nc.scalar.copy(
+                out=dst[:, :, P * jj : P * (jj + 1), :].bitcast(F32), in_=bank[:].rearrange("p a u m -> p a m u")
+            )
+
+        def quantise_k(key, h, q):
+            cq, cs = codes[key, h]
+            src = kin[key, h, q]
+            nc.vector.quantize_mx(
+                out=cq[:, q, :, :].rearrange("p a n -> p (a n)").bitcast(FP8X4),
+                scales=cs[:, q, :, :].rearrange("p a n -> p (a n)"),
+                in_=src[:].rearrange("p a n t -> p (a n t)"),
+            )
+
+        def g_tile(h, j):
+            transpose_tile("g", h, j, g_sb[h, j // 2][:, j % 2, :])
+
+        dg = {}
+        cw = {}
+
+        def c_levels01(h, j):
+            zt = z_sb[h, j]
+            for a in range(A):
+                b = psum.tile([P, 512], F32, name=f"dg{h}{j}{a}", tag="dg", bufs=2)
+                n = pe_levels(h, j)
+                for l in range(n):
+                    nc.tensor.matmul(
+                        b[:],
+                        lhsT=diag[h, j, l][:],
+                        rhs=zt[:, l, 512 * a : 512 * (a + 1)],
+                        start=(l == 0),
+                        stop=(l == n - 1),
+                    )
+                dg[h, j, a] = b
+
+        def c_level2(h, j):
+            zt = z_sb[h, j]
+            t = work.tile([P, D], BF16, name=f"cw{h}{j}", tag="cw", bufs=3)
+            c = j * L + 2
+            for a in range(A):
+                if pe_levels(h, j) == L:
+                    nc.scalar.copy(out=t[:, 512 * a : 512 * (a + 1)], in_=dg[h, j, a][:])
+                    continue
+                for u in range(2):
+                    nc.vector.scalar_tensor_tensor(
+                        out=t[:, 512 * a + 256 * u : 512 * a + 256 * (u + 1)].rearrange("p (k e) -> p k e", e=2),
+                        in0=zt[:, 2, 512 * a : 512 * (a + 1)].rearrange("p (k u e) -> p u k e", u=2, e=2)[:, u],
+                        scalar=gate_sb[:, h, c : c + 1],
+                        in1=dg[h, j, a][:].rearrange("p (k u e) -> p u k e", u=2, e=2)[:, u],
+                        op0=MULT,
+                        op1=ADD,
+                    )
+            cw[h, j] = t
+
+        def c_tile(h, j):
+            transpose_tile("c", h, j, cw[h, j][:])
+
+        mp = {}
+
+        def product(tag, key, wkey, h, e):
+            cq, cs = codes[key, h]
+            wt, slot = w_sb[wkey]
+            b = psum.tile([P, J, EB], F32, name=f"{wkey}_{h}{e}", tag="mp", bufs=4)
+            for j in range(J):
+                for a in range(A):
+                    nc.tensor.matmul_mx(
+                        b[:, j, :],
+                        lhsT=cq[:, j // 2, a, P * (j % 2) : P * (j % 2 + 1)].bitcast(FP8X4),
+                        lhsT_scale=cs[:, j // 2, a, P * (j % 2) : P * (j % 2 + 1)],
+                        rhs=wt[:, a, 2 * EB * e : 2 * EB * (e + 1)].bitcast(FP4X4),
+                        rhs_scale=w_sc[:, slot + a, EB * e : EB * (e + 1)],
+                        start=(a == 0),
+                        stop=(a == A - 1),
+                    )
+            mp[wkey, h, e] = b
+
+        mb = {}
+        sin = {}
+
+        def bias_m(h, e):
+            t = work.tile([P, EB, J], F32, name=f"mb{h}{e}", tag="mb", bufs=3)
+            nc.vector.tensor_tensor(
+                out=t[:],
+                in0=mp["h", h, e][:].rearrange("p j n -> p n j"),
+                in1=bh_bc[:, EB * e : EB * (e + 1)].unsqueeze(2).to_broadcast([P, EB, J]),
+                op=ADD,
+            )
+            mb[h, e] = t
+
+        def times_p(h, e):
+            if e % 2 == 0:
+                sin[h, e // 2] = work.tile([P, 2 * EB, J], BF16, name=f"sin{h}{e}", tag="sin", bufs=3, align_bytes=64)
+            t = sin[h, e // 2]
+            k = e % 2
+            nc.vector.tensor_tensor(
+                out=t[:, EB * k : EB * (k + 1), :],
+                in0=mp["p", h, e][:].rearrange("p j n -> p n j"),
+                in1=mb[h, e][:],
+                op=MULT,
+            )
+
+        def quantise_s(h, q):
+            sq, ss = codes["s", h]
+            nc.vector.quantize_mx(
+                out=sq[:, 256 * q : 256 * (q + 1)].bitcast(FP8X4),
+                scales=ss[:, 256 * q : 256 * (q + 1)],
+                in_=sin[h, q][:].rearrange("p n t -> p (n t)"),
+            )
+
+        xw = {}
+
+        def widen_x(h, j):
+            if j == 0:
+                xw[h] = work.tile([P, J, D], BF16, name=f"xw{h}", tag="xw", bufs=2)
+            nc.scalar.activation(
+                out=xw[h][:, j, :],
+                in_=x_sb[h][:, D * j : D * (j + 1)].bitcast(FP8),
+                func=COPY,
+                scale=xs_sb[:, h, j : j + 1],
+            )
+
+        xi = {}
+
+        def interleave_x(h, q):
+            t = work.tile([P, 512, J], BF16, name=f"xi{h}{q}", tag="xi", bufs=2, align_bytes=64)
+            src = xw[h][:, :, 512 * q : 512 * (q + 1)].rearrange("p j n -> p n j")
+            nc.scalar.copy(out=t[:], in_=src)
+            xi[h, q] = t
+
+        def quantise_x(h, q):
+            xq, xs = codes["x", h]
+            nc.vector.quantize_mx(
+                out=xq[:, 512 * q : 512 * (q + 1)].bitcast(FP8X4),
+                scales=xs[:, 512 * q : 512 * (q + 1)],
+                in_=xi[h, q][:].rearrange("p n t -> p (n t)"),
+            )
+
+        def out_tile(e, r, tag, bufs, engine):
+            b = psum.tile([P, 512], F32, name=f"o{e}{r}", tag=tag, bufs=bufs)
+            for h in range(H):
+                xq, xs = codes["x", h]
+                sq, ss = codes["s", h]
+                nc.tensor.matmul_mx(
+                    b[:],
+                    lhsT=xq[:, P * r : P * (r + 1)].bitcast(FP8X4),
+                    lhsT_scale=xs[:, P * r : P * (r + 1)],
+                    rhs=sq[:, 512 * e : 512 * (e + 1)].bitcast(FP8X4),
+                    rhs_scale=ss[:, 512 * e : 512 * (e + 1)],
+                    start=(h == 0),
+                    stop=(h == H - 1),
+                )
+            t = work.tile([P, 512], F32, name=f"ob{e}{r}", tag="ob", bufs=12)
+            if engine == 0:
+                nc.scalar.activation(out=t[:], in_=b[:], func=COPY, scale=1.0 / 32.0)
+            else:
+                nc.vector.tensor_scalar(out=t[:], in0=b[:], scalar1=1.0 / 32.0, scalar2=None, op0=MULT)
+            nc.sync.dma_start(out=out[P * r : P * (r + 1), 512 * e : 512 * (e + 1)], in_=t[:])
+
+        for j in range(J):
+            c_levels01(0, j)
+            if j > 0:
+                c_tile(0, j - 1)
+            c_level2(0, j)
+            if j == 2:
+                quantise_k("c", 0, 0)
+        g_tile(0, 0)
+        c_tile(0, 3)
+        g_tile(0, 1)
+        quantise_k("c", 0, 1)
+        spread_bias()
+        quantise_k("g", 0, 0)
+        g_tile(0, 2)
+        g_tile(0, 3)
+        product("m", "c", "h", 0, 0)
+        bias_m(0, 0)
+        quantise_k("g", 0, 1)
+
+        steps = [
+            lambda: (widen_x(0, 0), widen_x(0, 1)),
+            lambda: (widen_x(0, 2), widen_x(0, 3), c_levels01(1, 0)),
+            lambda: (c_level2(1, 0), interleave_x(0, 0), c_levels01(1, 1)),
+            lambda: (c_tile(1, 0), c_level2(1, 1), c_levels01(1, 2), interleave_x(0, 1), quantise_x(0, 0)),
+            lambda: (c_tile(1, 1), c_level2(1, 2), c_levels01(1, 3)),
+            lambda: (c_tile(1, 2), c_level2(1, 3), quantise_k("c", 1, 0), g_tile(1, 0), quantise_x(0, 1)),
+            lambda: (c_tile(1, 3), g_tile(1, 1), g_tile(1, 2), quantise_k("g", 1, 0), quantise_k("c", 1, 1)),
+            lambda: (g_tile(1, 3), widen_x(1, 0), widen_x(1, 1), quantise_k("g", 1, 1)),
+        ]
+        for i in range(H * NEB):
+            h, e = i // NEB, i % NEB
+            if i + 1 < H * NEB:
+                product("m", "c", "h", (i + 1) // NEB, (i + 1) % NEB)
+            product("p", "g", "p", h, e)
+            if h == 0:
+                steps[e]()
+            if i + 1 < H * NEB:
+                bias_m((i + 1) // NEB, (i + 1) % NEB)
+            times_p(h, e)
+            if e % 2 == 1:
+                quantise_s(h, e // 2)
+            if h == 1 and e in (0, 1):
+                widen_x(1, e + 2)
+            if h == 1 and e in (2, 3):
+                interleave_x(1, e - 2)
+            if h == 1 and e in (4, 5):
+                quantise_x(1, e - 4)
+        for r in range(8):
+            out_tile(0, r, "tp" if r % 2 else "dg", 2, 0)
+        for r in range(8):
+            out_tile(1, r, "mp", 4, r % 2 if r >= 6 else 0)

@@ -22,8 +22,10 @@ P = 128
 J = 4
 H = 2
 A = 2
+U = 4
+NT = 32
 EB = 128
-NEB = D // EB
+WIDE = 512
 
 FLOPS = 3 * 2 * T * D * D + 2 * L * T * D + 2 * T * D
 
@@ -36,44 +38,68 @@ def tile_focalmodulationqueryweightgrad_w4_kernel(
         keep = ctx.enter_context(tc.tile_pool(name="keep", bufs=1))
         work = ctx.enter_context(tc.tile_pool(name="work", bufs=2))
         psum = ctx.enter_context(tc.psum_pool(name="psum", bufs=1))
+        ctx.enter_context(tc.manual_schedule())
 
-        gate_sb = keep.tile([P, H, J * L], BF16, name="gate_sb")
-        nc.scalar.dma_start(out=gate_sb[:], in_=gates.rearrange("(h m j) l -> m h (j l)", h=H, j=J))
-        xs_sb = keep.tile([P, H, J], F32, name="xs_sb")
-        nc.scalar.dma_start(out=xs_sb[:], in_=x_scale.rearrange("(h m j) o -> m h (j o)", h=H, j=J))
-
-        ident = keep.tile([P, P], F32, name="ident")
-        make_identity(nc, ident[:])
+        raw_gates = keep.tile([P, H, 48], BF16, name="raw_gates")
         bh_row = keep.tile([P, D], BF16, name="bh_row")
-        nc.vector.memset(bh_row[:], 0.0)
-        w_sc = keep.tile([P, 4, D], U8, name="w_sc", align_bytes=64)
-        nc.vector.memset(w_sc[:].rearrange("p s n -> p (s n)").bitcast(I32), 0)
-        ident_bf = keep.tile([P, P], BF16, name="ident_bf")
-        nc.vector.tensor_copy(out=ident_bf[:], in_=ident[:])
-
-        def load_bias():
-            nc.sync.dma_start(out=bh_row[0:1, :], in_=bh.rearrange("(o n) -> o n", o=1))
-
+        w_sc = keep.tile([P, 2 * A, D], U8, name="w_sc", align_bytes=64)
+        ident = keep.tile([P, P], BF16, name="ident")
         ones = keep.tile([P, P], BF16, name="ones")
-        nc.vector.memset(ones[:], 1.0)
+        block = keep.tile([P, NT], F32, name="block")
+        table = keep.tile([P, H * U * J + 1, NT], BF16, name="table")
+        xs_sb = keep.tile([P, H, J], F32, name="xs_sb")
+        bh_bc = keep.tile([P, D], BF16, name="bh_bc")
 
-        g_view = g.rearrange("(h m j) k -> h m (j k)", h=H, j=J)
-        z_view = z.rearrange("l (h m j) d -> h m l (j d)", h=H, j=J)
+        def constants():
+            nc.vector.memset(raw_gates[:], 0.0)
+            nc.vector.memset(w_sc[:].rearrange("p s n -> p (s n)").bitcast(I32), 0)
+            nc.vector.memset(bh_row[:], 0.0)
+            nc.vector.memset(ones[:], 1.0)
+            make_identity(nc, ident[:])
+            nc.vector.tensor_reduce(
+                out=block[:], in_=ident[:].rearrange("p (n l) -> p n l", l=L + 1), axis=mybir.AxisListType.X, op=ADD
+            )
+            nc.vector.tensor_copy(out=table[:, H * U * J, :], in_=ident[:, L : P : L + 1])
+
+        def load_gates(queue):
+            rows = gates.rearrange("(h n r) l -> n h (r l)", h=H, r=U * J)
+            for l in range(L):
+                queue.dma_start(out=raw_gates[l : P : L + 1, :, 0:46], in_=rows[:, :, l : l + 46])
+
+        def load_bias(queue):
+            queue.dma_start(out=bh_row[0:1, :], in_=bh.rearrange("(o n) -> o n", o=1))
+
+        def load_xs(queue):
+            queue.dma_start(out=xs_sb[:], in_=x_scale.rearrange("(h m j) o -> m h (j o)", h=H, j=J))
+
+        def make_table(h):
+            nc.vector.tensor_tensor(
+                out=table[:, U * J * h : U * J * (h + 1), :],
+                in0=block[:].unsqueeze(1).to_broadcast([P, U * J, NT]),
+                in1=raw_gates[:, h, 0:46:L].unsqueeze(2).to_broadcast([P, U * J, NT]),
+                op=MULT,
+            )
+
+        def spread_bias():
+            b = psum.tile([P, D], BF16, name="bias", tag="mp", bufs=4)
+            for e in range(2):
+                cols = slice(WIDE * e, WIDE * (e + 1))
+                nc.tensor.matmul(b[:, cols], lhsT=ones[:], rhs=bh_row[:, cols], start=True, stop=True)
+            nc.scalar.copy(out=bh_bc[:], in_=b[:])
+
+        rows_of = [z[l].rearrange("(h n u j) d -> h n u (j d)", h=H, u=U, j=J) for l in range(L)]
+        rows_of.append(g.rearrange("(h n u j) d -> h n u (j d)", h=H, u=U, j=J))
+        zg = {}
+
+        def load_zg(h, j0, count):
+            t = keep.tile([P, U, count * D], BF16, name=f"zg{h}{j0}", align_bytes=64)
+            for l in range(L + 1):
+                nc.sync.dma_start(out=t[l : P : L + 1, :, :], in_=rows_of[l][h][:, :, D * j0 : D * (j0 + count)])
+            for j in range(j0, j0 + count):
+                zg[h, j] = (t, D * (j - j0))
+
         x_view = x_bytes.rearrange("(h m j) n -> h m (j n)", h=H, j=J)
-        g_sb = {}
-        z_sb = {}
         x_sb = {}
-
-        def load_g(h):
-            for q in range(2):
-                t = keep.tile([P, 2, D], BF16, name=f"g_sb{h}{q}", align_bytes=64)
-                nc.sync.dma_start(out=t[:].rearrange("p j k -> p (j k)"), in_=g_view[h][:, 2048 * q : 2048 * (q + 1)])
-                g_sb[h, q] = t
-
-        def load_z(h, j):
-            t = keep.tile([P, L, D], BF16, name=f"z_sb{h}{j}", align_bytes=64)
-            nc.sync.dma_start(out=t[:], in_=z_view[h][:, :, D * j : D * (j + 1)])
-            z_sb[h, j] = t
 
         def load_x(h):
             t = keep.tile([P, J * D], U8, name=f"x_sb{h}", align_bytes=64)
@@ -81,285 +107,316 @@ def tile_focalmodulationqueryweightgrad_w4_kernel(
             x_sb[h] = t
 
         w_sb = {}
+        w_in = {"h": (wh_words, wh_scales, 0), "p": (wp_words, wp_scales, A)}
 
-        def load_w(key, words, scales, slot):
+        def load_w(key):
             t = keep.tile([P, A, 2 * D], U8, name=f"w_{key}", align_bytes=64)
-            nc.sync.dma_start(out=t[:].bitcast(I32), in_=words.bitcast(I32).rearrange("a p n -> p a n"))
-            sv = scales.bitcast(I32).rearrange("a (q r) n -> r q a n", r=4)
+            nc.sync.dma_start(out=t[:].bitcast(I32), in_=w_in[key][0].bitcast(I32).rearrange("a p n -> p a n"))
+            w_sb[key] = t
+
+        def load_w_scales(key, queue):
+            slot = w_in[key][2]
+            sv = w_in[key][1].bitcast(I32).rearrange("a (q r) n -> r q a n", r=4)
             for r in range(4):
-                nc.sync.dma_start(out=w_sc[r:P:32, slot : slot + A, :].bitcast(I32), in_=sv[r])
-            w_sb[key] = (t, slot)
+                queue.dma_start(out=w_sc[r:P:32, slot : slot + A, :].bitcast(I32), in_=sv[r])
 
-        for j in range(J):
-            load_z(0, j)
-        load_w("h", wh_words, wh_scales, 2)
-        load_bias()
-        load_g(0)
-        load_w("p", wp_words, wp_scales, 0)
-        load_x(0)
-        for j in range(J):
-            load_z(1, j)
-        load_g(1)
-        load_x(1)
+        turned = {}
+        kin = {}
+        cg = {}
 
-        def pe_levels(h, j):
-            return 3 if (h, j) in () else 2
+        def turn(h, j, a):
+            t, base = zg[h, j]
+            b = psum.tile([P, U * 4, 2, NT], BF16, name=f"gt{h}{j}{a}", tag="gt", bufs=4)
+            for u in range(U):
+                i = U * J * h + J * u + j
+                last = H * U * J
+                for k in range(4):
+                    first = base + WIDE * a + k
+                    nc.tensor.matmul(
+                        b[:, 4 * u + k, :, :],
+                        lhsT=t[:, u, first : base + WIDE * (a + 1) : 4],
+                        rhs=table[:, i : last + 1 : last - i, :],
+                        start=True,
+                        stop=True,
+                    )
+            turned[h, j, a] = b
 
-        diag = {}
+        def copy(engine, dst, src):
+            if engine == "s":
+                nc.scalar.copy(out=dst, in_=src)
+            elif engine == "v":
+                nc.vector.tensor_copy(out=dst, in_=src)
+            else:
+                nc.gpsimd.tensor_scalar(out=dst, in0=src, scalar1=1.0, scalar2=0.0, op0=MULT, op1=ADD)
 
-        def make_diag(h, j):
-            for l in range(pe_levels(h, j)):
-                t = keep.tile([P, P], BF16, name=f"diag{h}{j}{l}")
-                c = j * L + l
-                (nc.vector if (h, j) in ((0, 0), (0, 1), (0, 2), (0, 3)) else nc.gpsimd).tensor_scalar(
-                    out=t[:], in0=ident_bf[:], scalar1=gate_sb[:, h, c : c + 1], scalar2=0.0, op0=MULT, op1=ADD
+        def take(h, j, a, engine):
+            if a == 0:
+                kin[h, j] = work.tile([P, 2, A, NT, U * 4], BF16, name=f"kin{h}{j}", tag="kin", bufs=3, align_bytes=64)
+            copy(engine, kin[h, j][:, :, a, :, :], turned[h, j, a][:].rearrange("p s c n -> p c n s"))
+
+        def quantise(dst, scales, src):
+            nc.vector.quantize_mx(out=dst.bitcast(FP8X4), scales=scales, in_=src)
+
+        def quantise_cg(h, j):
+            q = keep.tile([P, 2 * A * P], U32, name=f"cgq{h}{j}", align_bytes=64)
+            s = keep.tile([P, 2 * A * P], U8, name=f"cgs{h}{j}", align_bytes=64)
+            quantise(q[:], s[:], kin[h, j][:].rearrange("p c a n s -> p (c a n s)"))
+            cg[h, j] = (q, s)
+
+        def passes(dst, key, h, j, col0, width):
+            q, s = cg[h, j]
+            slot = w_in[key][2]
+            for a in range(A):
+                cols = slice(P * (slot + a), P * (slot + a + 1))
+                nc.tensor.matmul_mx(
+                    dst,
+                    lhsT=q[:, cols].bitcast(FP8X4),
+                    lhsT_scale=s[:, cols],
+                    rhs=w_sb[key][:, a, 2 * col0 : 2 * (col0 + width)].bitcast(FP4X4),
+                    rhs_scale=w_sc[:, slot + a, col0 : col0 + width],
+                    start=(a == 0),
+                    stop=(a == A - 1),
                 )
-                diag[h, j, l] = t
 
-        for h in range(H):
+        mp = {}
+        mb = {}
+
+        def product0(key, j, e):
+            b = psum.tile([P, WIDE], F32, name=f"{key}0{j}{e}", tag="mp", bufs=4)
+            passes(b[:], key, 0, j, WIDE * e, WIDE)
+            mp[key, 0, j, e] = b
+
+        def bias0(j, e):
+            t = work.tile([P, WIDE], F32, name=f"mb0{j}{e}", tag="mb", bufs=3)
+            nc.vector.tensor_tensor(out=t[:], in0=mp["h", 0, j, e][:], in1=bh_bc[:, WIDE * e : WIDE * (e + 1)], op=ADD)
+            mb[0, j, e] = t
+
+        s_slots = keep.tile([P, J, D], BF16, name="s_slots")
+
+        def times0(j, e):
+            nc.vector.tensor_tensor(
+                out=s_slots[:, j, WIDE * e : WIDE * (e + 1)], in0=mp["p", 0, j, e][:], in1=mb[0, j, e][:], op=MULT
+            )
+
+        def product1(key, e):
+            b = psum.tile([P, J, EB], F32, name=f"{key}1{e}", tag="mp", bufs=4)
             for j in range(J):
-                make_diag(h, j)
+                passes(b[:, j, :], key, 1, j, EB * e, EB)
+            mp[key, 1, e] = b
 
-        bh_bc = keep.tile([P, D], F32, name="bh_bc")
+        def bias1(e):
+            t = work.tile([P, EB, J], F32, name=f"mb1{e}", tag="mb", bufs=3)
+            nc.vector.tensor_tensor(
+                out=t[:],
+                in0=mp["h", 1, e][:].rearrange("p j n -> p n j"),
+                in1=bh_bc[:, EB * e : EB * (e + 1)].unsqueeze(2).to_broadcast([P, EB, J]),
+                op=ADD,
+            )
+            mb[1, e] = t
 
-        def spread_bias():
-            for e in range(2):
-                b = psum.tile([P, 512], F32, name=f"bias{e}", tag="mp", bufs=4)
-                nc.tensor.matmul(b[:], lhsT=ones[:], rhs=bh_row[:, 512 * e : 512 * (e + 1)], start=True, stop=True)
-                nc.scalar.copy(out=bh_bc[:, 512 * e : 512 * (e + 1)], in_=b[:])
+        woven = {}
+        QW = 256
+
+        def times1(e):
+            if e % 2 == 0:
+                woven["s", 1, e // 2] = work.tile([P, QW, J], BF16, name=f"s1_{e}", tag="wv", bufs=12, align_bytes=64)
+            nc.vector.tensor_tensor(
+                out=woven["s", 1, e // 2][:, EB * (e % 2) : EB * (e % 2 + 1), :],
+                in0=mp["p", 1, e][:].rearrange("p j n -> p n j"),
+                in1=mb[1, e][:],
+                op=MULT,
+            )
+
+        x_slots = {}
+
+        def widen(h, j, c, engine):
+            if (h, c) not in x_slots:
+                x_slots[h, c] = keep.tile([P, J, WIDE], BF16, name=f"xw{h}{c}")
+            dst = x_slots[h, c][:, j, :]
+            src = x_sb[h][:, D * j + WIDE * c : D * j + WIDE * (c + 1)].bitcast(FP8)
+            scale = xs_sb[:, h, j : j + 1]
+            if engine == "s":
+                nc.scalar.activation(out=dst, in_=src, func=COPY, scale=scale)
+            else:
+                nc.vector.tensor_scalar(out=dst, in0=src, scalar1=scale, scalar2=None, op0=MULT)
+
+        def weave(key, h, q, engine):
+            t = work.tile([P, QW, J], BF16, name=f"{key}{h}_{q}", tag="wv", bufs=12, align_bytes=64)
+            if key == "s":
+                src = s_slots[:, :, QW * q : QW * (q + 1)]
+            else:
+                src = x_slots[h, q // 2][:, :, QW * (q % 2) : QW * (q % 2 + 1)]
+            copy(engine, t[:], src.rearrange("p j n -> p n j"))
+            woven[key, h, q] = t
 
         codes = {}
-        kin = {}
-        for key in ("g", "c"):
-            for h in range(H):
-                q = keep.tile([P, 2, A, 256], U32, name=f"{key}q{h}", align_bytes=64)
-                s = keep.tile([P, 2, A, 256], U8, name=f"{key}s{h}", align_bytes=64)
-                codes[key, h] = (q, s)
         for key in ("x", "s"):
             for h in range(H):
                 q = keep.tile([P, D], U32, name=f"{key}q{h}", align_bytes=64)
                 s = keep.tile([P, D], U8, name=f"{key}s{h}", align_bytes=64)
                 codes[key, h] = (q, s)
 
-        def transpose_tile(key, h, j, src):
-            if j % 2 == 0:
-                kin[key, h, j // 2] = work.tile([P, A, 256, 4], BF16, name=f"kin_{key}{h}{j}", tag="kin", bufs=3, align_bytes=64)
-            dst = kin[key, h, j // 2]
-            words = src.bitcast(F32)
-            bank = psum.tile([P, A, 2, P], F32, name=f"tp_{key}{h}{j}", tag="tp", bufs=2)
-            for a in range(A):
-                for u in range(2):
-                    if key == "c":
-                        cols = words[:, 256 * a + P * u : 256 * a + P * (u + 1)]
-                    else:
-                        cols = words[:, 256 * a + u : 256 * (a + 1) : 2]
-                    nc.tensor.transpose(bank[:, a, u, :], cols, ident[:])
-            jj = j % 2
-            nc.scalar.copy(
-                out=dst[:, :, P * jj : P * (jj + 1), :].bitcast(F32), in_=bank[:].rearrange("p a u m -> p a m u")
-            )
-
-        def quantise_k(key, h, q):
+        def quantise_t(key, h, q):
             cq, cs = codes[key, h]
-            src = kin[key, h, q]
-            nc.vector.quantize_mx(
-                out=cq[:, q, :, :].rearrange("p a n -> p (a n)").bitcast(FP8X4),
-                scales=cs[:, q, :, :].rearrange("p a n -> p (a n)"),
-                in_=src[:].rearrange("p a n t -> p (a n t)"),
-            )
+            cols = slice(QW * q, QW * (q + 1))
+            quantise(cq[:, cols], cs[:, cols], woven[key, h, q][:].rearrange("p n t -> p (n t)"))
 
-        def g_tile(h, j):
-            transpose_tile("g", h, j, g_sb[h, j // 2][:, j % 2, :])
+        res = {}
 
-        dg = {}
-        cw = {}
-
-        def c_levels01(h, j):
-            zt = z_sb[h, j]
-            for a in range(A):
-                b = psum.tile([P, 512], F32, name=f"dg{h}{j}{a}", tag="dg", bufs=2)
-                n = pe_levels(h, j)
-                for l in range(n):
-                    nc.tensor.matmul(
-                        b[:],
-                        lhsT=diag[h, j, l][:],
-                        rhs=zt[:, l, 512 * a : 512 * (a + 1)],
-                        start=(l == 0),
-                        stop=(l == n - 1),
-                    )
-                dg[h, j, a] = b
-
-        def c_level2(h, j):
-            zt = z_sb[h, j]
-            t = work.tile([P, D], BF16, name=f"cw{h}{j}", tag="cw", bufs=3)
-            c = j * L + 2
-            for a in range(A):
-                if pe_levels(h, j) == L:
-                    nc.scalar.copy(out=t[:, 512 * a : 512 * (a + 1)], in_=dg[h, j, a][:])
-                    continue
-                for u in range(2):
-                    nc.vector.scalar_tensor_tensor(
-                        out=t[:, 512 * a + 256 * u : 512 * a + 256 * (u + 1)].rearrange("p (k e) -> p k e", e=2),
-                        in0=zt[:, 2, 512 * a : 512 * (a + 1)].rearrange("p (k u e) -> p u k e", u=2, e=2)[:, u],
-                        scalar=gate_sb[:, h, c : c + 1],
-                        in1=dg[h, j, a][:].rearrange("p (k u e) -> p u k e", u=2, e=2)[:, u],
-                        op0=MULT,
-                        op1=ADD,
-                    )
-            cw[h, j] = t
-
-        def c_tile(h, j):
-            transpose_tile("c", h, j, cw[h, j][:])
-
-        mp = {}
-
-        def product(tag, key, wkey, h, e):
-            cq, cs = codes[key, h]
-            wt, slot = w_sb[wkey]
-            b = psum.tile([P, J, EB], F32, name=f"{wkey}_{h}{e}", tag="mp", bufs=4)
-            for j in range(J):
-                for a in range(A):
+        def final(q, rp):
+            b = psum.tile([P, 2, QW], F32, name=f"o{q}{rp}", tag="gt", bufs=4)
+            for i in range(2):
+                rows = slice(QW * rp + P * i, QW * rp + P * (i + 1))
+                cols = slice(QW * q, QW * (q + 1))
+                for h in range(H):
+                    xq, xs = codes["x", h]
+                    sq, ss = codes["s", h]
                     nc.tensor.matmul_mx(
-                        b[:, j, :],
-                        lhsT=cq[:, j // 2, a, P * (j % 2) : P * (j % 2 + 1)].bitcast(FP8X4),
-                        lhsT_scale=cs[:, j // 2, a, P * (j % 2) : P * (j % 2 + 1)],
-                        rhs=wt[:, a, 2 * EB * e : 2 * EB * (e + 1)].bitcast(FP4X4),
-                        rhs_scale=w_sc[:, slot + a, EB * e : EB * (e + 1)],
-                        start=(a == 0),
-                        stop=(a == A - 1),
+                        b[:, i, :],
+                        lhsT=xq[:, rows].bitcast(FP8X4),
+                        lhsT_scale=xs[:, rows],
+                        rhs=sq[:, cols].bitcast(FP8X4),
+                        rhs_scale=ss[:, cols],
+                        start=(h == 0),
+                        stop=(h == H - 1),
                     )
-            mp[wkey, h, e] = b
+            res[q, rp] = b
 
-        mb = {}
-        sin = {}
-
-        def bias_m(h, e):
-            t = work.tile([P, EB, J], F32, name=f"mb{h}{e}", tag="mb", bufs=3)
-            nc.vector.tensor_tensor(
-                out=t[:],
-                in0=mp["h", h, e][:].rearrange("p j n -> p n j"),
-                in1=bh_bc[:, EB * e : EB * (e + 1)].unsqueeze(2).to_broadcast([P, EB, J]),
-                op=ADD,
-            )
-            mb[h, e] = t
-
-        def times_p(h, e):
-            if e % 2 == 0:
-                sin[h, e // 2] = work.tile([P, 2 * EB, J], BF16, name=f"sin{h}{e}", tag="sin", bufs=3, align_bytes=64)
-            t = sin[h, e // 2]
-            k = e % 2
-            nc.vector.tensor_tensor(
-                out=t[:, EB * k : EB * (k + 1), :],
-                in0=mp["p", h, e][:].rearrange("p j n -> p n j"),
-                in1=mb[h, e][:],
-                op=MULT,
-            )
-
-        def quantise_s(h, q):
-            sq, ss = codes["s", h]
-            nc.vector.quantize_mx(
-                out=sq[:, 256 * q : 256 * (q + 1)].bitcast(FP8X4),
-                scales=ss[:, 256 * q : 256 * (q + 1)],
-                in_=sin[h, q][:].rearrange("p n t -> p (n t)"),
-            )
-
-        xw = {}
-
-        def widen_x(h, j):
-            if j == 0:
-                xw[h] = work.tile([P, J, D], BF16, name=f"xw{h}", tag="xw", bufs=2)
-            nc.scalar.activation(
-                out=xw[h][:, j, :],
-                in_=x_sb[h][:, D * j : D * (j + 1)].bitcast(FP8),
-                func=COPY,
-                scale=xs_sb[:, h, j : j + 1],
-            )
-
-        xi = {}
-
-        def interleave_x(h, q):
-            t = work.tile([P, 512, J], BF16, name=f"xi{h}{q}", tag="xi", bufs=2, align_bytes=64)
-            src = xw[h][:, :, 512 * q : 512 * (q + 1)].rearrange("p j n -> p n j")
-            nc.scalar.copy(out=t[:], in_=src)
-            xi[h, q] = t
-
-        def quantise_x(h, q):
-            xq, xs = codes["x", h]
-            nc.vector.quantize_mx(
-                out=xq[:, 512 * q : 512 * (q + 1)].bitcast(FP8X4),
-                scales=xs[:, 512 * q : 512 * (q + 1)],
-                in_=xi[h, q][:].rearrange("p n t -> p (n t)"),
-            )
-
-        def out_tile(e, r, tag, bufs, engine):
-            b = psum.tile([P, 512], F32, name=f"o{e}{r}", tag=tag, bufs=bufs)
-            for h in range(H):
-                xq, xs = codes["x", h]
-                sq, ss = codes["s", h]
-                nc.tensor.matmul_mx(
-                    b[:],
-                    lhsT=xq[:, P * r : P * (r + 1)].bitcast(FP8X4),
-                    lhsT_scale=xs[:, P * r : P * (r + 1)],
-                    rhs=sq[:, 512 * e : 512 * (e + 1)].bitcast(FP8X4),
-                    rhs_scale=ss[:, 512 * e : 512 * (e + 1)],
-                    start=(h == 0),
-                    stop=(h == H - 1),
-                )
-            t = work.tile([P, 512], F32, name=f"ob{e}{r}", tag="ob", bufs=12)
-            if engine == 0:
-                nc.scalar.activation(out=t[:], in_=b[:], func=COPY, scale=1.0 / 32.0)
+        def store(q, rp, engine):
+            t = work.tile([P, 2, QW], F32, name=f"ob{q}{rp}", tag="ob", bufs=10)
+            if engine == "s":
+                nc.scalar.activation(out=t[:], in_=res[q, rp][:], func=COPY, scale=1.0 / 32.0)
             else:
-                nc.vector.tensor_scalar(out=t[:], in0=b[:], scalar1=1.0 / 32.0, scalar2=None, op0=MULT)
-            nc.sync.dma_start(out=out[P * r : P * (r + 1), 512 * e : 512 * (e + 1)], in_=t[:])
+                nc.vector.tensor_scalar(out=t[:], in0=res[q, rp][:], scalar1=1.0 / 32.0, scalar2=None, op0=MULT)
+            rows = out[QW * rp : QW * (rp + 1), QW * q : QW * (q + 1)]
+            nc.sync.dma_start(out=rows.rearrange("(i p) n -> p i n", p=P), in_=t[:])
 
+        constants()
+        load_gates(nc.scalar)
+        load_zg(0, 0, 1)
+        load_bias(nc.sync)
+        load_zg(0, 1, 1)
+        load_w_scales("h", nc.scalar)
+        load_w_scales("p", nc.gpsimd)
+        load_w("h")
+        load_w("p")
+        load_xs(nc.sync)
+        load_x(0)
+        load_zg(0, 2, 1)
+        load_zg(0, 3, 1)
         for j in range(J):
-            c_levels01(0, j)
-            if j > 0:
-                c_tile(0, j - 1)
-            c_level2(0, j)
-            if j == 2:
-                quantise_k("c", 0, 0)
-        g_tile(0, 0)
-        c_tile(0, 3)
-        g_tile(0, 1)
-        quantise_k("c", 0, 1)
-        spread_bias()
-        quantise_k("g", 0, 0)
-        g_tile(0, 2)
-        g_tile(0, 3)
-        product("m", "c", "h", 0, 0)
-        bias_m(0, 0)
-        quantise_k("g", 0, 1)
+            load_zg(1, j, 1)
+        load_x(1)
+        make_table(0)
+        make_table(1)
 
-        steps = [
-            lambda: (widen_x(0, 0), widen_x(0, 1)),
-            lambda: (widen_x(0, 2), widen_x(0, 3), c_levels01(1, 0)),
-            lambda: (c_level2(1, 0), interleave_x(0, 0), c_levels01(1, 1)),
-            lambda: (c_tile(1, 0), c_level2(1, 1), c_levels01(1, 2), interleave_x(0, 1), quantise_x(0, 0)),
-            lambda: (c_tile(1, 1), c_level2(1, 2), c_levels01(1, 3)),
-            lambda: (c_tile(1, 2), c_level2(1, 3), quantise_k("c", 1, 0), g_tile(1, 0), quantise_x(0, 1)),
-            lambda: (c_tile(1, 3), g_tile(1, 1), g_tile(1, 2), quantise_k("g", 1, 0), quantise_k("c", 1, 1)),
-            lambda: (g_tile(1, 3), widen_x(1, 0), widen_x(1, 1), quantise_k("g", 1, 1)),
-        ]
-        for i in range(H * NEB):
-            h, e = i // NEB, i % NEB
-            if i + 1 < H * NEB:
-                product("m", "c", "h", (i + 1) // NEB, (i + 1) % NEB)
-            product("p", "g", "p", h, e)
-            if h == 0:
-                steps[e]()
-            if i + 1 < H * NEB:
-                bias_m((i + 1) // NEB, (i + 1) % NEB)
-            times_p(h, e)
-            if e % 2 == 1:
-                quantise_s(h, e // 2)
-            if h == 1 and e in (0, 1):
-                widen_x(1, e + 2)
-            if h == 1 and e in (2, 3):
-                interleave_x(1, e - 2)
-            if h == 1 and e in (4, 5):
-                quantise_x(1, e - 4)
-        for r in range(8):
-            out_tile(0, r, "tp" if r % 2 else "dg", 2, 0)
-        for r in range(8):
-            out_tile(1, r, "mp", 4, r % 2 if r >= 6 else 0)
+        def turn_take(h, j, e0, e1):
+            turn(h, j, 0)
+            take(h, j, 0, e0)
+            turn(h, j, 1)
+            take(h, j, 1, e1)
+
+        def m_pair(j):
+            for e in range(2):
+                product0("h", j, e)
+                bias0(j, e)
+
+        def p_pair(j):
+            for e in range(2):
+                product0("p", j, e)
+                times0(j, e)
+
+        def widen_all(h, c, engine):
+            for j in range(J):
+                widen(h, j, c, engine)
+
+        turn_take(0, 0, "s", "v")
+        spread_bias()
+        quantise_cg(0, 0)
+        turn_take(0, 1, "s", "s")
+        m_pair(0)
+        quantise_cg(0, 1)
+        p_pair(0)
+        widen_all(0, 0, "s")
+        m_pair(1)
+        widen_all(0, 1, "v")
+        weave("x", 0, 2, "g")
+        weave("x", 0, 3, "g")
+        weave("x", 0, 0, "g")
+        weave("x", 0, 1, "g")
+        turn_take(0, 2, "s", "s")
+        p_pair(1)
+        quantise_cg(0, 2)
+        turn_take(0, 3, "s", "s")
+        m_pair(2)
+        quantise_cg(0, 3)
+        quantise_t("x", 0, 2)
+        quantise_t("x", 0, 3)
+        turn_take(1, 0, "s", "s")
+        p_pair(2)
+        quantise_cg(1, 0)
+        quantise_t("x", 0, 0)
+        quantise_t("x", 0, 1)
+        turn_take(1, 1, "s", "s")
+        m_pair(3)
+        quantise_cg(1, 1)
+        turn_take(1, 2, "s", "s")
+        quantise_cg(1, 2)
+        turn_take(1, 3, "s", "v")
+        quantise_cg(1, 3)
+        p_pair(3)
+        weave("s", 0, 0, "g")
+        widen_all(1, 0, "s")
+        weave("x", 1, 0, "s")
+        weave("x", 1, 1, "g")
+        widen_all(1, 1, "s")
+        weave("s", 0, 1, "g")
+
+        def step(e):
+            product1("h", e + 1)
+            bias1(e + 1)
+            product1("p", e)
+            times1(e)
+
+        def finish(q, rp, engine="s"):
+            final(q, rp)
+            store(q, rp, engine)
+
+        product1("h", 0)
+        bias1(0)
+        step(0)
+        quantise_t("s", 0, 0)
+        step(1)
+        quantise_t("x", 1, 0)
+        weave("x", 1, 2, "s")
+        weave("x", 1, 3, "g")
+        weave("s", 0, 2, "g")
+        weave("s", 0, 3, "g")
+        step(2)
+        quantise_t("s", 1, 0)
+        quantise_t("x", 1, 1)
+        step(3)
+        finish(0, 0)
+        quantise_t("s", 0, 1)
+        quantise_t("x", 1, 2)
+        finish(0, 1)
+        step(4)
+        quantise_t("s", 1, 1)
+        quantise_t("x", 1, 3)
+        finish(0, 2)
+        step(5)
+        finish(0, 3)
+        quantise_t("s", 0, 2)
+        finish(1, 0)
+        step(6)
+        quantise_t("s", 1, 2)
+        quantise_t("s", 0, 3)
+        finish(1, 1)
+        product1("p", 7)
+        times1(7)
+        finish(1, 2)
+        quantise_t("s", 1, 3)
+        finish(1, 3)
+        for q in (2, 3):
+            for rp in range(4):
+                finish(q, rp, "v" if rp % 2 == 0 else "s")

@@ -51,7 +51,7 @@ def tile_focalmodulationqueryweightgrad_w4_kernel(
         bh_bc = keep.tile([P, D], BF16, name="bh_bc")
 
         def constants():
-            nc.vector.memset(raw_gates[:], 0.0)
+            nc.gpsimd.memset(raw_gates[:], 0.0)
             nc.vector.memset(w_sc[:].rearrange("p s n -> p (s n)").bitcast(I32), 0)
             nc.vector.memset(bh_row[:], 0.0)
             nc.vector.memset(ones[:], 1.0)
@@ -91,12 +91,11 @@ def tile_focalmodulationqueryweightgrad_w4_kernel(
         rows_of.append(g.rearrange("(h n u j) d -> h n u (j d)", h=H, u=U, j=J))
         zg = {}
 
-        def load_zg(h, j0, count):
-            t = keep.tile([P, U, count * D], BF16, name=f"zg{h}{j0}", align_bytes=64)
-            for l in range(L + 1):
-                nc.sync.dma_start(out=t[l : P : L + 1, :, :], in_=rows_of[l][h][:, :, D * j0 : D * (j0 + count)])
-            for j in range(j0, j0 + count):
-                zg[h, j] = (t, D * (j - j0))
+        def load_zg(h, j, levels=range(L + 1)):
+            if (h, j) not in zg:
+                zg[h, j] = keep.tile([P, U, D], BF16, name=f"zg{h}{j}", align_bytes=64)
+            for l in levels:
+                nc.sync.dma_start(out=zg[h, j][l : P : L + 1, :, :], in_=rows_of[l][h][:, :, D * j : D * (j + 1)])
 
         x_view = x_bytes.rearrange("(h m j) n -> h m (j n)", h=H, j=J)
         x_sb = {}
@@ -125,16 +124,15 @@ def tile_focalmodulationqueryweightgrad_w4_kernel(
         cg = {}
 
         def turn(h, j, a):
-            t, base = zg[h, j]
+            t = zg[h, j]
             b = psum.tile([P, U * 4, 2, NT], BF16, name=f"gt{h}{j}{a}", tag="gt", bufs=4)
             for u in range(U):
                 i = U * J * h + J * u + j
                 last = H * U * J
                 for k in range(4):
-                    first = base + WIDE * a + k
                     nc.tensor.matmul(
                         b[:, 4 * u + k, :, :],
-                        lhsT=t[:, u, first : base + WIDE * (a + 1) : 4],
+                        lhsT=t[:, u, WIDE * a + k : WIDE * (a + 1) : 4],
                         rhs=table[:, i : last + 1 : last - i, :],
                         start=True,
                         stop=True,
@@ -198,11 +196,11 @@ def tile_focalmodulationqueryweightgrad_w4_kernel(
                 out=s_slots[:, j, WIDE * e : WIDE * (e + 1)], in0=mp["p", 0, j, e][:], in1=mb[0, j, e][:], op=MULT
             )
 
-        def product1(key, e):
-            b = psum.tile([P, J, EB], F32, name=f"{key}1{e}", tag="mp", bufs=4)
-            for j in range(J):
-                passes(b[:, j, :], key, 1, j, EB * e, EB)
-            mp[key, 1, e] = b
+        def product1(key, e, slots=range(J)):
+            if (key, 1, e) not in mp:
+                mp[key, 1, e] = psum.tile([P, J, EB], F32, name=f"{key}1{e}", tag="mp", bufs=4)
+            for j in slots:
+                passes(mp[key, 1, e][:, j, :], key, 1, j, EB * e, EB)
 
         def bias1(e):
             t = work.tile([P, EB, J], F32, name=f"mb1{e}", tag="mb", bufs=3)
@@ -219,7 +217,7 @@ def tile_focalmodulationqueryweightgrad_w4_kernel(
 
         def times1(e):
             if e % 2 == 0:
-                woven["s", 1, e // 2] = work.tile([P, QW, J], BF16, name=f"s1_{e}", tag="wv", bufs=12, align_bytes=64)
+                woven["s", 1, e // 2] = work.tile([P, QW, J], BF16, name=f"s1_{e}", tag="wv", bufs=10, align_bytes=64)
             nc.vector.tensor_tensor(
                 out=woven["s", 1, e // 2][:, EB * (e % 2) : EB * (e % 2 + 1), :],
                 in0=mp["p", 1, e][:].rearrange("p j n -> p n j"),
@@ -241,12 +239,12 @@ def tile_focalmodulationqueryweightgrad_w4_kernel(
                 nc.vector.tensor_scalar(out=dst, in0=src, scalar1=scale, scalar2=None, op0=MULT)
 
         def weave(key, h, q, engine):
-            t = work.tile([P, QW, J], BF16, name=f"{key}{h}_{q}", tag="wv", bufs=12, align_bytes=64)
+            t = work.tile([P, QW, J], BF16, name=f"{key}{h}_{q}", tag="wv", bufs=10, align_bytes=64)
             if key == "s":
                 src = s_slots[:, :, QW * q : QW * (q + 1)]
             else:
                 src = x_slots[h, q // 2][:, :, QW * (q % 2) : QW * (q % 2 + 1)]
-            copy(engine, t[:], src.rearrange("p j n -> p n j"))
+            copy(engine, t[:].rearrange("p (c i) j -> p c j i", i=4), src.rearrange("p j (c i) -> p c j i", i=4))
             woven[key, h, q] = t
 
         codes = {}
@@ -292,20 +290,21 @@ def tile_focalmodulationqueryweightgrad_w4_kernel(
             nc.sync.dma_start(out=rows.rearrange("(i p) n -> p i n", p=P), in_=t[:])
 
         constants()
-        load_gates(nc.scalar)
-        load_zg(0, 0, 1)
+        load_zg(0, 0, (0, 1))
+        load_gates(nc.sync)
+        load_zg(0, 0, (2, 3))
+        load_zg(0, 1)
         load_bias(nc.sync)
-        load_zg(0, 1, 1)
-        load_w_scales("h", nc.scalar)
-        load_w_scales("p", nc.gpsimd)
+        load_w_scales("h", nc.sync)
         load_w("h")
         load_w("p")
+        load_w_scales("p", nc.sync)
         load_xs(nc.sync)
         load_x(0)
-        load_zg(0, 2, 1)
-        load_zg(0, 3, 1)
+        load_zg(0, 2)
+        load_zg(0, 3)
         for j in range(J):
-            load_zg(1, j, 1)
+            load_zg(1, j)
         load_x(1)
         make_table(0)
         make_table(1)
@@ -330,48 +329,6 @@ def tile_focalmodulationqueryweightgrad_w4_kernel(
             for j in range(J):
                 widen(h, j, c, engine)
 
-        turn_take(0, 0, "s", "v")
-        spread_bias()
-        quantise_cg(0, 0)
-        turn_take(0, 1, "s", "s")
-        m_pair(0)
-        quantise_cg(0, 1)
-        p_pair(0)
-        widen_all(0, 0, "s")
-        m_pair(1)
-        widen_all(0, 1, "v")
-        weave("x", 0, 2, "g")
-        weave("x", 0, 3, "g")
-        weave("x", 0, 0, "g")
-        weave("x", 0, 1, "g")
-        turn_take(0, 2, "s", "s")
-        p_pair(1)
-        quantise_cg(0, 2)
-        turn_take(0, 3, "s", "s")
-        m_pair(2)
-        quantise_cg(0, 3)
-        quantise_t("x", 0, 2)
-        quantise_t("x", 0, 3)
-        turn_take(1, 0, "s", "s")
-        p_pair(2)
-        quantise_cg(1, 0)
-        quantise_t("x", 0, 0)
-        quantise_t("x", 0, 1)
-        turn_take(1, 1, "s", "s")
-        m_pair(3)
-        quantise_cg(1, 1)
-        turn_take(1, 2, "s", "s")
-        quantise_cg(1, 2)
-        turn_take(1, 3, "s", "v")
-        quantise_cg(1, 3)
-        p_pair(3)
-        weave("s", 0, 0, "g")
-        widen_all(1, 0, "s")
-        weave("x", 1, 0, "s")
-        weave("x", 1, 1, "g")
-        widen_all(1, 1, "s")
-        weave("s", 0, 1, "g")
-
         def step(e):
             product1("h", e + 1)
             bias1(e + 1)
@@ -382,41 +339,110 @@ def tile_focalmodulationqueryweightgrad_w4_kernel(
             final(q, rp)
             store(q, rp, engine)
 
-        product1("h", 0)
+        turn_take(0, 0, "s", "v")
+        spread_bias()
+        quantise_cg(0, 0)
+        turn_take(0, 1, "s", "s")
+        m_pair(0)
+        quantise_cg(0, 1)
+        p_pair(0)
+        widen_all(0, 0, "s")
+        m_pair(1)
+        widen_all(0, 1, "v")
+        weave("x", 0, 0, "v")
+        turn_take(0, 2, "s", "s")
+        p_pair(1)
+        quantise_cg(0, 2)
+        weave("x", 0, 1, "v")
+        turn_take(0, 3, "s", "s")
+        m_pair(2)
+        quantise_cg(0, 3)
+        weave("x", 0, 2, "v")
+        turn_take(1, 0, "s", "s")
+        p_pair(2)
+        quantise_cg(1, 0)
+        weave("x", 0, 3, "v")
+        turn_take(1, 1, "s", "s")
+        m_pair(3)
+        quantise_cg(1, 1)
+        quantise_t("x", 0, 0)
+        quantise_t("x", 0, 1)
+        turn_take(1, 2, "s", "s")
+        p_pair(3)
+        quantise_cg(1, 2)
+        turn_take(1, 3, "s", "v")
+        quantise_cg(1, 3)
+        first = (("h", 0), ("h", 1), ("p", 0), ("p", 1))
+        for slots in ((0, 1), (2,)):
+            for key, e in first:
+                product1(key, e, slots)
+        widen_all(1, 0, "s")
+        weave("x", 1, 0, "s")
+        weave("s", 0, 0, "v")
+        product1("h", 0, (3,))
         bias1(0)
-        step(0)
+        product1("h", 1, (3,))
+        bias1(1)
+        product1("p", 0, (3,))
+        times1(0)
+        product1("p", 1, (3,))
+        product1("h", 2)
+        bias1(2)
+        times1(1)
+        weave("x", 1, 1, "s")
+        widen_all(1, 1, "s")
+        product1("h", 3)
+        product1("p", 2)
         quantise_t("s", 0, 0)
-        step(1)
         quantise_t("x", 1, 0)
-        weave("x", 1, 2, "s")
-        weave("x", 1, 3, "g")
-        weave("s", 0, 2, "g")
-        weave("s", 0, 3, "g")
-        step(2)
         quantise_t("s", 1, 0)
-        quantise_t("x", 1, 1)
-        step(3)
+        bias1(3)
+        times1(2)
+        product1("h", 4)
+        product1("p", 3)
         finish(0, 0)
-        quantise_t("s", 0, 1)
-        quantise_t("x", 1, 2)
+        quantise_t("x", 1, 1)
+        weave("s", 0, 1, "v")
+        bias1(4)
+        times1(3)
+        weave("x", 1, 2, "s")
+        product1("h", 5)
+        product1("p", 4)
         finish(0, 1)
-        step(4)
+        quantise_t("s", 0, 1)
+        quantise_t("x", 0, 2)
+        bias1(5)
         quantise_t("s", 1, 1)
-        quantise_t("x", 1, 3)
-        finish(0, 2)
-        step(5)
-        finish(0, 3)
-        quantise_t("s", 0, 2)
+        times1(4)
+        weave("x", 1, 3, "s")
+        product1("h", 6)
+        product1("p", 5)
         finish(1, 0)
-        step(6)
-        quantise_t("s", 1, 2)
-        quantise_t("s", 0, 3)
         finish(1, 1)
-        product1("p", 7)
-        times1(7)
+        quantise_t("x", 1, 2)
+        quantise_t("x", 0, 3)
+        bias1(6)
+        times1(5)
+        weave("s", 0, 2, "s")
+        product1("h", 7)
+        product1("p", 6)
+        finish(0, 2)
         finish(1, 2)
-        quantise_t("s", 1, 3)
+        quantise_t("x", 1, 3)
+        weave("s", 0, 3, "v")
+        bias1(7)
+        quantise_t("s", 1, 2)
+        times1(6)
+        product1("p", 7)
+        finish(0, 3)
         finish(1, 3)
-        for q in (2, 3):
-            for rp in range(4):
-                finish(q, rp, "v" if rp % 2 == 0 else "s")
+        quantise_t("s", 0, 2)
+        times1(7)
+        quantise_t("s", 0, 3)
+        finish(2, 0)
+        finish(2, 1)
+        quantise_t("s", 1, 3)
+        finish(2, 2)
+        finish(2, 3, "v")
+        for rp in range(4):
+            finish(3, rp, "v" if rp % 2 == 1 else "s")

@@ -80,22 +80,27 @@ def tile_focalmodulationqueryweightgrad_w4_kernel(
                 op=MULT,
             )
 
-        def spread_bias():
+        def spread_bias(engine="s"):
             b = psum.tile([P, D], BF16, name="bias", tag="mp", bufs=4)
             for e in range(2):
                 cols = slice(WIDE * e, WIDE * (e + 1))
                 nc.tensor.matmul(b[:, cols], lhsT=ones[:], rhs=bh_row[:, cols], start=True, stop=True)
-            nc.scalar.copy(out=bh_bc[:], in_=b[:])
+            copy(engine, bh_bc[:], b[:])
 
         rows_of = [z[l].rearrange("(h n u j) d -> h n u (j d)", h=H, u=U, j=J) for l in range(L)]
         rows_of.append(g.rearrange("(h n u j) d -> h n u (j d)", h=H, u=U, j=J))
         zg = {}
 
-        def load_zg(h, j, levels=range(L + 1)):
-            if (h, j) not in zg:
-                zg[h, j] = keep.tile([P, U, D], BF16, name=f"zg{h}{j}", align_bytes=64)
+        def load_zg(h, j, levels=range(L + 1), a=None):
+            first, width = (0, D) if a is None else (WIDE * a, WIDE)
+            if (h, j, first) not in zg:
+                t = keep.tile([P, U, width], BF16, name=f"zg{h}{j}{first}", align_bytes=64)
+                for k in range(0, width, WIDE):
+                    zg[h, j, first + k] = (t, k)
+            t = zg[h, j, first][0]
             for l in levels:
-                nc.sync.dma_start(out=zg[h, j][l : P : L + 1, :, :], in_=rows_of[l][h][:, :, D * j : D * (j + 1)])
+                src = rows_of[l][h][:, :, D * j + first : D * j + first + width]
+                nc.sync.dma_start(out=t[l : P : L + 1, :, :], in_=src)
 
         x_view = x_bytes.rearrange("(h m j) n -> h m (j n)", h=H, j=J)
         x_sb = {}
@@ -113,31 +118,31 @@ def tile_focalmodulationqueryweightgrad_w4_kernel(
             nc.sync.dma_start(out=t[:].bitcast(I32), in_=w_in[key][0].bitcast(I32).rearrange("a p n -> p a n"))
             w_sb[key] = t
 
-        def load_w_scales(key, queue):
+        def load_w_scales(key, queue, rows=range(4)):
             slot = w_in[key][2]
             sv = w_in[key][1].bitcast(I32).rearrange("a (q r) n -> r q a n", r=4)
-            for r in range(4):
+            for r in rows:
                 queue.dma_start(out=w_sc[r:P:32, slot : slot + A, :].bitcast(I32), in_=sv[r])
 
         turned = {}
         kin = {}
         cg = {}
 
-        def turn(h, j, a):
-            t = zg[h, j]
-            b = psum.tile([P, U * 4, 2, NT], BF16, name=f"gt{h}{j}{a}", tag="gt", bufs=4)
-            for u in range(U):
+        def turn(h, j, a, groups=range(U)):
+            t, first = zg[h, j, WIDE * a]
+            b = psum.tile([P, len(groups) * 4, 2, NT], BF16, name=f"gt{h}{j}{a}{groups[0]}", tag="gt", bufs=4)
+            for n, u in enumerate(groups):
                 i = U * J * h + J * u + j
                 last = H * U * J
                 for k in range(4):
                     nc.tensor.matmul(
-                        b[:, 4 * u + k, :, :],
-                        lhsT=t[:, u, WIDE * a + k : WIDE * (a + 1) : 4],
+                        b[:, 4 * n + k, :, :],
+                        lhsT=t[:, u, first + k : first + WIDE : 4],
                         rhs=table[:, i : last + 1 : last - i, :],
                         start=True,
                         stop=True,
                     )
-            turned[h, j, a] = b
+            turned[h, j, a, groups[0]] = b
 
         def copy(engine, dst, src):
             if engine == "s":
@@ -147,25 +152,31 @@ def tile_focalmodulationqueryweightgrad_w4_kernel(
             else:
                 nc.gpsimd.tensor_scalar(out=dst, in0=src, scalar1=1.0, scalar2=0.0, op0=MULT, op1=ADD)
 
-        def take(h, j, a, engine):
-            if a == 0:
-                kin[h, j] = work.tile([P, 2, A, NT, U * 4], BF16, name=f"kin{h}{j}", tag="kin", bufs=3, align_bytes=64)
-            copy(engine, kin[h, j][:, :, a, :, :], turned[h, j, a][:].rearrange("p s c n -> p c n s"))
+        def take(h, j, a, engine, groups=range(U)):
+            if (h, j) not in kin:
+                kin[h, j] = work.tile([P, A, 2, NT, U * 4], BF16, name=f"kin{h}{j}", tag="kin", bufs=3, align_bytes=64)
+            dst = kin[h, j][:, a, :, :, 4 * groups[0] : 4 * (groups[-1] + 1)]
+            copy(engine, dst, turned[h, j, a, groups[0]][:].rearrange("p s c n -> p c n s"))
 
         def quantise(dst, scales, src):
             nc.vector.quantize_mx(out=dst.bitcast(FP8X4), scales=scales, in_=src)
 
-        def quantise_cg(h, j):
-            q = keep.tile([P, 2 * A * P], U32, name=f"cgq{h}{j}", align_bytes=64)
-            s = keep.tile([P, 2 * A * P], U8, name=f"cgs{h}{j}", align_bytes=64)
-            quantise(q[:], s[:], kin[h, j][:].rearrange("p c a n s -> p (c a n s)"))
-            cg[h, j] = (q, s)
+        def quantise_cg(h, j, first=0, count=A):
+            if (h, j) not in cg:
+                q = keep.tile([P, A * 2 * P], U32, name=f"cgq{h}{j}", align_bytes=64)
+                s = keep.tile([P, A * 2 * P], U8, name=f"cgs{h}{j}", align_bytes=64)
+                cg[h, j] = (q, s)
+            q, s = cg[h, j]
+            cols = slice(2 * P * first, 2 * P * (first + count))
+            src = kin[h, j][:, first : first + count, :, :, :]
+            quantise(q[:, cols], s[:, cols], src.rearrange("p a c n s -> p (a c n s)"))
 
         def passes(dst, key, h, j, col0, width):
             q, s = cg[h, j]
             slot = w_in[key][2]
             for a in range(A):
-                cols = slice(P * (slot + a), P * (slot + a + 1))
+                first = P * (2 * a + slot // A)
+                cols = slice(first, first + P)
                 nc.tensor.matmul_mx(
                     dst,
                     lhsT=q[:, cols].bitcast(FP8X4),
@@ -185,7 +196,7 @@ def tile_focalmodulationqueryweightgrad_w4_kernel(
             mp[key, 0, j, e] = b
 
         def bias0(j, e):
-            t = work.tile([P, WIDE], F32, name=f"mb0{j}{e}", tag="mb", bufs=3)
+            t = work.tile([P, WIDE], F32, name=f"mb0{j}{e}", tag="mb", bufs=4)
             nc.vector.tensor_tensor(out=t[:], in0=mp["h", 0, j, e][:], in1=bh_bc[:, WIDE * e : WIDE * (e + 1)], op=ADD)
             mb[0, j, e] = t
 
@@ -203,7 +214,7 @@ def tile_focalmodulationqueryweightgrad_w4_kernel(
                 passes(mp[key, 1, e][:, j, :], key, 1, j, EB * e, EB)
 
         def bias1(e):
-            t = work.tile([P, EB, J], F32, name=f"mb1{e}", tag="mb", bufs=3)
+            t = work.tile([P, EB, J], F32, name=f"mb1{e}", tag="mb", bufs=4)
             nc.vector.tensor_tensor(
                 out=t[:],
                 in0=mp["h", 1, e][:].rearrange("p j n -> p n j"),
@@ -217,7 +228,7 @@ def tile_focalmodulationqueryweightgrad_w4_kernel(
 
         def times1(e):
             if e % 2 == 0:
-                woven["s", 1, e // 2] = work.tile([P, QW, J], BF16, name=f"s1_{e}", tag="wv", bufs=10, align_bytes=64)
+                woven["s", 1, e // 2] = work.tile([P, QW, J], BF16, name=f"s1_{e}", tag="s1", bufs=2, align_bytes=64)
             nc.vector.tensor_tensor(
                 out=woven["s", 1, e // 2][:, EB * (e % 2) : EB * (e % 2 + 1), :],
                 in0=mp["p", 1, e][:].rearrange("p j n -> p n j"),
@@ -239,12 +250,15 @@ def tile_focalmodulationqueryweightgrad_w4_kernel(
                 nc.vector.tensor_scalar(out=dst, in0=src, scalar1=scale, scalar2=None, op0=MULT)
 
         def weave(key, h, q, engine):
-            t = work.tile([P, QW, J], BF16, name=f"{key}{h}_{q}", tag="wv", bufs=10, align_bytes=64)
+            t = work.tile([P, QW, J], BF16, name=f"{key}{h}_{q}", tag="gw" if engine == "g" else "wv", bufs=1 if engine == "g" else 6, align_bytes=64)
             if key == "s":
                 src = s_slots[:, :, QW * q : QW * (q + 1)]
             else:
                 src = x_slots[h, q // 2][:, :, QW * (q % 2) : QW * (q % 2 + 1)]
-            copy(engine, t[:].rearrange("p (c i) j -> p c j i", i=4), src.rearrange("p j (c i) -> p c j i", i=4))
+            if engine == "g":
+                copy(engine, t[:], src.rearrange("p j n -> p n j"))
+            else:
+                copy(engine, t[:].rearrange("p (c i) j -> p c j i", i=4), src.rearrange("p j (c i) -> p c j i", i=4))
             woven[key, h, q] = t
 
         codes = {}
@@ -293,14 +307,17 @@ def tile_focalmodulationqueryweightgrad_w4_kernel(
         load_zg(0, 0, (0, 1))
         load_gates(nc.sync)
         load_zg(0, 0, (2, 3))
-        load_zg(0, 1)
         load_bias(nc.sync)
-        load_w_scales("h", nc.sync)
+        load_zg(0, 1, (0, 1))
+        load_w_scales("h", nc.sync, (0, 1, 2))
+        load_zg(0, 1, (2, 3))
         load_w("h")
+        load_w_scales("h", nc.sync, (3,))
+        load_w_scales("p", nc.sync, (0, 1))
         load_w("p")
-        load_w_scales("p", nc.sync)
-        load_xs(nc.sync)
+        load_w_scales("p", nc.sync, (2, 3))
         load_x(0)
+        load_xs(nc.sync)
         load_zg(0, 2)
         load_zg(0, 3)
         for j in range(J):
@@ -349,36 +366,39 @@ def tile_focalmodulationqueryweightgrad_w4_kernel(
         widen_all(0, 0, "s")
         m_pair(1)
         widen_all(0, 1, "v")
-        weave("x", 0, 0, "v")
+        weave("x", 0, 2, "g")
         turn_take(0, 2, "s", "s")
         p_pair(1)
         quantise_cg(0, 2)
-        weave("x", 0, 1, "v")
+        quantise_t("x", 0, 2)
+        weave("x", 0, 3, "g")
         turn_take(0, 3, "s", "s")
         m_pair(2)
         quantise_cg(0, 3)
-        weave("x", 0, 2, "v")
+        quantise_t("x", 0, 3)
+        weave("x", 0, 0, "g")
         turn_take(1, 0, "s", "s")
         p_pair(2)
         quantise_cg(1, 0)
-        weave("x", 0, 3, "v")
+        quantise_t("x", 0, 0)
+        weave("x", 0, 1, "g")
         turn_take(1, 1, "s", "s")
         m_pair(3)
         quantise_cg(1, 1)
-        quantise_t("x", 0, 0)
-        quantise_t("x", 0, 1)
         turn_take(1, 2, "s", "s")
         p_pair(3)
         quantise_cg(1, 2)
         turn_take(1, 3, "s", "v")
         quantise_cg(1, 3)
+        quantise_t("x", 0, 1)
+        weave("s", 0, 0, "g")
         first = (("h", 0), ("h", 1), ("p", 0), ("p", 1))
         for slots in ((0, 1), (2,)):
             for key, e in first:
                 product1(key, e, slots)
         widen_all(1, 0, "s")
         weave("x", 1, 0, "s")
-        weave("s", 0, 0, "v")
+        weave("x", 1, 1, "s")
         product1("h", 0, (3,))
         bias1(0)
         product1("h", 1, (3,))
@@ -389,60 +409,59 @@ def tile_focalmodulationqueryweightgrad_w4_kernel(
         product1("h", 2)
         bias1(2)
         times1(1)
-        weave("x", 1, 1, "s")
         widen_all(1, 1, "s")
+        weave("x", 1, 2, "s")
+        weave("x", 1, 3, "s")
         product1("h", 3)
         product1("p", 2)
-        quantise_t("s", 0, 0)
-        quantise_t("x", 1, 0)
         quantise_t("s", 1, 0)
+        quantise_t("x", 1, 0)
+        quantise_t("x", 1, 1)
+        quantise_t("s", 0, 0)
+        weave("s", 0, 1, "g")
         bias1(3)
         times1(2)
         product1("h", 4)
         product1("p", 3)
-        finish(0, 0)
-        quantise_t("x", 1, 1)
-        weave("s", 0, 1, "v")
+        final(0, 0)
         bias1(4)
         times1(3)
-        weave("x", 1, 2, "s")
         product1("h", 5)
+        final(0, 1)
         product1("p", 4)
-        finish(0, 1)
-        quantise_t("s", 0, 1)
-        quantise_t("x", 0, 2)
-        bias1(5)
         quantise_t("s", 1, 1)
+        quantise_t("x", 1, 2)
+        quantise_t("x", 1, 3)
+        quantise_t("s", 0, 1)
+        weave("s", 0, 2, "g")
+        store(0, 0, "s")
+        store(0, 1, "s")
+        bias1(5)
         times1(4)
-        weave("x", 1, 3, "s")
         product1("h", 6)
         product1("p", 5)
-        finish(1, 0)
-        finish(1, 1)
-        quantise_t("x", 1, 2)
-        quantise_t("x", 0, 3)
+        finish(0, 2)
+        finish(0, 3)
         bias1(6)
         times1(5)
-        weave("s", 0, 2, "s")
         product1("h", 7)
+        finish(1, 0)
         product1("p", 6)
-        finish(0, 2)
-        finish(1, 2)
-        quantise_t("x", 1, 3)
-        weave("s", 0, 3, "v")
-        bias1(7)
+        finish(1, 1)
         quantise_t("s", 1, 2)
+        quantise_t("s", 0, 2)
+        weave("s", 0, 3, "g")
+        bias1(7)
         times1(6)
         product1("p", 7)
-        finish(0, 3)
+        finish(1, 2)
         finish(1, 3)
-        quantise_t("s", 0, 2)
         times1(7)
-        quantise_t("s", 0, 3)
         finish(2, 0)
-        finish(2, 1)
+        quantise_t("s", 0, 3)
         quantise_t("s", 1, 3)
-        finish(2, 2)
-        finish(2, 3, "v")
-        for rp in range(4):
-            finish(3, rp, "v" if rp % 2 == 1 else "s")
+        finish(2, 1)
+        finish(2, 2, "v")
+        finish(2, 3)
+        for n in range(4):
+            finish(3, n, "v" if n % 2 == 0 else "s")

@@ -26,6 +26,7 @@ U = 4
 NT = 32
 EB = 128
 WIDE = 512
+BANKS = {"gt": 3, "mp": 5}
 
 FLOPS = 3 * 2 * T * D * D + 2 * L * T * D + 2 * T * D
 
@@ -81,7 +82,7 @@ def tile_focalmodulationqueryweightgrad_w4_kernel(
             )
 
         def spread_bias(engine="s"):
-            b = psum.tile([P, D], BF16, name="bias", tag="mp", bufs=4)
+            b = psum.tile([P, D], BF16, name="bias", tag="mp", bufs=BANKS["mp"])
             for e in range(2):
                 cols = slice(WIDE * e, WIDE * (e + 1))
                 nc.tensor.matmul(b[:, cols], lhsT=ones[:], rhs=bh_row[:, cols], start=True, stop=True)
@@ -130,7 +131,7 @@ def tile_focalmodulationqueryweightgrad_w4_kernel(
 
         def turn(h, j, a, groups=range(U)):
             t, first = zg[h, j, WIDE * a]
-            b = psum.tile([P, len(groups) * 4, 2, NT], BF16, name=f"gt{h}{j}{a}{groups[0]}", tag="gt", bufs=4)
+            b = psum.tile([P, len(groups) * 4, 2, NT], BF16, name=f"gt{h}{j}{a}{groups[0]}", tag="gt", bufs=BANKS["gt"])
             for n, u in enumerate(groups):
                 i = U * J * h + J * u + j
                 last = H * U * J
@@ -191,7 +192,7 @@ def tile_focalmodulationqueryweightgrad_w4_kernel(
         mb = {}
 
         def product0(key, j, e):
-            b = psum.tile([P, WIDE], F32, name=f"{key}0{j}{e}", tag="mp", bufs=4)
+            b = psum.tile([P, WIDE], F32, name=f"{key}0{j}{e}", tag="mp", bufs=BANKS["mp"])
             passes(b[:], key, 0, j, WIDE * e, WIDE)
             mp[key, 0, j, e] = b
 
@@ -207,9 +208,9 @@ def tile_focalmodulationqueryweightgrad_w4_kernel(
                 out=s_slots[:, j, WIDE * e : WIDE * (e + 1)], in0=mp["p", 0, j, e][:], in1=mb[0, j, e][:], op=MULT
             )
 
-        def product1(key, e, slots=range(J)):
+        def product1(key, e, slots=range(J), tag="mp"):
             if (key, 1, e) not in mp:
-                mp[key, 1, e] = psum.tile([P, J, EB], F32, name=f"{key}1{e}", tag="mp", bufs=4)
+                mp[key, 1, e] = psum.tile([P, J, EB], F32, name=f"{key}1{e}", tag=tag, bufs=BANKS[tag])
             for j in slots:
                 passes(mp[key, 1, e][:, j, :], key, 1, j, EB * e, EB)
 
@@ -276,7 +277,7 @@ def tile_focalmodulationqueryweightgrad_w4_kernel(
         res = {}
 
         def final(q, rp):
-            b = psum.tile([P, 2, QW], F32, name=f"o{q}{rp}", tag="gt", bufs=4)
+            b = psum.tile([P, 2, QW], F32, name=f"o{q}{rp}", tag="gt", bufs=BANKS["gt"])
             for i in range(2):
                 rows = slice(QW * rp + P * i, QW * rp + P * (i + 1))
                 cols = slice(QW * q, QW * (q + 1))
@@ -320,8 +321,10 @@ def tile_focalmodulationqueryweightgrad_w4_kernel(
         load_xs(nc.sync)
         load_zg(0, 2)
         load_zg(0, 3)
-        for j in range(J):
+        for j in range(J - 1):
             load_zg(1, j)
+        for a in range(A):
+            load_zg(1, J - 1, a=a)
         load_x(1)
         make_table(0)
         make_table(1)
@@ -368,37 +371,47 @@ def tile_focalmodulationqueryweightgrad_w4_kernel(
         widen_all(0, 1, "v")
         weave("x", 0, 2, "g")
         turn_take(0, 2, "s", "s")
+        weave("x", 0, 0, "v")
         p_pair(1)
         quantise_cg(0, 2)
+        quantise_t("x", 0, 0)
         quantise_t("x", 0, 2)
         weave("x", 0, 3, "g")
         turn_take(0, 3, "s", "s")
         m_pair(2)
         quantise_cg(0, 3)
         quantise_t("x", 0, 3)
-        weave("x", 0, 0, "g")
-        turn_take(1, 0, "s", "s")
-        p_pair(2)
-        quantise_cg(1, 0)
-        quantise_t("x", 0, 0)
         weave("x", 0, 1, "g")
-        turn_take(1, 1, "s", "s")
+        p_pair(2)
+        turn_take(1, 0, "s", "s")
         m_pair(3)
-        quantise_cg(1, 1)
-        turn_take(1, 2, "s", "s")
+        quantise_cg(1, 0)
+        turn_take(1, 1, "s", "s")
         p_pair(3)
-        quantise_cg(1, 2)
-        turn_take(1, 3, "s", "v")
-        quantise_cg(1, 3)
+        quantise_cg(1, 1)
         quantise_t("x", 0, 1)
         weave("s", 0, 0, "g")
-        first = (("h", 0), ("h", 1), ("p", 0), ("p", 1))
-        for slots in ((0, 1), (2,)):
-            for key, e in first:
-                product1(key, e, slots)
+        turn_take(1, 2, "s", "s")
+        turn(1, 3, 0)
+        take(1, 3, 0, "v")
+        first = (("h", 0), ("h", 1), ("p", 0), ("p", 1), ("h", 2))
+        for key, e in first[:2]:
+            product1(key, e, (0, 1))
+        turn(1, 3, 1, (0, 1))
+        take(1, 3, 1, "s", (0, 1))
+        turn(1, 3, 1, (2, 3))
+        quantise_cg(1, 2)
+        take(1, 3, 1, "s", (2, 3))
+        quantise_cg(1, 3, 0, 1)
+        for key, e in first[2:]:
+            product1(key, e, (0, 1))
+        for key, e in first:
+            product1(key, e, (2,))
+        quantise_cg(1, 3, 1, 1)
+        weave("s", 0, 2, "v")
+        quantise_t("s", 0, 0)
+        weave("s", 0, 1, "g")
         widen_all(1, 0, "s")
-        weave("x", 1, 0, "s")
-        weave("x", 1, 1, "s")
         product1("h", 0, (3,))
         bias1(0)
         product1("h", 1, (3,))
@@ -406,62 +419,59 @@ def tile_focalmodulationqueryweightgrad_w4_kernel(
         product1("p", 0, (3,))
         times1(0)
         product1("p", 1, (3,))
-        product1("h", 2)
-        bias1(2)
+        product1("h", 2, (3,))
         times1(1)
+        weave("x", 1, 0, "s")
         widen_all(1, 1, "s")
-        weave("x", 1, 2, "s")
-        weave("x", 1, 3, "s")
-        product1("h", 3)
         product1("p", 2)
-        quantise_t("s", 1, 0)
-        quantise_t("x", 1, 0)
-        quantise_t("x", 1, 1)
-        quantise_t("s", 0, 0)
-        weave("s", 0, 1, "g")
-        bias1(3)
-        times1(2)
-        product1("h", 4)
+        product1("h", 3)
+        bias1(2)
         product1("p", 3)
-        final(0, 0)
-        bias1(4)
-        times1(3)
-        product1("h", 5)
-        final(0, 1)
-        product1("p", 4)
-        quantise_t("s", 1, 1)
-        quantise_t("x", 1, 2)
-        quantise_t("x", 1, 3)
+        product1("h", 4)
+        quantise_t("x", 1, 0)
+        quantise_t("s", 1, 0)
         quantise_t("s", 0, 1)
-        weave("s", 0, 2, "g")
-        store(0, 0, "s")
-        store(0, 1, "s")
+        weave("x", 1, 1, "g")
+        bias1(3)
+        product1("h", 5)
+        times1(2)
+        finish(0, 0)
+        weave("x", 1, 2, "s")
+        product1("p", 4)
+        times1(3)
+        bias1(4)
+        product1("p", 5)
+        quantise_t("s", 1, 1)
+        quantise_t("x", 1, 1)
+        weave("x", 1, 3, "g")
         bias1(5)
+        finish(1, 0)
+        finish(0, 1)
         times1(4)
         product1("h", 6)
-        product1("p", 5)
-        finish(0, 2)
-        finish(0, 3)
-        bias1(6)
-        times1(5)
-        product1("h", 7)
-        finish(1, 0)
-        product1("p", 6)
         finish(1, 1)
-        quantise_t("s", 1, 2)
+        times1(5)
+        quantise_t("x", 1, 2)
         quantise_t("s", 0, 2)
+        quantise_t("x", 1, 3)
         weave("s", 0, 3, "g")
-        bias1(7)
-        times1(6)
-        product1("p", 7)
+        product1("h", 7)
+        finish(0, 2)
         finish(1, 2)
+        bias1(6)
+        product1("p", 6)
+        bias1(7)
+        quantise_t("s", 1, 2)
+        finish(0, 3)
         finish(1, 3)
-        times1(7)
+        times1(6)
         finish(2, 0)
+        product1("p", 7)
         quantise_t("s", 0, 3)
-        quantise_t("s", 1, 3)
         finish(2, 1)
-        finish(2, 2, "v")
+        times1(7)
+        finish(2, 2)
+        quantise_t("s", 1, 3)
         finish(2, 3)
         for n in range(4):
             finish(3, n, "v" if n % 2 == 0 else "s")

@@ -317,10 +317,10 @@ def tile_focalmodulationqueryweightgrad_w4_kernel(
         load_w_scales("p", nc.sync, (0, 1))
         load_w("p")
         load_w_scales("p", nc.sync, (2, 3))
-        load_x(0)
-        load_xs(nc.sync)
         load_zg(0, 2)
+        load_xs(nc.sync)
         load_zg(0, 3)
+        load_x(0)
         for j in range(J - 1):
             load_zg(1, j)
         for a in range(A):
@@ -362,54 +362,58 @@ def tile_focalmodulationqueryweightgrad_w4_kernel(
         turn_take(0, 0, "s", "v")
         spread_bias()
         quantise_cg(0, 0)
-        turn_take(0, 1, "s", "s")
-        m_pair(0)
+        turn_take(0, 1, "s", "v")
+        product0("h", 0, 0)
+        product0("h", 0, 1)
         quantise_cg(0, 1)
+        bias0(0, 0)
+        bias0(0, 1)
         p_pair(0)
-        widen_all(0, 0, "s")
         m_pair(1)
-        widen_all(0, 1, "v")
-        weave("x", 0, 2, "g")
-        turn_take(0, 2, "s", "s")
-        weave("x", 0, 0, "v")
-        p_pair(1)
+        turn_take(0, 2, "s", "v")
+        product0("p", 1, 0)
+        product0("p", 1, 1)
         quantise_cg(0, 2)
-        quantise_t("x", 0, 0)
-        quantise_t("x", 0, 2)
-        weave("x", 0, 3, "g")
+        times0(1, 0)
+        times0(1, 1)
         turn_take(0, 3, "s", "s")
+        widen(0, 0, 0, "v")
         m_pair(2)
+        widen(0, 1, 0, "s")
+        widen(0, 2, 0, "s")
+        widen(0, 0, 1, "s")
         quantise_cg(0, 3)
-        quantise_t("x", 0, 3)
-        weave("x", 0, 1, "g")
         p_pair(2)
+        widen(0, 3, 0, "v")
+        weave("x", 0, 0, "v")
+        weave("x", 0, 1, "g")
         turn_take(1, 0, "s", "s")
         m_pair(3)
-        quantise_cg(1, 0)
         turn_take(1, 1, "s", "s")
+        quantise_cg(1, 0)
         p_pair(3)
         quantise_cg(1, 1)
-        quantise_t("x", 0, 1)
-        weave("s", 0, 0, "g")
+        for j in range(1, J):
+            widen(0, j, 1, "v")
         turn_take(1, 2, "s", "s")
         turn(1, 3, 0)
         take(1, 3, 0, "v")
         first = (("h", 0), ("h", 1), ("p", 0), ("p", 1), ("h", 2))
-        for key, e in first[:2]:
-            product1(key, e, (0, 1))
+        for key, e in first:
+            product1(key, e, (0,))
         turn(1, 3, 1, (0, 1))
         take(1, 3, 1, "s", (0, 1))
         turn(1, 3, 1, (2, 3))
         quantise_cg(1, 2)
         take(1, 3, 1, "s", (2, 3))
         quantise_cg(1, 3, 0, 1)
-        for key, e in first[2:]:
-            product1(key, e, (0, 1))
-        for key, e in first:
-            product1(key, e, (2,))
+        quantise_t("x", 0, 0)
+        for j in (1, 2):
+            for key, e in first:
+                product1(key, e, (j,))
         quantise_cg(1, 3, 1, 1)
-        weave("s", 0, 2, "v")
-        quantise_t("s", 0, 0)
+        weave("s", 0, 0, "v")
+        quantise_t("x", 0, 1)
         weave("s", 0, 1, "g")
         widen_all(1, 0, "s")
         product1("h", 0, (3,))
@@ -423,55 +427,60 @@ def tile_focalmodulationqueryweightgrad_w4_kernel(
         times1(1)
         weave("x", 1, 0, "s")
         widen_all(1, 1, "s")
-        product1("p", 2)
+        product1("p", 2, tag="gt")
         product1("h", 3)
         bias1(2)
         product1("p", 3)
         product1("h", 4)
+        quantise_t("s", 0, 0)
         quantise_t("x", 1, 0)
         quantise_t("s", 1, 0)
         quantise_t("s", 0, 1)
         weave("x", 1, 1, "g")
+        weave("x", 1, 2, "s")
         bias1(3)
         product1("h", 5)
         times1(2)
         finish(0, 0)
-        weave("x", 1, 2, "s")
+        weave("x", 0, 3, "s")
         product1("p", 4)
         times1(3)
         bias1(4)
         product1("p", 5)
         quantise_t("s", 1, 1)
+        quantise_t("x", 1, 2)
         quantise_t("x", 1, 1)
-        weave("x", 1, 3, "g")
+        weave("x", 0, 2, "g")
         bias1(5)
+        product1("h", 6)
         finish(1, 0)
         finish(0, 1)
+        weave("s", 0, 2, "s")
         times1(4)
-        product1("h", 6)
         finish(1, 1)
         times1(5)
-        quantise_t("x", 1, 2)
+        quantise_t("x", 0, 3)
+        weave("x", 1, 3, "v")
+        quantise_t("s", 1, 2)
         quantise_t("s", 0, 2)
         quantise_t("x", 1, 3)
+        quantise_t("x", 0, 2)
         weave("s", 0, 3, "g")
         product1("h", 7)
-        finish(0, 2)
-        finish(1, 2)
-        bias1(6)
         product1("p", 6)
-        bias1(7)
-        quantise_t("s", 1, 2)
-        finish(0, 3)
-        finish(1, 3)
-        times1(6)
-        finish(2, 0)
         product1("p", 7)
-        quantise_t("s", 0, 3)
-        finish(2, 1)
+        bias1(6)
+        bias1(7)
+        finish(2, 0)
+        finish(0, 3)
+        times1(6)
+        finish(0, 2)
         times1(7)
-        finish(2, 2)
+        finish(1, 2)
+        finish(1, 3)
+        quantise_t("s", 0, 3)
         quantise_t("s", 1, 3)
-        finish(2, 3)
+        for n in range(1, 4):
+            finish(2, n)
         for n in range(4):
             finish(3, n, "v" if n % 2 == 0 else "s")

@@ -41,9 +41,21 @@ def tile_focalmodulationqueryweightgrad_w4_kernel(
         psum = ctx.enter_context(tc.psum_pool(name="psum", bufs=1))
         ctx.enter_context(tc.manual_schedule())
 
+        def placed(name, shape, dtype, size, offset):
+            inner = 1
+            for n in shape:
+                inner *= n
+            pad = offset // size
+            t = keep.tile([P, pad + inner], dtype, name=name, align_bytes=256)
+            return t, pad
+
         raw_gates = keep.tile([P, H, 48], BF16, name="raw_gates")
         bh_row = keep.tile([P, D], BF16, name="bh_row")
-        w_sc = keep.tile([P, 2 * A, D], U8, name="w_sc", align_bytes=64)
+        w_sc_all = keep.tile([P, 2 * (A * D + 256)], U8, name="w_sc", align_bytes=256)
+        w_sc = {}
+        for n, (key, offset) in enumerate((("h", 192), ("p", 64))):
+            first = n * (A * D + 256) + offset
+            w_sc[key] = w_sc_all[:, first : first + A * D].rearrange("p (a n) -> p a n", a=A)
         ident = keep.tile([P, P], BF16, name="ident")
         ones = keep.tile([P, P], BF16, name="ones")
         block = keep.tile([P, NT], F32, name="block")
@@ -53,7 +65,7 @@ def tile_focalmodulationqueryweightgrad_w4_kernel(
 
         def constants():
             nc.gpsimd.memset(raw_gates[:], 0.0)
-            nc.vector.memset(w_sc[:].rearrange("p s n -> p (s n)").bitcast(I32), 0)
+            nc.vector.memset(w_sc_all[:].bitcast(I32), 0)
             nc.vector.memset(bh_row[:], 0.0)
             nc.vector.memset(ones[:], 1.0)
             make_identity(nc, ident[:])
@@ -106,24 +118,24 @@ def tile_focalmodulationqueryweightgrad_w4_kernel(
         x_view = x_bytes.rearrange("(h m j) n -> h m (j n)", h=H, j=J)
         x_sb = {}
 
-        def load_x(h):
-            t = keep.tile([P, J * D], U8, name=f"x_sb{h}", align_bytes=64)
-            nc.sync.dma_start(out=t[:], in_=x_view[h])
-            x_sb[h] = t
+        def load_x(h, first=0, count=J):
+            t = keep.tile([P, count * D], U8, name=f"x_sb{h}{first}", align_bytes=64)
+            nc.sync.dma_start(out=t[:], in_=x_view[h][:, D * first : D * (first + count)])
+            for j in range(count):
+                x_sb[h, first + j] = (t, D * j)
 
         w_sb = {}
         w_in = {"h": (wh_words, wh_scales, 0), "p": (wp_words, wp_scales, A)}
 
         def load_w(key):
-            t = keep.tile([P, A, 2 * D], U8, name=f"w_{key}", align_bytes=64)
-            nc.sync.dma_start(out=t[:].bitcast(I32), in_=w_in[key][0].bitcast(I32).rearrange("a p n -> p a n"))
-            w_sb[key] = t
+            t, pad = placed(f"w_{key}", [A, 2 * D], U8, 1, 128)
+            w_sb[key] = t[:, pad:].rearrange("p (a n) -> p a n", a=A)
+            nc.sync.dma_start(out=w_sb[key].bitcast(I32), in_=w_in[key][0].bitcast(I32).rearrange("a p n -> p a n"))
 
         def load_w_scales(key, queue, rows=range(4)):
-            slot = w_in[key][2]
             sv = w_in[key][1].bitcast(I32).rearrange("a (q r) n -> r q a n", r=4)
             for r in rows:
-                queue.dma_start(out=w_sc[r:P:32, slot : slot + A, :].bitcast(I32), in_=sv[r])
+                queue.dma_start(out=w_sc[key][r:P:32, :, :].bitcast(I32), in_=sv[r])
 
         turned = {}
         kin = {}
@@ -164,9 +176,9 @@ def tile_focalmodulationqueryweightgrad_w4_kernel(
 
         def quantise_cg(h, j, first=0, count=A):
             if (h, j) not in cg:
-                q = keep.tile([P, A * 2 * P], U32, name=f"cgq{h}{j}", align_bytes=64)
-                s = keep.tile([P, A * 2 * P], U8, name=f"cgs{h}{j}", align_bytes=64)
-                cg[h, j] = (q, s)
+                q, _ = placed(f"cgq{h}{j}", [A * 2 * P], U32, 4, 0)
+                s, pad = placed(f"cgs{h}{j}", [A * 2 * P], U8, 1, 64)
+                cg[h, j] = (q, s[:, pad:])
             q, s = cg[h, j]
             cols = slice(2 * P * first, 2 * P * (first + count))
             src = kin[h, j][:, first : first + count, :, :, :]
@@ -183,7 +195,7 @@ def tile_focalmodulationqueryweightgrad_w4_kernel(
                     lhsT=q[:, cols].bitcast(FP8X4),
                     lhsT_scale=s[:, cols],
                     rhs=w_sb[key][:, a, 2 * col0 : 2 * (col0 + width)].bitcast(FP4X4),
-                    rhs_scale=w_sc[:, slot + a, col0 : col0 + width],
+                    rhs_scale=w_sc[key][:, a, col0 : col0 + width],
                     start=(a == 0),
                     stop=(a == A - 1),
                 )
@@ -243,7 +255,8 @@ def tile_focalmodulationqueryweightgrad_w4_kernel(
             if (h, c) not in x_slots:
                 x_slots[h, c] = keep.tile([P, J, WIDE], BF16, name=f"xw{h}{c}")
             dst = x_slots[h, c][:, j, :]
-            src = x_sb[h][:, D * j + WIDE * c : D * j + WIDE * (c + 1)].bitcast(FP8)
+            t, first = x_sb[h, j]
+            src = t[:, first + WIDE * c : first + WIDE * (c + 1)].bitcast(FP8)
             scale = xs_sb[:, h, j : j + 1]
             if engine == "s":
                 nc.scalar.activation(out=dst, in_=src, func=COPY, scale=scale)
@@ -265,9 +278,9 @@ def tile_focalmodulationqueryweightgrad_w4_kernel(
         codes = {}
         for key in ("x", "s"):
             for h in range(H):
-                q = keep.tile([P, D], U32, name=f"{key}q{h}", align_bytes=64)
-                s = keep.tile([P, D], U8, name=f"{key}s{h}", align_bytes=64)
-                codes[key, h] = (q, s)
+                q, qpad = placed(f"{key}q{h}", [D], U32, 4, 0 if key == "x" else 128)
+                s, spad = placed(f"{key}s{h}", [D], U8, 1, 64 if key == "x" else 192)
+                codes[key, h] = (q[:, qpad:], s[:, spad:])
 
         def quantise_t(key, h, q):
             cq, cs = codes[key, h]
@@ -317,10 +330,11 @@ def tile_focalmodulationqueryweightgrad_w4_kernel(
         load_w_scales("p", nc.sync, (0, 1))
         load_w("p")
         load_w_scales("p", nc.sync, (2, 3))
-        load_zg(0, 2)
+        load_x(0, 0, 2)
         load_xs(nc.sync)
+        load_zg(0, 2)
         load_zg(0, 3)
-        load_x(0)
+        load_x(0, 2, 2)
         for j in range(J - 1):
             load_zg(1, j)
         for a in range(A):
@@ -369,6 +383,9 @@ def tile_focalmodulationqueryweightgrad_w4_kernel(
         bias0(0, 0)
         bias0(0, 1)
         p_pair(0)
+        for c in range(2):
+            for j in range(2):
+                widen(0, j, c, "s")
         m_pair(1)
         turn_take(0, 2, "s", "v")
         product0("p", 1, 0)
@@ -377,11 +394,10 @@ def tile_focalmodulationqueryweightgrad_w4_kernel(
         times0(1, 0)
         times0(1, 1)
         turn_take(0, 3, "s", "s")
-        widen(0, 0, 0, "v")
+        widen(0, 2, 0, "v")
         m_pair(2)
-        widen(0, 1, 0, "s")
-        widen(0, 2, 0, "s")
-        widen(0, 0, 1, "s")
+        widen(0, 2, 1, "s")
+        widen(0, 3, 1, "s")
         quantise_cg(0, 3)
         p_pair(2)
         widen(0, 3, 0, "v")
@@ -393,8 +409,7 @@ def tile_focalmodulationqueryweightgrad_w4_kernel(
         quantise_cg(1, 0)
         p_pair(3)
         quantise_cg(1, 1)
-        for j in range(1, J):
-            widen(0, j, 1, "v")
+        weave("x", 0, 2, "v")
         turn_take(1, 2, "s", "s")
         turn(1, 3, 0)
         take(1, 3, 0, "v")
@@ -403,14 +418,17 @@ def tile_focalmodulationqueryweightgrad_w4_kernel(
             product1(key, e, (0,))
         turn(1, 3, 1, (0, 1))
         take(1, 3, 1, "s", (0, 1))
+        for key, e in first[:3]:
+            product1(key, e, (1,))
         turn(1, 3, 1, (2, 3))
         quantise_cg(1, 2)
         take(1, 3, 1, "s", (2, 3))
         quantise_cg(1, 3, 0, 1)
         quantise_t("x", 0, 0)
-        for j in (1, 2):
-            for key, e in first:
-                product1(key, e, (j,))
+        for key, e in first[3:]:
+            product1(key, e, (1,))
+        for key, e in first:
+            product1(key, e, (2,))
         quantise_cg(1, 3, 1, 1)
         weave("s", 0, 0, "v")
         quantise_t("x", 0, 1)
@@ -450,37 +468,35 @@ def tile_focalmodulationqueryweightgrad_w4_kernel(
         quantise_t("s", 1, 1)
         quantise_t("x", 1, 2)
         quantise_t("x", 1, 1)
-        weave("x", 0, 2, "g")
+        weave("x", 1, 3, "g")
         bias1(5)
         product1("h", 6)
         finish(1, 0)
         finish(0, 1)
-        weave("s", 0, 2, "s")
         times1(4)
         finish(1, 1)
+        weave("s", 0, 2, "s")
         times1(5)
-        quantise_t("x", 0, 3)
-        weave("x", 1, 3, "v")
-        quantise_t("s", 1, 2)
-        quantise_t("s", 0, 2)
-        quantise_t("x", 1, 3)
         quantise_t("x", 0, 2)
+        quantise_t("x", 0, 3)
+        quantise_t("s", 1, 2)
+        quantise_t("x", 1, 3)
         weave("s", 0, 3, "g")
         product1("h", 7)
         product1("p", 6)
         product1("p", 7)
         bias1(6)
         bias1(7)
-        finish(2, 0)
-        finish(0, 3)
-        times1(6)
         finish(0, 2)
-        times1(7)
         finish(1, 2)
+        times1(6)
+        finish(0, 3)
+        times1(7)
         finish(1, 3)
+        quantise_t("s", 0, 2)
         quantise_t("s", 0, 3)
         quantise_t("s", 1, 3)
-        for n in range(1, 4):
+        for n in range(4):
             finish(2, n)
         for n in range(4):
             finish(3, n, "v" if n % 2 == 0 else "s")

@@ -65,9 +65,9 @@ def tile_focalmodulationqueryweightgrad_w4_kernel(
 
         def constants():
             nc.gpsimd.memset(raw_gates[:], 0.0)
-            nc.vector.memset(w_sc_all[:].bitcast(I32), 0)
             nc.vector.memset(bh_row[:], 0.0)
             nc.vector.memset(ones[:], 1.0)
+            nc.vector.memset(w_sc_all[:].bitcast(I32), 0)
             make_identity(nc, ident[:])
             nc.vector.tensor_reduce(
                 out=block[:], in_=ident[:].rearrange("p (n l) -> p n l", l=L + 1), axis=mybir.AxisListType.X, op=ADD
@@ -319,9 +319,9 @@ def tile_focalmodulationqueryweightgrad_w4_kernel(
 
         constants()
         load_zg(0, 0, (0, 1))
+        load_bias(nc.sync)
         load_gates(nc.sync)
         load_zg(0, 0, (2, 3))
-        load_bias(nc.sync)
         load_zg(0, 1, (0, 1))
         load_w_scales("h", nc.sync, (0, 1, 2))
         load_zg(0, 1, (2, 3))
@@ -373,8 +373,8 @@ def tile_focalmodulationqueryweightgrad_w4_kernel(
             final(q, rp)
             store(q, rp, engine)
 
-        turn_take(0, 0, "s", "v")
         spread_bias()
+        turn_take(0, 0, "s", "v")
         quantise_cg(0, 0)
         turn_take(0, 1, "s", "v")
         product0("h", 0, 0)

@@ -41,21 +41,9 @@ def tile_focalmodulationqueryweightgrad_w4_kernel(
         psum = ctx.enter_context(tc.psum_pool(name="psum", bufs=1))
         ctx.enter_context(tc.manual_schedule())
 
-        def placed(name, shape, dtype, size, offset):
-            inner = 1
-            for n in shape:
-                inner *= n
-            pad = offset // size
-            t = keep.tile([P, pad + inner], dtype, name=name, align_bytes=256)
-            return t, pad
-
         raw_gates = keep.tile([P, H, 48], BF16, name="raw_gates")
         bh_row = keep.tile([P, D], BF16, name="bh_row")
-        w_sc_all = keep.tile([P, 2 * (A * D + 256)], U8, name="w_sc", align_bytes=256)
-        w_sc = {}
-        for n, (key, offset) in enumerate((("h", 192), ("p", 64))):
-            first = n * (A * D + 256) + offset
-            w_sc[key] = w_sc_all[:, first : first + A * D].rearrange("p (a n) -> p a n", a=A)
+        w_sc = keep.tile([P, 2 * A, D], U8, name="w_sc", align_bytes=64)
         ident = keep.tile([P, P], BF16, name="ident")
         ones = keep.tile([P, P], BF16, name="ones")
         block = keep.tile([P, NT], F32, name="block")
@@ -67,7 +55,7 @@ def tile_focalmodulationqueryweightgrad_w4_kernel(
             nc.gpsimd.memset(raw_gates[:], 0.0)
             nc.vector.memset(bh_row[:], 0.0)
             nc.vector.memset(ones[:], 1.0)
-            nc.vector.memset(w_sc_all[:].bitcast(I32), 0)
+            nc.vector.memset(w_sc[:].rearrange("p s n -> p (s n)").bitcast(I32), 0)
             make_identity(nc, ident[:])
             nc.vector.tensor_reduce(
                 out=block[:], in_=ident[:].rearrange("p (n l) -> p n l", l=L + 1), axis=mybir.AxisListType.X, op=ADD
@@ -128,14 +116,15 @@ def tile_focalmodulationqueryweightgrad_w4_kernel(
         w_in = {"h": (wh_words, wh_scales, 0), "p": (wp_words, wp_scales, A)}
 
         def load_w(key):
-            t, pad = placed(f"w_{key}", [A, 2 * D], U8, 1, 128)
-            w_sb[key] = t[:, pad:].rearrange("p (a n) -> p a n", a=A)
-            nc.sync.dma_start(out=w_sb[key].bitcast(I32), in_=w_in[key][0].bitcast(I32).rearrange("a p n -> p a n"))
+            t = keep.tile([P, A, 2 * D], U8, name=f"w_{key}", align_bytes=64)
+            nc.sync.dma_start(out=t[:].bitcast(I32), in_=w_in[key][0].bitcast(I32).rearrange("a p n -> p a n"))
+            w_sb[key] = t
 
         def load_w_scales(key, queue, rows=range(4)):
+            slot = w_in[key][2]
             sv = w_in[key][1].bitcast(I32).rearrange("a (q r) n -> r q a n", r=4)
             for r in rows:
-                queue.dma_start(out=w_sc[key][r:P:32, :, :].bitcast(I32), in_=sv[r])
+                queue.dma_start(out=w_sc[r:P:32, slot : slot + A, :].bitcast(I32), in_=sv[r])
 
         turned = {}
         kin = {}
@@ -176,9 +165,9 @@ def tile_focalmodulationqueryweightgrad_w4_kernel(
 
         def quantise_cg(h, j, first=0, count=A):
             if (h, j) not in cg:
-                q, _ = placed(f"cgq{h}{j}", [A * 2 * P], U32, 4, 0)
-                s, pad = placed(f"cgs{h}{j}", [A * 2 * P], U8, 1, 64)
-                cg[h, j] = (q, s[:, pad:])
+                q = keep.tile([P, A * 2 * P], U32, name=f"cgq{h}{j}", align_bytes=64)
+                s = keep.tile([P, A * 2 * P], U8, name=f"cgs{h}{j}", align_bytes=64)
+                cg[h, j] = (q, s)
             q, s = cg[h, j]
             cols = slice(2 * P * first, 2 * P * (first + count))
             src = kin[h, j][:, first : first + count, :, :, :]
@@ -195,7 +184,7 @@ def tile_focalmodulationqueryweightgrad_w4_kernel(
                     lhsT=q[:, cols].bitcast(FP8X4),
                     lhsT_scale=s[:, cols],
                     rhs=w_sb[key][:, a, 2 * col0 : 2 * (col0 + width)].bitcast(FP4X4),
-                    rhs_scale=w_sc[key][:, a, col0 : col0 + width],
+                    rhs_scale=w_sc[:, slot + a, col0 : col0 + width],
                     start=(a == 0),
                     stop=(a == A - 1),
                 )
@@ -278,9 +267,9 @@ def tile_focalmodulationqueryweightgrad_w4_kernel(
         codes = {}
         for key in ("x", "s"):
             for h in range(H):
-                q, qpad = placed(f"{key}q{h}", [D], U32, 4, 0 if key == "x" else 128)
-                s, spad = placed(f"{key}s{h}", [D], U8, 1, 64 if key == "x" else 192)
-                codes[key, h] = (q[:, qpad:], s[:, spad:])
+                q = keep.tile([P, D], U32, name=f"{key}q{h}", align_bytes=64)
+                s = keep.tile([P, D], U8, name=f"{key}s{h}", align_bytes=64)
+                codes[key, h] = (q, s)
 
         def quantise_t(key, h, q):
             cq, cs = codes[key, h]

@@ -24,7 +24,8 @@ H = 2
 A = 2
 U = 4
 NT = 32
-EB = 128
+QW = 256
+NQ = D // QW
 WIDE = 512
 BANKS = {"gt": 3, "mp": 5}
 
@@ -43,7 +44,7 @@ def tile_focalmodulationqueryweightgrad_w4_kernel(
 
         raw_gates = keep.tile([P, H, 48], BF16, name="raw_gates")
         bh_row = keep.tile([P, D], BF16, name="bh_row")
-        w_sc = keep.tile([P, 2 * A, D], U8, name="w_sc", align_bytes=64)
+        w_sc = {key: keep.tile([P, A, D], U8, name=f"w_sc{key}", align_bytes=64) for key in "hp"}
         ident = keep.tile([P, P], BF16, name="ident")
         ones = keep.tile([P, P], BF16, name="ones")
         block = keep.tile([P, NT], F32, name="block")
@@ -55,23 +56,24 @@ def tile_focalmodulationqueryweightgrad_w4_kernel(
             nc.gpsimd.memset(raw_gates[:], 0.0)
             nc.vector.memset(bh_row[:], 0.0)
             nc.vector.memset(ones[:], 1.0)
-            nc.vector.memset(w_sc[:].rearrange("p s n -> p (s n)").bitcast(I32), 0)
+            for key in "hp":
+                nc.vector.memset(w_sc[key][:].rearrange("p s n -> p (s n)").bitcast(I32), 0)
             make_identity(nc, ident[:])
             nc.vector.tensor_reduce(
                 out=block[:], in_=ident[:].rearrange("p (n l) -> p n l", l=L + 1), axis=mybir.AxisListType.X, op=ADD
             )
             nc.vector.tensor_copy(out=table[:, H * U * J, :], in_=ident[:, L : P : L + 1])
 
-        def load_gates(queue):
+        def load_gates():
             rows = gates.rearrange("(h n r) l -> n h (r l)", h=H, r=U * J)
             for l in range(L):
-                queue.dma_start(out=raw_gates[l : P : L + 1, :, 0:46], in_=rows[:, :, l : l + 46])
+                nc.sync.dma_start(out=raw_gates[l : P : L + 1, :, 0:46], in_=rows[:, :, l : l + 46])
 
-        def load_bias(queue):
-            queue.dma_start(out=bh_row[0:1, :], in_=bh.rearrange("(o n) -> o n", o=1))
+        def load_bias():
+            nc.sync.dma_start(out=bh_row[0:1, :], in_=bh.rearrange("(o n) -> o n", o=1))
 
-        def load_xs(queue):
-            queue.dma_start(out=xs_sb[:], in_=x_scale.rearrange("(h m j) o -> m h (j o)", h=H, j=J))
+        def load_xs():
+            nc.sync.dma_start(out=xs_sb[:], in_=x_scale.rearrange("(h m j) o -> m h (j o)", h=H, j=J))
 
         def make_table(h):
             nc.vector.tensor_tensor(
@@ -81,27 +83,31 @@ def tile_focalmodulationqueryweightgrad_w4_kernel(
                 op=MULT,
             )
 
-        def spread_bias(engine="s"):
+        def copy(engine, dst, src):
+            if engine == "s":
+                nc.scalar.copy(out=dst, in_=src)
+            elif engine == "v":
+                nc.vector.tensor_copy(out=dst, in_=src)
+            else:
+                nc.gpsimd.tensor_scalar(out=dst, in0=src, scalar1=1.0, scalar2=0.0, op0=MULT, op1=ADD)
+
+        def spread_bias():
             b = psum.tile([P, D], BF16, name="bias", tag="mp", bufs=BANKS["mp"])
             for e in range(2):
                 cols = slice(WIDE * e, WIDE * (e + 1))
                 nc.tensor.matmul(b[:, cols], lhsT=ones[:], rhs=bh_row[:, cols], start=True, stop=True)
-            copy(engine, bh_bc[:], b[:])
+            copy("s", bh_bc[:], b[:])
 
         rows_of = [z[l].rearrange("(h n u j) d -> h n u (j d)", h=H, u=U, j=J) for l in range(L)]
         rows_of.append(g.rearrange("(h n u j) d -> h n u (j d)", h=H, u=U, j=J))
         zg = {}
 
-        def load_zg(h, j, levels=range(L + 1), a=None):
-            first, width = (0, D) if a is None else (WIDE * a, WIDE)
-            if (h, j, first) not in zg:
-                t = keep.tile([P, U, width], BF16, name=f"zg{h}{j}{first}", align_bytes=64)
-                for k in range(0, width, WIDE):
-                    zg[h, j, first + k] = (t, k)
-            t = zg[h, j, first][0]
+        def load_zg(t, levels=range(L + 1)):
+            h, j = divmod(t, J)
+            if t not in zg:
+                zg[t] = keep.tile([P, U, D], BF16, name=f"zg{t}", align_bytes=64)
             for l in levels:
-                src = rows_of[l][h][:, :, D * j + first : D * j + first + width]
-                nc.sync.dma_start(out=t[l : P : L + 1, :, :], in_=src)
+                nc.sync.dma_start(out=zg[t][l : P : L + 1, :, :], in_=rows_of[l][h][:, :, D * j : D * (j + 1)])
 
         x_view = x_bytes.rearrange("(h m j) n -> h m (j n)", h=H, j=J)
         x_sb = {}
@@ -113,379 +119,305 @@ def tile_focalmodulationqueryweightgrad_w4_kernel(
                 x_sb[h, first + j] = (t, D * j)
 
         w_sb = {}
-        w_in = {"h": (wh_words, wh_scales, 0), "p": (wp_words, wp_scales, A)}
+        w_in = {"h": (wh_words, wh_scales, 0), "p": (wp_words, wp_scales, 1)}
 
         def load_w(key):
             t = keep.tile([P, A, 2 * D], U8, name=f"w_{key}", align_bytes=64)
             nc.sync.dma_start(out=t[:].bitcast(I32), in_=w_in[key][0].bitcast(I32).rearrange("a p n -> p a n"))
             w_sb[key] = t
 
-        def load_w_scales(key, queue, rows=range(4)):
-            slot = w_in[key][2]
+        def load_w_scales(key, rows=range(4)):
             sv = w_in[key][1].bitcast(I32).rearrange("a (q r) n -> r q a n", r=4)
             for r in rows:
-                queue.dma_start(out=w_sc[r:P:32, slot : slot + A, :].bitcast(I32), in_=sv[r])
+                nc.sync.dma_start(out=w_sc[key][r:P:32, :, :].bitcast(I32), in_=sv[r])
 
         turned = {}
         kin = {}
         cg = {}
 
-        def turn(h, j, a, groups=range(U)):
-            t, first = zg[h, j, WIDE * a]
-            b = psum.tile([P, len(groups) * 4, 2, NT], BF16, name=f"gt{h}{j}{a}{groups[0]}", tag="gt", bufs=BANKS["gt"])
-            for n, u in enumerate(groups):
+        def turn(t, a):
+            h, j = divmod(t, J)
+            b = psum.tile([P, U * 4, 2, NT], BF16, name=f"gt{t}{a}", tag="gt", bufs=BANKS["gt"])
+            last = H * U * J
+            for u in range(U):
                 i = U * J * h + J * u + j
-                last = H * U * J
                 for k in range(4):
                     nc.tensor.matmul(
-                        b[:, 4 * n + k, :, :],
-                        lhsT=t[:, u, first + k : first + WIDE : 4],
+                        b[:, 4 * u + k, :, :],
+                        lhsT=zg[t][:, u, WIDE * a + k : WIDE * (a + 1) : 4],
                         rhs=table[:, i : last + 1 : last - i, :],
                         start=True,
                         stop=True,
                     )
-            turned[h, j, a, groups[0]] = b
+            turned[t, a] = b
 
-        def copy(engine, dst, src):
-            if engine == "s":
-                nc.scalar.copy(out=dst, in_=src)
-            elif engine == "v":
-                nc.vector.tensor_copy(out=dst, in_=src)
-            else:
-                nc.gpsimd.tensor_scalar(out=dst, in0=src, scalar1=1.0, scalar2=0.0, op0=MULT, op1=ADD)
+        def take(t, a, engine):
+            if t not in kin:
+                kin[t] = work.tile([P, A, 2, NT, U * 4], BF16, name=f"kin{t}", tag="kin", bufs=3, align_bytes=64)
+            copy(engine, kin[t][:, a, :, :, :], turned[t, a][:].rearrange("p s c n -> p c n s"))
 
-        def take(h, j, a, engine, groups=range(U)):
-            if (h, j) not in kin:
-                kin[h, j] = work.tile([P, A, 2, NT, U * 4], BF16, name=f"kin{h}{j}", tag="kin", bufs=3, align_bytes=64)
-            dst = kin[h, j][:, a, :, :, 4 * groups[0] : 4 * (groups[-1] + 1)]
-            copy(engine, dst, turned[h, j, a, groups[0]][:].rearrange("p s c n -> p c n s"))
+        def turn_take(t, e0="s", e1="s"):
+            turn(t, 0)
+            take(t, 0, e0)
+            turn(t, 1)
+            take(t, 1, e1)
 
         def quantise(dst, scales, src):
             nc.vector.quantize_mx(out=dst.bitcast(FP8X4), scales=scales, in_=src)
 
-        def quantise_cg(h, j, first=0, count=A):
-            if (h, j) not in cg:
-                q = keep.tile([P, A * 2 * P], U32, name=f"cgq{h}{j}", align_bytes=64)
-                s = keep.tile([P, A * 2 * P], U8, name=f"cgs{h}{j}", align_bytes=64)
-                cg[h, j] = (q, s)
-            q, s = cg[h, j]
+        def quantise_cg(t, first=0, count=A):
+            if t not in cg:
+                q = keep.tile([P, A * 2 * P], U32, name=f"cgq{t}", align_bytes=64)
+                s = keep.tile([P, A * 2 * P], U8, name=f"cgs{t}", align_bytes=64)
+                cg[t] = (q, s)
+            q, s = cg[t]
             cols = slice(2 * P * first, 2 * P * (first + count))
-            src = kin[h, j][:, first : first + count, :, :, :]
+            src = kin[t][:, first : first + count, :, :, :]
             quantise(q[:, cols], s[:, cols], src.rearrange("p a c n s -> p (a c n s)"))
-
-        def passes(dst, key, h, j, col0, width):
-            q, s = cg[h, j]
-            slot = w_in[key][2]
-            for a in range(A):
-                first = P * (2 * a + slot // A)
-                cols = slice(first, first + P)
-                nc.tensor.matmul_mx(
-                    dst,
-                    lhsT=q[:, cols].bitcast(FP8X4),
-                    lhsT_scale=s[:, cols],
-                    rhs=w_sb[key][:, a, 2 * col0 : 2 * (col0 + width)].bitcast(FP4X4),
-                    rhs_scale=w_sc[:, slot + a, col0 : col0 + width],
-                    start=(a == 0),
-                    stop=(a == A - 1),
-                )
 
         mp = {}
         mb = {}
+        paired = {}
+        woven = {}
 
-        def product0(key, j, e):
-            b = psum.tile([P, WIDE], F32, name=f"{key}0{j}{e}", tag="mp", bufs=BANKS["mp"])
-            passes(b[:], key, 0, j, WIDE * e, WIDE)
-            mp[key, 0, j, e] = b
+        def product(key, k, q, slots=range(2), tag="mp"):
+            if (key, k, q) not in mp:
+                mp[key, k, q] = psum.tile([P, 2, QW], F32, name=f"{key}{k}{q}", tag=tag, bufs=BANKS[tag])
+            for i in slots:
+                codes, scales = cg[2 * k + i]
+                for a in range(A):
+                    first = P * (2 * a + w_in[key][2])
+                    cols = slice(first, first + P)
+                    nc.tensor.matmul_mx(
+                        mp[key, k, q][:, i, :],
+                        lhsT=codes[:, cols].bitcast(FP8X4),
+                        lhsT_scale=scales[:, cols],
+                        rhs=w_sb[key][:, a, 2 * QW * q : 2 * QW * (q + 1)].bitcast(FP4X4),
+                        rhs_scale=w_sc[key][:, a, QW * q : QW * (q + 1)],
+                        start=(a == 0),
+                        stop=(a == A - 1),
+                    )
 
-        def bias0(j, e):
-            t = work.tile([P, WIDE], F32, name=f"mb0{j}{e}", tag="mb", bufs=4)
-            nc.vector.tensor_tensor(out=t[:], in0=mp["h", 0, j, e][:], in1=bh_bc[:, WIDE * e : WIDE * (e + 1)], op=ADD)
-            mb[0, j, e] = t
-
-        s_slots = keep.tile([P, J, D], BF16, name="s_slots")
-
-        def times0(j, e):
-            nc.vector.tensor_tensor(
-                out=s_slots[:, j, WIDE * e : WIDE * (e + 1)], in0=mp["p", 0, j, e][:], in1=mb[0, j, e][:], op=MULT
-            )
-
-        def product1(key, e, slots=range(J), tag="mp"):
-            if (key, 1, e) not in mp:
-                mp[key, 1, e] = psum.tile([P, J, EB], F32, name=f"{key}1{e}", tag=tag, bufs=BANKS[tag])
-            for j in slots:
-                passes(mp[key, 1, e][:, j, :], key, 1, j, EB * e, EB)
-
-        def bias1(e):
-            t = work.tile([P, EB, J], F32, name=f"mb1{e}", tag="mb", bufs=4)
+        def bias(k, q):
+            t = work.tile([P, QW, 2], F32, name=f"mb{k}{q}", tag="mb", bufs=4)
             nc.vector.tensor_tensor(
                 out=t[:],
-                in0=mp["h", 1, e][:].rearrange("p j n -> p n j"),
-                in1=bh_bc[:, EB * e : EB * (e + 1)].unsqueeze(2).to_broadcast([P, EB, J]),
+                in0=mp["h", k, q][:].rearrange("p i n -> p n i"),
+                in1=bh_bc[:, QW * q : QW * (q + 1)].unsqueeze(2).to_broadcast([P, QW, 2]),
                 op=ADD,
             )
-            mb[1, e] = t
+            mb[k, q] = t
 
-        woven = {}
-        QW = 256
-
-        def times1(e):
-            if e % 2 == 0:
-                woven["s", 1, e // 2] = work.tile([P, QW, J], BF16, name=f"s1_{e}", tag="s1", bufs=2, align_bytes=64)
+        def times(k, q):
+            h, r = divmod(k, 2)
+            if (h, q) not in paired:
+                paired[h, q] = keep.tile([P, 2, QW, 2], BF16, name=f"sp{h}{q}", align_bytes=64)
             nc.vector.tensor_tensor(
-                out=woven["s", 1, e // 2][:, EB * (e % 2) : EB * (e % 2 + 1), :],
-                in0=mp["p", 1, e][:].rearrange("p j n -> p n j"),
-                in1=mb[1, e][:],
-                op=MULT,
+                out=paired[h, q][:, r, :, :], in0=mp["p", k, q][:].rearrange("p i n -> p n i"), in1=mb[k, q][:], op=MULT
             )
+
+        def weave_s(h, q, engine="s"):
+            t = work.tile([P, QW, J], BF16, name=f"s{h}_{q}", tag="sw", bufs=8, align_bytes=64)
+            word = U32 if engine == "s" else I32
+            words = paired[h, q][:].rearrange("p r n i -> p r (n i)").bitcast(word)
+            copy(engine, t[:].bitcast(word), words.rearrange("p r n -> p n r"))
+            woven["s", h, q] = t
 
         x_slots = {}
 
-        def widen(h, j, c, engine):
+        def widen(h, c, engine, slots=range(J)):
             if (h, c) not in x_slots:
                 x_slots[h, c] = keep.tile([P, J, WIDE], BF16, name=f"xw{h}{c}")
-            dst = x_slots[h, c][:, j, :]
-            t, first = x_sb[h, j]
-            src = t[:, first + WIDE * c : first + WIDE * (c + 1)].bitcast(FP8)
-            scale = xs_sb[:, h, j : j + 1]
-            if engine == "s":
-                nc.scalar.activation(out=dst, in_=src, func=COPY, scale=scale)
-            else:
-                nc.vector.tensor_scalar(out=dst, in0=src, scalar1=scale, scalar2=None, op0=MULT)
+            for j in slots:
+                dst = x_slots[h, c][:, j, :]
+                t, first = x_sb[h, j]
+                src = t[:, first + WIDE * c : first + WIDE * (c + 1)].bitcast(FP8)
+                scale = xs_sb[:, h, j : j + 1]
+                if engine == "s":
+                    nc.scalar.activation(out=dst, in_=src, func=COPY, scale=scale)
+                else:
+                    nc.vector.tensor_scalar(out=dst, in0=src, scalar1=scale, scalar2=None, op0=MULT)
 
-        def weave(key, h, q, engine):
-            t = work.tile([P, QW, J], BF16, name=f"{key}{h}_{q}", tag="gw" if engine == "g" else "wv", bufs=1 if engine == "g" else 6, align_bytes=64)
-            if key == "s":
-                src = s_slots[:, :, QW * q : QW * (q + 1)]
-            else:
-                src = x_slots[h, q // 2][:, :, QW * (q % 2) : QW * (q % 2 + 1)]
+        def weave_x(h, q, engine):
+            src = x_slots[h, q // 2][:, :, QW * (q % 2) : QW * (q % 2 + 1)]
             if engine == "g":
+                t = work.tile([P, QW, J], BF16, name=f"x{h}_{q}", tag="gw", bufs=1, align_bytes=64)
                 copy(engine, t[:], src.rearrange("p j n -> p n j"))
             else:
+                t = work.tile([P, QW, J], BF16, name=f"x{h}_{q}", tag="xw", bufs=4, align_bytes=64)
                 copy(engine, t[:].rearrange("p (c i) j -> p c j i", i=4), src.rearrange("p j (c i) -> p c j i", i=4))
-            woven[key, h, q] = t
+            woven["x", h, q] = t
 
-        codes = {}
+        codes_t = {}
         for key in ("x", "s"):
             for h in range(H):
-                q = keep.tile([P, D], U32, name=f"{key}q{h}", align_bytes=64)
-                s = keep.tile([P, D], U8, name=f"{key}s{h}", align_bytes=64)
-                codes[key, h] = (q, s)
+                cq = keep.tile([P, D], U32, name=f"{key}q{h}", align_bytes=64)
+                cs = keep.tile([P, D], U8, name=f"{key}s{h}", align_bytes=64)
+                codes_t[key, h] = (cq, cs)
 
         def quantise_t(key, h, q):
-            cq, cs = codes[key, h]
+            cq, cs = codes_t[key, h]
             cols = slice(QW * q, QW * (q + 1))
             quantise(cq[:, cols], cs[:, cols], woven[key, h, q][:].rearrange("p n t -> p (n t)"))
 
-        res = {}
-
-        def final(q, rp):
-            b = psum.tile([P, 2, QW], F32, name=f"o{q}{rp}", tag="gt", bufs=BANKS["gt"])
-            for i in range(2):
-                rows = slice(QW * rp + P * i, QW * rp + P * (i + 1))
-                cols = slice(QW * q, QW * (q + 1))
-                for h in range(H):
-                    xq, xs = codes["x", h]
-                    sq, ss = codes["s", h]
-                    nc.tensor.matmul_mx(
-                        b[:, i, :],
-                        lhsT=xq[:, rows].bitcast(FP8X4),
-                        lhsT_scale=xs[:, rows],
-                        rhs=sq[:, cols].bitcast(FP8X4),
-                        rhs_scale=ss[:, cols],
-                        start=(h == 0),
-                        stop=(h == H - 1),
-                    )
-            res[q, rp] = b
-
-        def store(q, rp, engine):
-            t = work.tile([P, 2, QW], F32, name=f"ob{q}{rp}", tag="ob", bufs=10)
+        def finish(c, r, engine="s", tag="gt"):
+            b = psum.tile([P, WIDE], F32, name=f"o{c}{r}", tag=tag, bufs=BANKS[tag])
+            cols = slice(WIDE * c, WIDE * (c + 1))
+            rows = slice(P * r, P * (r + 1))
+            for h in range(H):
+                xq, xs = codes_t["x", h]
+                sq, ss = codes_t["s", h]
+                nc.tensor.matmul_mx(
+                    b[:],
+                    lhsT=xq[:, rows].bitcast(FP8X4),
+                    lhsT_scale=xs[:, rows],
+                    rhs=sq[:, cols].bitcast(FP8X4),
+                    rhs_scale=ss[:, cols],
+                    start=(h == 0),
+                    stop=(h == H - 1),
+                )
+            t = work.tile([P, WIDE], F32, name=f"ob{c}{r}", tag="ob", bufs=10)
             if engine == "s":
-                nc.scalar.activation(out=t[:], in_=res[q, rp][:], func=COPY, scale=1.0 / 32.0)
+                nc.scalar.activation(out=t[:], in_=b[:], func=COPY, scale=1.0 / 32.0)
             else:
-                nc.vector.tensor_scalar(out=t[:], in0=res[q, rp][:], scalar1=1.0 / 32.0, scalar2=None, op0=MULT)
-            rows = out[QW * rp : QW * (rp + 1), QW * q : QW * (q + 1)]
-            nc.sync.dma_start(out=rows.rearrange("(i p) n -> p i n", p=P), in_=t[:])
+                nc.vector.tensor_scalar(out=t[:], in0=b[:], scalar1=1.0 / 32.0, scalar2=None, op0=MULT)
+            nc.sync.dma_start(out=out[rows, cols], in_=t[:])
 
         constants()
-        load_zg(0, 0, (0, 1))
-        load_bias(nc.sync)
-        load_gates(nc.sync)
-        load_zg(0, 0, (2, 3))
-        load_zg(0, 1, (0, 1))
-        load_w_scales("h", nc.sync, (0, 1, 2))
-        load_zg(0, 1, (2, 3))
+        load_zg(0, (0, 1))
+        load_bias()
+        load_gates()
+        load_zg(0, (2, 3))
+        load_zg(1, (0, 1))
+        load_w_scales("h", (0, 1, 2))
+        load_zg(1, (2, 3))
         load_w("h")
-        load_w_scales("h", nc.sync, (3,))
-        load_w_scales("p", nc.sync, (0, 1))
+        load_w_scales("h", (3,))
+        load_xs()
+        load_x(0)
+        load_zg(2)
+        load_w_scales("p", (0, 1))
         load_w("p")
-        load_w_scales("p", nc.sync, (2, 3))
-        load_x(0, 0, 2)
-        load_xs(nc.sync)
-        load_zg(0, 2)
-        load_zg(0, 3)
-        load_x(0, 2, 2)
-        for j in range(J - 1):
-            load_zg(1, j)
-        for a in range(A):
-            load_zg(1, J - 1, a=a)
+        load_w_scales("p", (2, 3))
+        load_zg(3)
+        load_zg(4)
+        load_zg(5)
         load_x(1)
+        load_zg(6)
+        load_zg(7)
         make_table(0)
         make_table(1)
 
-        def turn_take(h, j, e0, e1):
-            turn(h, j, 0)
-            take(h, j, 0, e0)
-            turn(h, j, 1)
-            take(h, j, 1, e1)
+        def m_two(k, q, slots=range(2)):
+            for e in (q, q + 1):
+                product("h", k, e, slots)
+            for e in (q, q + 1):
+                bias(k, e)
 
-        def m_pair(j):
-            for e in range(2):
-                product0("h", j, e)
-                bias0(j, e)
+        def p_two(k, q, slots=range(2)):
+            for e in (q, q + 1):
+                product("p", k, e, slots)
+            for e in (q, q + 1):
+                times(k, e)
 
-        def p_pair(j):
-            for e in range(2):
-                product0("p", j, e)
-                times0(j, e)
+        def ahead(k, banks):
+            for key, q in banks:
+                product(key, k, q, (0,))
 
-        def widen_all(h, c, engine):
-            for j in range(J):
-                widen(h, j, c, engine)
-
-        def step(e):
-            product1("h", e + 1)
-            bias1(e + 1)
-            product1("p", e)
-            times1(e)
-
-        def finish(q, rp, engine="s"):
-            final(q, rp)
-            store(q, rp, engine)
+        def next_x(h, q):
+            quantise_t("x", h, q)
+            if NQ * h + q + 1 < H * NQ:
+                weave_x(*divmod(NQ * h + q + 1, NQ), "g")
 
         spread_bias()
-        turn_take(0, 0, "s", "v")
-        quantise_cg(0, 0)
-        turn_take(0, 1, "s", "v")
-        product0("h", 0, 0)
-        product0("h", 0, 1)
-        quantise_cg(0, 1)
-        bias0(0, 0)
-        bias0(0, 1)
-        p_pair(0)
-        for c in range(2):
-            for j in range(2):
-                widen(0, j, c, "s")
-        m_pair(1)
-        turn_take(0, 2, "s", "v")
-        product0("p", 1, 0)
-        product0("p", 1, 1)
-        quantise_cg(0, 2)
-        times0(1, 0)
-        times0(1, 1)
-        turn_take(0, 3, "s", "s")
-        widen(0, 2, 0, "v")
-        m_pair(2)
-        widen(0, 2, 1, "s")
-        widen(0, 3, 1, "s")
-        quantise_cg(0, 3)
-        p_pair(2)
-        widen(0, 3, 0, "v")
-        weave("x", 0, 0, "v")
-        weave("x", 0, 1, "g")
-        turn_take(1, 0, "s", "s")
-        m_pair(3)
-        turn_take(1, 1, "s", "s")
-        quantise_cg(1, 0)
-        p_pair(3)
-        quantise_cg(1, 1)
-        weave("x", 0, 2, "v")
-        turn_take(1, 2, "s", "s")
-        turn(1, 3, 0)
-        take(1, 3, 0, "v")
-        first = (("h", 0), ("h", 1), ("p", 0), ("p", 1), ("h", 2))
-        for key, e in first:
-            product1(key, e, (0,))
-        turn(1, 3, 1, (0, 1))
-        take(1, 3, 1, "s", (0, 1))
-        for key, e in first[:3]:
-            product1(key, e, (1,))
-        turn(1, 3, 1, (2, 3))
-        quantise_cg(1, 2)
-        take(1, 3, 1, "s", (2, 3))
-        quantise_cg(1, 3, 0, 1)
-        quantise_t("x", 0, 0)
-        for key, e in first[3:]:
-            product1(key, e, (1,))
-        for key, e in first:
-            product1(key, e, (2,))
-        quantise_cg(1, 3, 1, 1)
-        weave("s", 0, 0, "v")
-        quantise_t("x", 0, 1)
-        weave("s", 0, 1, "g")
-        widen_all(1, 0, "s")
-        product1("h", 0, (3,))
-        bias1(0)
-        product1("h", 1, (3,))
-        bias1(1)
-        product1("p", 0, (3,))
-        times1(0)
-        product1("p", 1, (3,))
-        product1("h", 2, (3,))
-        times1(1)
-        weave("x", 1, 0, "s")
-        widen_all(1, 1, "s")
-        product1("p", 2, tag="gt")
-        product1("h", 3)
-        bias1(2)
-        product1("p", 3)
-        product1("h", 4)
+        turn_take(0, "s", "v")
+        quantise_cg(0)
+        turn_take(1, "s", "v")
+        ahead(0, [("h", q) for q in range(NQ)])
+        quantise_cg(1)
+        widen(0, 0, "s")
+        weave_x(0, 0, "g")
+        widen(0, 1, "s", (0, 1))
+        m_two(0, 0, (1,))
+        m_two(0, 2, (1,))
+        turn_take(2)
+        next_x(0, 0)
+        p_two(0, 0)
+        widen(0, 1, "s", (2, 3))
+        for q in (2, 3):
+            product("p", 0, q)
+        times(0, 2)
+        quantise_cg(2)
+        times(0, 3)
+        turn_take(3, "s", "v")
+        ahead(1, [("h", 0), ("h", 1), ("p", 0), ("p", 1)])
+        quantise_cg(3)
+        next_x(0, 1)
+        turn_take(4)
+        m_two(1, 0, (1,))
+        p_two(1, 0, (1,))
+        turn_take(5)
+        quantise_cg(4)
+        next_x(0, 2)
+        m_two(1, 2)
+        for q in (2, 3):
+            product("p", 1, q)
+        times(1, 2)
+        ahead(2, [("h", 0), ("h", 1)])
+        quantise_cg(5)
+        quantise_t("x", 0, 3)
+        widen(1, 0, "s")
+        weave_x(1, 0, "g")
+        turn_take(6)
+        times(1, 3)
+        m_two(2, 0, (1,))
+        p_two(2, 0)
+        weave_s(0, 0)
+        turn_take(7)
+        quantise_cg(6)
+        next_x(1, 0)
+        m_two(2, 2)
+        widen(1, 1, "s")
+        for q in (2, 3):
+            product("p", 2, q)
+        times(2, 2)
+        ahead(3, [("h", 0), ("h", 1), ("p", 0)])
+        quantise_cg(7)
         quantise_t("s", 0, 0)
-        quantise_t("x", 1, 0)
+        next_x(1, 1)
+        times(2, 3)
+        for q in range(1, NQ):
+            weave_s(0, q)
+        m_two(3, 0, (1,))
+        product("p", 3, 0, (1,))
+        product("p", 3, 1)
+        times(3, 0)
+        times(3, 1)
+        product("h", 3, 2)
+        product("h", 3, 3)
+        weave_s(1, 0, "v")
+        weave_s(1, 1, "v")
         quantise_t("s", 1, 0)
         quantise_t("s", 0, 1)
-        weave("x", 1, 1, "g")
-        weave("x", 1, 2, "s")
-        bias1(3)
-        product1("h", 5)
-        times1(2)
-        finish(0, 0)
-        weave("x", 0, 3, "s")
-        product1("p", 4)
-        times1(3)
-        bias1(4)
-        product1("p", 5)
         quantise_t("s", 1, 1)
-        quantise_t("x", 1, 2)
-        quantise_t("x", 1, 1)
-        weave("x", 1, 3, "g")
-        bias1(5)
-        product1("h", 6)
-        finish(1, 0)
-        finish(0, 1)
-        times1(4)
-        finish(1, 1)
-        weave("s", 0, 2, "s")
-        times1(5)
-        quantise_t("x", 0, 2)
-        quantise_t("x", 0, 3)
-        quantise_t("s", 1, 2)
-        quantise_t("x", 1, 3)
-        weave("s", 0, 3, "g")
-        product1("h", 7)
-        product1("p", 6)
-        product1("p", 7)
-        bias1(6)
-        bias1(7)
-        finish(0, 2)
-        finish(1, 2)
-        times1(6)
-        finish(0, 3)
-        times1(7)
-        finish(1, 3)
+        next_x(1, 2)
+        product("p", 3, 2)
+        product("p", 3, 3)
+        bias(3, 2)
+        bias(3, 3)
+        finish(0, 0)
+        times(3, 2)
+        times(3, 3)
+        for r in range(1, 6):
+            finish(0, r)
+        next_x(1, 3)
+        weave_s(1, 2, "v")
+        weave_s(1, 3, "v")
         quantise_t("s", 0, 2)
         quantise_t("s", 0, 3)
+        quantise_t("s", 1, 2)
         quantise_t("s", 1, 3)
-        for n in range(4):
-            finish(2, n)
-        for n in range(4):
-            finish(3, n, "v" if n % 2 == 0 else "s")
+        finish(0, 6, tag="mp")
+        finish(0, 7, tag="mp")
+        for r in range(8):
+            finish(1, r, "v" if r % 2 == 0 else "s", tag="mp")

@@ -126,10 +126,10 @@ def tile_focalmodulationqueryweightgrad_w4_kernel(
             nc.sync.dma_start(out=t[:].bitcast(I32), in_=w_in[key][0].bitcast(I32).rearrange("a p n -> p a n"))
             w_sb[key] = t
 
-        def load_w_scales(key, rows=range(4)):
+        def load_w_scales(key, queue, rows=range(4)):
             sv = w_in[key][1].bitcast(I32).rearrange("a (q r) n -> r q a n", r=4)
             for r in rows:
-                nc.sync.dma_start(out=w_sc[key][r:P:32, :, :].bitcast(I32), in_=sv[r])
+                queue.dma_start(out=w_sc[key][r:P:32, :, :].bitcast(I32), in_=sv[r])
 
         turned = {}
         kin = {}
@@ -240,11 +240,11 @@ def tile_focalmodulationqueryweightgrad_w4_kernel(
 
         def weave_x(h, q, engine):
             src = x_slots[h, q // 2][:, :, QW * (q % 2) : QW * (q % 2 + 1)]
+            tag, bufs = ("xw", 2) if engine == "s" else ("gw", 1)
+            t = work.tile([P, QW, J], BF16, name=f"x{h}_{q}", tag=tag, bufs=bufs, align_bytes=64)
             if engine == "g":
-                t = work.tile([P, QW, J], BF16, name=f"x{h}_{q}", tag="gw", bufs=1, align_bytes=64)
                 copy(engine, t[:], src.rearrange("p j n -> p n j"))
             else:
-                t = work.tile([P, QW, J], BF16, name=f"x{h}_{q}", tag="xw", bufs=4, align_bytes=64)
                 copy(engine, t[:].rearrange("p (c i) j -> p c j i", i=4), src.rearrange("p j (c i) -> p c j i", i=4))
             woven["x", h, q] = t
 
@@ -260,9 +260,9 @@ def tile_focalmodulationqueryweightgrad_w4_kernel(
             cols = slice(QW * q, QW * (q + 1))
             quantise(cq[:, cols], cs[:, cols], woven[key, h, q][:].rearrange("p n t -> p (n t)"))
 
-        def finish(c, r, engine="s", tag="gt"):
-            b = psum.tile([P, WIDE], F32, name=f"o{c}{r}", tag=tag, bufs=BANKS[tag])
-            cols = slice(WIDE * c, WIDE * (c + 1))
+        def finish(c, r, engine="s", tag="gt", width=WIDE):
+            b = psum.tile([P, width], F32, name=f"o{width}{c}{r}", tag=tag, bufs=BANKS[tag])
+            cols = slice(width * c, width * (c + 1))
             rows = slice(P * r, P * (r + 1))
             for h in range(H):
                 xq, xs = codes_t["x", h]
@@ -276,7 +276,7 @@ def tile_focalmodulationqueryweightgrad_w4_kernel(
                     start=(h == 0),
                     stop=(h == H - 1),
                 )
-            t = work.tile([P, WIDE], F32, name=f"ob{c}{r}", tag="ob", bufs=10)
+            t = work.tile([P, width], F32, name=f"ob{width}{c}{r}", tag="ob", bufs=8)
             if engine == "s":
                 nc.scalar.activation(out=t[:], in_=b[:], func=COPY, scale=1.0 / 32.0)
             else:
@@ -289,16 +289,16 @@ def tile_focalmodulationqueryweightgrad_w4_kernel(
         load_gates()
         load_zg(0, (2, 3))
         load_zg(1, (0, 1))
-        load_w_scales("h", (0, 1, 2))
+        load_w_scales("h", nc.sync, (0, 1, 2))
         load_zg(1, (2, 3))
         load_w("h")
-        load_w_scales("h", (3,))
+        load_w_scales("h", nc.sync, (3,))
         load_xs()
         load_x(0)
         load_zg(2)
-        load_w_scales("p", (0, 1))
+        load_w_scales("p", nc.sync, (0, 1))
         load_w("p")
-        load_w_scales("p", (2, 3))
+        load_w_scales("p", nc.sync, (2, 3))
         load_zg(3)
         load_zg(4)
         load_zg(5)
@@ -306,7 +306,6 @@ def tile_focalmodulationqueryweightgrad_w4_kernel(
         load_zg(6)
         load_zg(7)
         make_table(0)
-        make_table(1)
 
         def m_two(k, q, slots=range(2)):
             for e in (q, q + 1):
@@ -324,24 +323,24 @@ def tile_focalmodulationqueryweightgrad_w4_kernel(
             for key, q in banks:
                 product(key, k, q, (0,))
 
-        def next_x(h, q):
-            quantise_t("x", h, q)
-            if NQ * h + q + 1 < H * NQ:
-                weave_x(*divmod(NQ * h + q + 1, NQ), "g")
-
         spread_bias()
         turn_take(0, "s", "v")
         quantise_cg(0)
         turn_take(1, "s", "v")
         ahead(0, [("h", q) for q in range(NQ)])
         quantise_cg(1)
+        make_table(1)
         widen(0, 0, "s")
-        weave_x(0, 0, "g")
         widen(0, 1, "s", (0, 1))
         m_two(0, 0, (1,))
-        m_two(0, 2, (1,))
+        weave_x(0, 0, "v")
+        for q in (2, 3):
+            product("h", 0, q, (1,))
+        bias(0, 2)
+        quantise_t("x", 0, 0)
+        weave_x(0, 1, "g")
+        bias(0, 3)
         turn_take(2)
-        next_x(0, 0)
         p_two(0, 0)
         widen(0, 1, "s", (2, 3))
         for q in (2, 3):
@@ -350,15 +349,17 @@ def tile_focalmodulationqueryweightgrad_w4_kernel(
         quantise_cg(2)
         times(0, 3)
         turn_take(3, "s", "v")
+        weave_x(0, 2, "s")
         ahead(1, [("h", 0), ("h", 1), ("p", 0), ("p", 1)])
         quantise_cg(3)
-        next_x(0, 1)
+        quantise_t("x", 0, 1)
+        weave_x(0, 3, "g")
         turn_take(4)
         m_two(1, 0, (1,))
         p_two(1, 0, (1,))
         turn_take(5)
         quantise_cg(4)
-        next_x(0, 2)
+        quantise_t("x", 0, 2)
         m_two(1, 2)
         for q in (2, 3):
             product("p", 1, q)
@@ -375,7 +376,6 @@ def tile_focalmodulationqueryweightgrad_w4_kernel(
         weave_s(0, 0)
         turn_take(7)
         quantise_cg(6)
-        next_x(1, 0)
         m_two(2, 2)
         widen(1, 1, "s")
         for q in (2, 3):
@@ -384,10 +384,14 @@ def tile_focalmodulationqueryweightgrad_w4_kernel(
         ahead(3, [("h", 0), ("h", 1), ("p", 0)])
         quantise_cg(7)
         quantise_t("s", 0, 0)
-        next_x(1, 1)
+        quantise_t("x", 1, 0)
+        weave_x(1, 1, "g")
         times(2, 3)
-        for q in range(1, NQ):
-            weave_s(0, q)
+        weave_s(0, 1)
+        weave_x(1, 2, "s")
+        weave_x(1, 3, "s")
+        weave_s(0, 2)
+        weave_s(0, 3)
         m_two(3, 0, (1,))
         product("p", 3, 0, (1,))
         product("p", 3, 1)
@@ -397,20 +401,21 @@ def tile_focalmodulationqueryweightgrad_w4_kernel(
         product("h", 3, 3)
         weave_s(1, 0, "v")
         weave_s(1, 1, "v")
-        quantise_t("s", 1, 0)
         quantise_t("s", 0, 1)
+        quantise_t("s", 1, 0)
         quantise_t("s", 1, 1)
-        next_x(1, 2)
+        quantise_t("x", 1, 1)
         product("p", 3, 2)
         product("p", 3, 3)
         bias(3, 2)
         bias(3, 3)
         finish(0, 0)
+        quantise_t("x", 1, 2)
         times(3, 2)
         times(3, 3)
+        quantise_t("x", 1, 3)
         for r in range(1, 6):
             finish(0, r)
-        next_x(1, 3)
         weave_s(1, 2, "v")
         weave_s(1, 3, "v")
         quantise_t("s", 0, 2)

@@ -27,7 +27,7 @@ NT = 32
 QW = 256
 NQ = D // QW
 WIDE = 512
-BANKS = {"gt": 3, "mp": 5}
+BANKS = 8
 
 FLOPS = 3 * 2 * T * D * D + 2 * L * T * D + 2 * T * D
 
@@ -51,6 +51,18 @@ def tile_focalmodulationqueryweightgrad_w4_kernel(
         table = keep.tile([P, H * U * J + 1, NT], BF16, name="table")
         xs_sb = keep.tile([P, H, J], F32, name="xs_sb")
         bh_bc = keep.tile([P, D], BF16, name="bh_bc")
+
+        empty = list(range(BANKS))
+        held = {}
+
+        def bank(name, shape, dtype):
+            n = empty[0]
+            empty.remove(n)
+            held[name] = n
+            return psum.tile(shape, dtype, name=name, tag=f"bank{n}")
+
+        def emptied(name):
+            empty.append(held[name])
 
         def constants():
             nc.gpsimd.memset(raw_gates[:], 0.0)
@@ -92,22 +104,27 @@ def tile_focalmodulationqueryweightgrad_w4_kernel(
                 nc.gpsimd.tensor_scalar(out=dst, in0=src, scalar1=1.0, scalar2=0.0, op0=MULT, op1=ADD)
 
         def spread_bias():
-            b = psum.tile([P, D], BF16, name="bias", tag="mp", bufs=BANKS["mp"])
+            b = bank("bias", [P, D], BF16)
             for e in range(2):
                 cols = slice(WIDE * e, WIDE * (e + 1))
                 nc.tensor.matmul(b[:, cols], lhsT=ones[:], rhs=bh_row[:, cols], start=True, stop=True)
             copy("s", bh_bc[:], b[:])
+            emptied("bias")
 
         rows_of = [z[l].rearrange("(h n u j) d -> h n u (j d)", h=H, u=U, j=J) for l in range(L)]
         rows_of.append(g.rearrange("(h n u j) d -> h n u (j d)", h=H, u=U, j=J))
         zg = {}
 
-        def load_zg(t, levels=range(L + 1)):
+        def load_zg(t, levels=range(L + 1), a=None):
             h, j = divmod(t, J)
-            if t not in zg:
-                zg[t] = keep.tile([P, U, D], BF16, name=f"zg{t}", align_bytes=64)
+            first, width = (0, D) if a is None else (WIDE * a, WIDE)
+            if (t, first) not in zg:
+                tile = keep.tile([P, U, width], BF16, name=f"zg{t}_{first}", align_bytes=64)
+                for k in range(0, width, WIDE):
+                    zg[t, first + k] = (tile, k)
             for l in levels:
-                nc.sync.dma_start(out=zg[t][l : P : L + 1, :, :], in_=rows_of[l][h][:, :, D * j : D * (j + 1)])
+                src = rows_of[l][h][:, :, D * j + first : D * j + first + width]
+                nc.sync.dma_start(out=zg[t, first][0][l : P : L + 1, :, :], in_=src)
 
         x_view = x_bytes.rearrange("(h m j) n -> h m (j n)", h=H, j=J)
         x_sb = {}
@@ -137,14 +154,15 @@ def tile_focalmodulationqueryweightgrad_w4_kernel(
 
         def turn(t, a):
             h, j = divmod(t, J)
-            b = psum.tile([P, U * 4, 2, NT], BF16, name=f"gt{t}{a}", tag="gt", bufs=BANKS["gt"])
+            tile, first = zg[t, WIDE * a]
+            b = bank(f"gt{t}{a}", [P, U * 4, 2, NT], BF16)
             last = H * U * J
             for u in range(U):
                 i = U * J * h + J * u + j
                 for k in range(4):
                     nc.tensor.matmul(
                         b[:, 4 * u + k, :, :],
-                        lhsT=zg[t][:, u, WIDE * a + k : WIDE * (a + 1) : 4],
+                        lhsT=tile[:, u, first + k : first + WIDE : 4],
                         rhs=table[:, i : last + 1 : last - i, :],
                         start=True,
                         stop=True,
@@ -153,8 +171,9 @@ def tile_focalmodulationqueryweightgrad_w4_kernel(
 
         def take(t, a, engine):
             if t not in kin:
-                kin[t] = work.tile([P, A, 2, NT, U * 4], BF16, name=f"kin{t}", tag="kin", bufs=3, align_bytes=64)
-            copy(engine, kin[t][:, a, :, :, :], turned[t, a][:].rearrange("p s c n -> p c n s"))
+                kin[t] = work.tile([P, A, 2 * NT, U * 4], BF16, name=f"kin{t}", tag="kin", bufs=3, align_bytes=64)
+            copy(engine, kin[t][:, a, :, :], turned[t, a][:].rearrange("p s c n -> p (c n) s"))
+            emptied(f"gt{t}{a}")
 
         def turn_take(t, e0="s", e1="s"):
             turn(t, 0)
@@ -172,17 +191,17 @@ def tile_focalmodulationqueryweightgrad_w4_kernel(
                 cg[t] = (q, s)
             q, s = cg[t]
             cols = slice(2 * P * first, 2 * P * (first + count))
-            src = kin[t][:, first : first + count, :, :, :]
-            quantise(q[:, cols], s[:, cols], src.rearrange("p a c n s -> p (a c n s)"))
+            src = kin[t][:, first : first + count, :, :]
+            quantise(q[:, cols], s[:, cols], src.rearrange("p a n s -> p (a n s)"))
 
         mp = {}
         mb = {}
         paired = {}
         woven = {}
 
-        def product(key, k, q, slots=range(2), tag="mp"):
+        def product(key, k, q, slots=range(2)):
             if (key, k, q) not in mp:
-                mp[key, k, q] = psum.tile([P, 2, QW], F32, name=f"{key}{k}{q}", tag=tag, bufs=BANKS[tag])
+                mp[key, k, q] = bank(f"{key}{k}{q}", [P, 2, QW], F32)
             for i in slots:
                 codes, scales = cg[2 * k + i]
                 for a in range(A):
@@ -207,6 +226,7 @@ def tile_focalmodulationqueryweightgrad_w4_kernel(
                 op=ADD,
             )
             mb[k, q] = t
+            emptied(f"h{k}{q}")
 
         def times(k, q):
             h, r = divmod(k, 2)
@@ -215,9 +235,11 @@ def tile_focalmodulationqueryweightgrad_w4_kernel(
             nc.vector.tensor_tensor(
                 out=paired[h, q][:, r, :, :], in0=mp["p", k, q][:].rearrange("p i n -> p n i"), in1=mb[k, q][:], op=MULT
             )
+            emptied(f"p{k}{q}")
 
-        def weave_s(h, q, engine="s"):
-            t = work.tile([P, QW, J], BF16, name=f"s{h}_{q}", tag="sw", bufs=8, align_bytes=64)
+        def weave_s(h, q, engine="s", chained=False):
+            tag, bufs = ("gw", 1) if chained else ("sw", 6)
+            t = work.tile([P, QW, J], BF16, name=f"s{h}_{q}", tag=tag, bufs=bufs, align_bytes=64)
             word = U32 if engine == "s" else I32
             words = paired[h, q][:].rearrange("p r n i -> p r (n i)").bitcast(word)
             copy(engine, t[:].bitcast(word), words.rearrange("p r n -> p n r"))
@@ -238,9 +260,9 @@ def tile_focalmodulationqueryweightgrad_w4_kernel(
                 else:
                     nc.vector.tensor_scalar(out=dst, in0=src, scalar1=scale, scalar2=None, op0=MULT)
 
-        def weave_x(h, q, engine):
+        def weave_x(h, q, engine, chained=True):
             src = x_slots[h, q // 2][:, :, QW * (q % 2) : QW * (q % 2 + 1)]
-            tag, bufs = ("xw", 2) if engine == "s" else ("gw", 1)
+            tag, bufs = ("gw", 1) if chained else ("xw", 3)
             t = work.tile([P, QW, J], BF16, name=f"x{h}_{q}", tag=tag, bufs=bufs, align_bytes=64)
             if engine == "g":
                 copy(engine, t[:], src.rearrange("p j n -> p n j"))
@@ -260,8 +282,35 @@ def tile_focalmodulationqueryweightgrad_w4_kernel(
             cols = slice(QW * q, QW * (q + 1))
             quantise(cq[:, cols], cs[:, cols], woven[key, h, q][:].rearrange("p n t -> p (n t)"))
 
-        def finish(c, r, engine="s", tag="gt", width=WIDE):
-            b = psum.tile([P, width], F32, name=f"o{width}{c}{r}", tag=tag, bufs=BANKS[tag])
+        def finish_quarter(q, rp, engine):
+            name = f"oq{q}{rp}"
+            b = bank(name, [P, 2, QW], F32)
+            cols = slice(QW * q, QW * (q + 1))
+            for i in range(2):
+                rows = slice(QW * rp + P * i, QW * rp + P * (i + 1))
+                for h in range(H):
+                    xq, xs = codes_t["x", h]
+                    sq, ss = codes_t["s", h]
+                    nc.tensor.matmul_mx(
+                        b[:, i, :],
+                        lhsT=xq[:, rows].bitcast(FP8X4),
+                        lhsT_scale=xs[:, rows],
+                        rhs=sq[:, cols].bitcast(FP8X4),
+                        rhs_scale=ss[:, cols],
+                        start=(h == 0),
+                        stop=(h == H - 1),
+                    )
+            t = work.tile([P, 2, QW], F32, name=f"b{name}", tag="ob", bufs=8)
+            if engine == "s":
+                nc.scalar.activation(out=t[:], in_=b[:], func=COPY, scale=1.0 / 32.0)
+            else:
+                nc.vector.tensor_scalar(out=t[:], in0=b[:], scalar1=1.0 / 32.0, scalar2=None, op0=MULT)
+            emptied(name)
+            rows = out[QW * rp : QW * (rp + 1), cols]
+            nc.sync.dma_start(out=rows.rearrange("(i p) n -> p i n", p=P), in_=t[:])
+
+        def finish(c, r, engine="s", width=WIDE):
+            b = bank(f"o{width}{c}{r}", [P, width], F32)
             cols = slice(width * c, width * (c + 1))
             rows = slice(P * r, P * (r + 1))
             for h in range(H):
@@ -281,6 +330,7 @@ def tile_focalmodulationqueryweightgrad_w4_kernel(
                 nc.scalar.activation(out=t[:], in_=b[:], func=COPY, scale=1.0 / 32.0)
             else:
                 nc.vector.tensor_scalar(out=t[:], in0=b[:], scalar1=1.0 / 32.0, scalar2=None, op0=MULT)
+            emptied(f"o{width}{c}{r}")
             nc.sync.dma_start(out=out[rows, cols], in_=t[:])
 
         constants()
@@ -304,7 +354,8 @@ def tile_focalmodulationqueryweightgrad_w4_kernel(
         load_zg(5)
         load_x(1)
         load_zg(6)
-        load_zg(7)
+        for a in range(A):
+            load_zg(7, a=a)
         make_table(0)
 
         def m_two(k, q, slots=range(2)):
@@ -349,7 +400,7 @@ def tile_focalmodulationqueryweightgrad_w4_kernel(
         quantise_cg(2)
         times(0, 3)
         turn_take(3, "s", "v")
-        weave_x(0, 2, "s")
+        weave_x(0, 2, "s", False)
         ahead(1, [("h", 0), ("h", 1), ("p", 0), ("p", 1)])
         quantise_cg(3)
         quantise_t("x", 0, 1)
@@ -357,72 +408,83 @@ def tile_focalmodulationqueryweightgrad_w4_kernel(
         turn_take(4)
         m_two(1, 0, (1,))
         p_two(1, 0, (1,))
+        for q in (2, 3):
+            product("h", 1, q)
         turn_take(5)
         quantise_cg(4)
         quantise_t("x", 0, 2)
-        m_two(1, 2)
+        bias(1, 2)
+        bias(1, 3)
         for q in (2, 3):
             product("p", 1, q)
+        ahead(2, [("h", 0), ("h", 1), ("p", 0)])
         times(1, 2)
-        ahead(2, [("h", 0), ("h", 1)])
+        ahead(2, [("p", 1)])
+        times(1, 3)
+        ahead(2, [("h", 2)])
         quantise_cg(5)
         quantise_t("x", 0, 3)
         widen(1, 0, "s")
-        weave_x(1, 0, "g")
         turn_take(6)
-        times(1, 3)
+        weave_s(0, 0, "v")
+        weave_s(0, 1, "v", True)
+        quantise_t("s", 0, 0)
+        quantise_t("s", 0, 1)
+        weave_x(1, 0, "g")
         m_two(2, 0, (1,))
-        p_two(2, 0)
-        weave_s(0, 0)
+        p_two(2, 0, (1,))
+        product("h", 2, 2, (1,))
         turn_take(7)
         quantise_cg(6)
-        m_two(2, 2)
-        widen(1, 1, "s")
+        quantise_cg(7, 0, 1)
+        product("h", 2, 3)
+        bias(2, 2)
         for q in (2, 3):
             product("p", 2, q)
-        times(2, 2)
-        ahead(3, [("h", 0), ("h", 1), ("p", 0)])
-        quantise_cg(7)
-        quantise_t("s", 0, 0)
+        bias(2, 3)
+        ahead(3, [("h", 0), ("h", 1), ("p", 0), ("p", 1)])
+        quantise_cg(7, 1, 1)
         quantise_t("x", 1, 0)
         weave_x(1, 1, "g")
-        times(2, 3)
-        weave_s(0, 1)
-        weave_x(1, 2, "s")
-        weave_x(1, 3, "s")
-        weave_s(0, 2)
-        weave_s(0, 3)
+        times(2, 2)
+        widen(1, 1, "s")
+        weave_x(1, 2, "s", False)
+        weave_x(1, 3, "s", False)
         m_two(3, 0, (1,))
-        product("p", 3, 0, (1,))
-        product("p", 3, 1)
+        for q in range(2):
+            product("p", 3, q, (1,))
+        for q in (2, 3):
+            product("h", 3, q)
         times(3, 0)
+        product("p", 3, 2)
         times(3, 1)
-        product("h", 3, 2)
-        product("h", 3, 3)
+        product("p", 3, 3)
         weave_s(1, 0, "v")
         weave_s(1, 1, "v")
-        quantise_t("s", 0, 1)
         quantise_t("s", 1, 0)
+        finish_quarter(0, 0, "s")
         quantise_t("s", 1, 1)
+        finish_quarter(1, 0, "s")
         quantise_t("x", 1, 1)
-        product("p", 3, 2)
-        product("p", 3, 3)
-        bias(3, 2)
-        bias(3, 3)
-        finish(0, 0)
         quantise_t("x", 1, 2)
-        times(3, 2)
-        times(3, 3)
+        finish(0, 2)
+        finish(0, 3)
+        bias(3, 2)
+        times(2, 3)
         quantise_t("x", 1, 3)
-        for r in range(1, 6):
+        times(3, 2)
+        weave_s(0, 2, "v")
+        bias(3, 3)
+        for r in range(4, 8):
             finish(0, r)
         weave_s(1, 2, "v")
-        weave_s(1, 3, "v")
         quantise_t("s", 0, 2)
-        quantise_t("s", 0, 3)
         quantise_t("s", 1, 2)
+        times(3, 3)
+        weave_s(0, 3, "v")
+        weave_s(1, 3, "v")
+        quantise_t("s", 0, 3)
         quantise_t("s", 1, 3)
-        finish(0, 6, tag="mp")
-        finish(0, 7, tag="mp")
-        for r in range(8):
-            finish(1, r, "v" if r % 2 == 0 else "s", tag="mp")
+        for q in (2, 3):
+            for rp in range(4):
+                finish_quarter(q, rp, "v" if q == 3 and rp % 2 == 0 else "s")

@@ -42,10 +42,11 @@ def tile_focalmodulationqueryweightgrad_w4_kernel(
         psum = ctx.enter_context(tc.psum_pool(name="psum", bufs=1))
         ctx.enter_context(tc.manual_schedule())
 
-        raw_gates = keep.tile([P, H, 48], BF16, name="raw_gates")
+        raw_gates = keep.tile([P, H * U * J, L], BF16, name="raw_gates")
         bh_row = keep.tile([P, D], BF16, name="bh_row")
         w_sc = {key: keep.tile([P, A, D], U8, name=f"w_sc{key}", align_bytes=64) for key in "hp"}
-        ident = keep.tile([P, P], BF16, name="ident")
+        padded = keep.tile([P, P + L + 1], BF16, name="padded")
+        ident = padded[:, 0:P]
         ones = keep.tile([P, P], BF16, name="ones")
         block = keep.tile([P, NT], F32, name="block")
         table = keep.tile([P, H * U * J + 1, NT], BF16, name="table")
@@ -70,30 +71,40 @@ def tile_focalmodulationqueryweightgrad_w4_kernel(
             nc.vector.memset(ones[:], 1.0)
             for key in "hp":
                 nc.vector.memset(w_sc[key][:].rearrange("p s n -> p (s n)").bitcast(I32), 0)
-            make_identity(nc, ident[:])
+            nc.gpsimd.memset(padded[:, P:], 0.0)
+            make_identity(nc, ident)
             nc.vector.tensor_reduce(
-                out=block[:], in_=ident[:].rearrange("p (n l) -> p n l", l=L + 1), axis=mybir.AxisListType.X, op=ADD
+                out=block[:], in_=ident.rearrange("p (n l) -> p n l", l=L + 1), axis=mybir.AxisListType.X, op=ADD
             )
             nc.vector.tensor_copy(out=table[:, H * U * J, :], in_=ident[:, L : P : L + 1])
 
         def load_gates():
-            rows = gates.rearrange("(h n r) l -> n h (r l)", h=H, r=U * J)
-            for l in range(L):
-                nc.sync.dma_start(out=raw_gates[l : P : L + 1, :, 0:46], in_=rows[:, :, l : l + 46])
+            nc.sync.dma_start(
+                out=raw_gates[L : P : L + 1, :, :].rearrange("n (h r) l -> n h (r l)", h=H),
+                in_=gates.rearrange("(h n r) l -> n h (r l)", h=H, r=U * J),
+            )
 
         def load_bias():
             nc.sync.dma_start(out=bh_row[0:1, :], in_=bh.rearrange("(o n) -> o n", o=1))
 
         def load_xs():
-            nc.sync.dma_start(out=xs_sb[:], in_=x_scale.rearrange("(h m j) o -> m h (j o)", h=H, j=J))
+            nc.gpsimd.dma_start(out=xs_sb[:], in_=x_scale.rearrange("(h m j) o -> m h (j o)", h=H, j=J))
 
-        def make_table(h):
-            nc.vector.tensor_tensor(
-                out=table[:, U * J * h : U * J * (h + 1), :],
-                in0=block[:].unsqueeze(1).to_broadcast([P, U * J, NT]),
-                in1=raw_gates[:, h, 0:46:L].unsqueeze(2).to_broadcast([P, U * J, NT]),
-                op=MULT,
-            )
+        def make_tables():
+            b = bank("gates", [P, H * U * J], F32)
+            for l in range(L):
+                nc.tensor.matmul(
+                    b[:], lhsT=padded[:, L - l : P + L - l], rhs=raw_gates[:, :, l], start=(l == 0), stop=(l == L - 1)
+                )
+            for h in range(H):
+                rows = slice(U * J * h, U * J * (h + 1))
+                nc.vector.tensor_tensor(
+                    out=table[:, rows, :],
+                    in0=b[:, rows].unsqueeze(2).to_broadcast([P, U * J, NT]),
+                    in1=block[:].unsqueeze(1).to_broadcast([P, U * J, NT]),
+                    op=MULT,
+                )
+            emptied("gates")
 
         def copy(engine, dst, src):
             if engine == "s":
@@ -119,7 +130,7 @@ def tile_focalmodulationqueryweightgrad_w4_kernel(
             h, j = divmod(t, J)
             first, width = (0, D) if a is None else (WIDE * a, WIDE)
             if (t, first) not in zg:
-                tile = keep.tile([P, U, width], BF16, name=f"zg{t}_{first}", align_bytes=64)
+                tile = work.tile([P, U, width], BF16, name=f"zg{t}_{first}", tag="big", bufs=8, align_bytes=64)
                 for k in range(0, width, WIDE):
                     zg[t, first + k] = (tile, k)
             for l in levels:
@@ -199,46 +210,58 @@ def tile_focalmodulationqueryweightgrad_w4_kernel(
         paired = {}
         woven = {}
 
-        def product(key, k, q, slots=range(2)):
-            if (key, k, q) not in mp:
-                mp[key, k, q] = bank(f"{key}{k}{q}", [P, 2, QW], F32)
-            for i in slots:
-                codes, scales = cg[2 * k + i]
-                for a in range(A):
-                    first = P * (2 * a + w_in[key][2])
-                    cols = slice(first, first + P)
-                    nc.tensor.matmul_mx(
-                        mp[key, k, q][:, i, :],
-                        lhsT=codes[:, cols].bitcast(FP8X4),
-                        lhsT_scale=scales[:, cols],
-                        rhs=w_sb[key][:, a, 2 * QW * q : 2 * QW * (q + 1)].bitcast(FP4X4),
-                        rhs_scale=w_sc[key][:, a, QW * q : QW * (q + 1)],
-                        start=(a == 0),
-                        stop=(a == A - 1),
-                    )
+        def passes(dst, key, t, first, width):
+            codes, scales = cg[t]
+            for a in range(A):
+                col = P * (2 * a + w_in[key][2])
+                nc.tensor.matmul_mx(
+                    dst,
+                    lhsT=codes[:, col : col + P].bitcast(FP8X4),
+                    lhsT_scale=scales[:, col : col + P],
+                    rhs=w_sb[key][:, a, 2 * first : 2 * (first + width)].bitcast(FP4X4),
+                    rhs_scale=w_sc[key][:, a, first : first + width],
+                    start=(a == 0),
+                    stop=(a == A - 1),
+                )
 
-        def bias(k, q):
-            t = work.tile([P, QW, 2], F32, name=f"mb{k}{q}", tag="mb", bufs=4)
-            nc.vector.tensor_tensor(
-                out=t[:],
-                in0=mp["h", k, q][:].rearrange("p i n -> p n i"),
-                in1=bh_bc[:, QW * q : QW * (q + 1)].unsqueeze(2).to_broadcast([P, QW, 2]),
-                op=ADD,
-            )
-            mb[k, q] = t
-            emptied(f"h{k}{q}")
+        def product_m(t, halves=range(2)):
+            for c in halves:
+                mp["m", t, c] = bank(f"m{t}{c}", [P, WIDE], F32)
+                passes(mp["m", t, c][:], "h", t, WIDE * c, WIDE)
 
-        def times(k, q):
+        def product_p(t, qs=range(NQ)):
+            k, i = divmod(t, 2)
+            for q in qs:
+                if ("p", k, q) not in mp:
+                    mp["p", k, q] = bank(f"p{k}{q}", [P, 2, QW], F32)
+                passes(mp["p", k, q][:, i, :], "p", t, QW * q, QW)
+
+        def bias(t, halves=range(2)):
+            k, i = divmod(t, 2)
+            for c in halves:
+                if i == 0:
+                    mb[k, c] = work.tile([P, 2, WIDE], F32, name=f"mb{k}{c}", tag="mb", bufs=4)
+                nc.vector.tensor_tensor(
+                    out=mb[k, c][:, i, :], in0=mp["m", t, c][:], in1=bh_bc[:, WIDE * c : WIDE * (c + 1)], op=ADD
+                )
+                emptied(f"m{t}{c}")
+
+        def times(k, qs=range(NQ)):
             h, r = divmod(k, 2)
-            if (h, q) not in paired:
-                paired[h, q] = keep.tile([P, 2, QW, 2], BF16, name=f"sp{h}{q}", align_bytes=64)
-            nc.vector.tensor_tensor(
-                out=paired[h, q][:, r, :, :], in0=mp["p", k, q][:].rearrange("p i n -> p n i"), in1=mb[k, q][:], op=MULT
-            )
-            emptied(f"p{k}{q}")
+            for q in qs:
+                if r == 0:
+                    paired[h, q] = keep.tile([P, 2, QW, 2], BF16, name=f"sp{h}{q}", align_bytes=64)
+                c, e = divmod(q, 2)
+                nc.vector.tensor_tensor(
+                    out=paired[h, q][:, r, :, :],
+                    in0=mp["p", k, q][:].rearrange("p i n -> p n i"),
+                    in1=mb[k, c][:, :, QW * e : QW * (e + 1)].rearrange("p i n -> p n i"),
+                    op=MULT,
+                )
+                emptied(f"p{k}{q}")
 
-        def weave_s(h, q, engine="s", chained=False):
-            tag, bufs = ("gw", 1) if chained else ("sw", 6)
+        def weave_s(h, q, engine="s", chain=None):
+            tag, bufs = (chain, 1) if chain else ("sw", 5)
             t = work.tile([P, QW, J], BF16, name=f"s{h}_{q}", tag=tag, bufs=bufs, align_bytes=64)
             word = U32 if engine == "s" else I32
             words = paired[h, q][:].rearrange("p r n i -> p r (n i)").bitcast(word)
@@ -260,9 +283,9 @@ def tile_focalmodulationqueryweightgrad_w4_kernel(
                 else:
                     nc.vector.tensor_scalar(out=dst, in0=src, scalar1=scale, scalar2=None, op0=MULT)
 
-        def weave_x(h, q, engine, chained=True):
+        def weave_x(h, q, engine, chain=None):
             src = x_slots[h, q // 2][:, :, QW * (q % 2) : QW * (q % 2 + 1)]
-            tag, bufs = ("gw", 1) if chained else ("xw", 3)
+            tag, bufs = (chain, 1) if chain else ("xw", 4)
             t = work.tile([P, QW, J], BF16, name=f"x{h}_{q}", tag=tag, bufs=bufs, align_bytes=64)
             if engine == "g":
                 copy(engine, t[:], src.rearrange("p j n -> p n j"))
@@ -282,12 +305,15 @@ def tile_focalmodulationqueryweightgrad_w4_kernel(
             cols = slice(QW * q, QW * (q + 1))
             quantise(cq[:, cols], cs[:, cols], woven[key, h, q][:].rearrange("p n t -> p (n t)"))
 
-        def finish_quarter(q, rp, engine):
-            name = f"oq{q}{rp}"
-            b = bank(name, [P, 2, QW], F32)
-            cols = slice(QW * q, QW * (q + 1))
-            for i in range(2):
-                rows = slice(QW * rp + P * i, QW * rp + P * (i + 1))
+        staged = {}
+
+        def finish(first, width, r, engine, g0, group):
+            count = WIDE // width
+            name = f"o{first}_{r}"
+            b = bank(name, [P, count, width], F32)
+            cols = slice(first, first + width)
+            for i in range(count):
+                rows = slice(P * (count * r + i), P * (count * r + i + 1))
                 for h in range(H):
                     xq, xs = codes_t["x", h]
                     sq, ss = codes_t["s", h]
@@ -300,191 +326,168 @@ def tile_focalmodulationqueryweightgrad_w4_kernel(
                         start=(h == 0),
                         stop=(h == H - 1),
                     )
-            t = work.tile([P, 2, QW], F32, name=f"b{name}", tag="ob", bufs=8)
+            i = r - g0
+            if i == 0:
+                staged[first, g0] = work.tile([P, group * count, width], F32, name=f"ob{first}_{g0}", tag="big", bufs=8, align_bytes=64)
+            t = staged[first, g0]
+            dst = t[:, count * i : count * (i + 1), :]
             if engine == "s":
-                nc.scalar.activation(out=t[:], in_=b[:], func=COPY, scale=1.0 / 32.0)
+                nc.scalar.activation(out=dst, in_=b[:], func=COPY, scale=1.0 / 32.0)
             else:
-                nc.vector.tensor_scalar(out=t[:], in0=b[:], scalar1=1.0 / 32.0, scalar2=None, op0=MULT)
+                nc.vector.tensor_scalar(out=dst, in0=b[:], scalar1=1.0 / 32.0, scalar2=None, op0=MULT)
             emptied(name)
-            rows = out[QW * rp : QW * (rp + 1), cols]
-            nc.sync.dma_start(out=rows.rearrange("(i p) n -> p i n", p=P), in_=t[:])
-
-        def finish(c, r, engine="s", width=WIDE):
-            b = bank(f"o{width}{c}{r}", [P, width], F32)
-            cols = slice(width * c, width * (c + 1))
-            rows = slice(P * r, P * (r + 1))
-            for h in range(H):
-                xq, xs = codes_t["x", h]
-                sq, ss = codes_t["s", h]
-                nc.tensor.matmul_mx(
-                    b[:],
-                    lhsT=xq[:, rows].bitcast(FP8X4),
-                    lhsT_scale=xs[:, rows],
-                    rhs=sq[:, cols].bitcast(FP8X4),
-                    rhs_scale=ss[:, cols],
-                    start=(h == 0),
-                    stop=(h == H - 1),
-                )
-            t = work.tile([P, width], F32, name=f"ob{width}{c}{r}", tag="ob", bufs=8)
-            if engine == "s":
-                nc.scalar.activation(out=t[:], in_=b[:], func=COPY, scale=1.0 / 32.0)
-            else:
-                nc.vector.tensor_scalar(out=t[:], in0=b[:], scalar1=1.0 / 32.0, scalar2=None, op0=MULT)
-            emptied(f"o{width}{c}{r}")
-            nc.sync.dma_start(out=out[rows, cols], in_=t[:])
+            if i == group - 1:
+                rows = out[P * count * g0 : P * count * (g0 + group), cols]
+                nc.sync.dma_start(out=rows.rearrange("(i p) n -> p i n", p=P), in_=t[:])
 
         constants()
+        load_gates()
         load_zg(0, (0, 1))
         load_bias()
-        load_gates()
         load_zg(0, (2, 3))
-        load_zg(1, (0, 1))
-        load_w_scales("h", nc.sync, (0, 1, 2))
-        load_zg(1, (2, 3))
-        load_w("h")
-        load_w_scales("h", nc.sync, (3,))
+        load_w_scales("p", nc.gpsimd)
         load_xs()
-        load_x(0)
-        load_zg(2)
-        load_w_scales("p", nc.sync, (0, 1))
+        load_zg(1, (0, 1))
+        load_w_scales("h", nc.sync, (0, 1))
+        load_zg(1, (2, 3))
+        load_w_scales("h", nc.sync, (2, 3))
+        load_w("h")
         load_w("p")
-        load_w_scales("p", nc.sync, (2, 3))
-        load_zg(3)
-        load_zg(4)
-        load_zg(5)
+        load_x(0)
+        for t in (2, 3, 4):
+            load_zg(t)
         load_x(1)
-        load_zg(6)
-        for a in range(A):
-            load_zg(7, a=a)
-        make_table(0)
+        for t in (5, 6, 7):
+            load_zg(t)
+        make_tables()
 
-        def m_two(k, q, slots=range(2)):
-            for e in (q, q + 1):
-                product("h", k, e, slots)
-            for e in (q, q + 1):
-                bias(k, e)
+        def turn_both(t):
+            for a in range(A):
+                turn(t, a)
 
-        def p_two(k, q, slots=range(2)):
-            for e in (q, q + 1):
-                product("p", k, e, slots)
-            for e in (q, q + 1):
-                times(k, e)
-
-        def ahead(k, banks):
-            for key, q in banks:
-                product(key, k, q, (0,))
+        def pair_p(k, qs):
+            for q in qs:
+                for i in range(2):
+                    product_p(2 * k + i, (q,))
 
         spread_bias()
         turn_take(0, "s", "v")
         quantise_cg(0)
         turn_take(1, "s", "v")
-        ahead(0, [("h", q) for q in range(NQ)])
+        product_m(0)
+        product_p(0)
         quantise_cg(1)
-        make_table(1)
+        bias(0)
         widen(0, 0, "s")
+        weave_x(0, 0, "g", "ga")
+        weave_x(0, 1, "g", "gb")
         widen(0, 1, "s", (0, 1))
-        m_two(0, 0, (1,))
-        weave_x(0, 0, "v")
-        for q in (2, 3):
-            product("h", 0, q, (1,))
-        bias(0, 2)
-        quantise_t("x", 0, 0)
-        weave_x(0, 1, "g")
-        bias(0, 3)
-        turn_take(2)
-        p_two(0, 0)
+        product_m(1)
+        product_p(1)
+        bias(1)
+        times(0)
+        turn_take(2, "s", "v")
         widen(0, 1, "s", (2, 3))
-        for q in (2, 3):
-            product("p", 0, q)
-        times(0, 2)
         quantise_cg(2)
-        times(0, 3)
-        turn_take(3, "s", "v")
-        weave_x(0, 2, "s", False)
-        ahead(1, [("h", 0), ("h", 1), ("p", 0), ("p", 1)])
-        quantise_cg(3)
         quantise_t("x", 0, 1)
-        weave_x(0, 3, "g")
-        turn_take(4)
-        m_two(1, 0, (1,))
-        p_two(1, 0, (1,))
-        for q in (2, 3):
-            product("h", 1, q)
-        turn_take(5)
-        quantise_cg(4)
+        quantise_t("x", 0, 0)
+        weave_x(0, 2, "g", "ga")
+        turn_both(3)
+        product_m(2)
+        product_p(2, (0, 1))
+        take(3, 0, "s")
+        bias(2, (0,))
+        take(3, 1, "s")
+        bias(2, (1,))
+        turn_both(4)
+        quantise_cg(3)
         quantise_t("x", 0, 2)
-        bias(1, 2)
-        bias(1, 3)
-        for q in (2, 3):
-            product("p", 1, q)
-        ahead(2, [("h", 0), ("h", 1), ("p", 0)])
-        times(1, 2)
-        ahead(2, [("p", 1)])
-        times(1, 3)
-        ahead(2, [("h", 2)])
-        quantise_cg(5)
+        weave_x(0, 3, "g", "ga")
+        product_m(3)
+        product_p(3, (0, 1))
+        take(4, 0, "s")
+        bias(3, (0,))
+        take(4, 1, "s")
+        bias(3, (1,))
+        widen(1, 0, "s", (0, 1, 2))
+        pair_p(1, (2, 3))
+        times(1, (0, 1))
+        turn_both(5)
+        quantise_cg(4)
         quantise_t("x", 0, 3)
-        widen(1, 0, "s")
-        turn_take(6)
+        times(1, (2,))
+        product_m(4)
+        take(5, 0, "s")
+        times(1, (3,))
+        turn_both(6)
+        bias(4, (0,))
+        take(5, 1, "s")
+        widen(1, 0, "s", (3,))
+        product_p(4, (0, 1))
         weave_s(0, 0, "v")
-        weave_s(0, 1, "v", True)
+        weave_s(0, 1, "v", "ga")
+        quantise_cg(5)
+        take(6, 0, "s")
+        product_m(5, (0,))
+        product_p(5, (0, 1))
         quantise_t("s", 0, 0)
         quantise_t("s", 0, 1)
-        weave_x(1, 0, "g")
-        m_two(2, 0, (1,))
-        p_two(2, 0, (1,))
-        product("h", 2, 2, (1,))
-        turn_take(7)
+        weave_x(1, 0, "g", "ga")
+        bias(4, (1,))
+        take(6, 1, "s")
+        bias(5, (0,))
+        turn_both(7)
+        product_m(5, (1,))
+        times(2, (0,))
         quantise_cg(6)
-        quantise_cg(7, 0, 1)
-        product("h", 2, 3)
-        bias(2, 2)
-        for q in (2, 3):
-            product("p", 2, q)
-        bias(2, 3)
-        ahead(3, [("h", 0), ("h", 1), ("p", 0), ("p", 1)])
-        quantise_cg(7, 1, 1)
-        quantise_t("x", 1, 0)
-        weave_x(1, 1, "g")
-        times(2, 2)
+        times(2, (1,))
+        take(7, 0, "s")
+        product_m(6, (0,))
+        product_p(6, (0, 1))
+        take(7, 1, "s")
+        bias(5, (1,))
+        pair_p(2, (2,))
+        bias(6, (0,))
         widen(1, 1, "s")
-        weave_x(1, 2, "s", False)
-        weave_x(1, 3, "s", False)
-        m_two(3, 0, (1,))
-        for q in range(2):
-            product("p", 3, q, (1,))
-        for q in (2, 3):
-            product("h", 3, q)
-        times(3, 0)
-        product("p", 3, 2)
-        times(3, 1)
-        product("p", 3, 3)
+        pair_p(2, (3,))
+        quantise_cg(7)
+        quantise_t("x", 1, 0)
+        weave_x(1, 1, "g", "ga")
+        product_m(7, (0,))
+        product_p(7, (0, 1))
+        times(2, (2,))
+        bias(7, (0,))
+        weave_s(0, 2, "s")
+        weave_x(1, 2, "s")
+        weave_x(1, 3, "s")
+        product_m(6, (1,))
+        times(2, (3,))
+        product_m(7, (1,))
+        times(3, (0, 1))
+        pair_p(3, (2, 3))
         weave_s(1, 0, "v")
         weave_s(1, 1, "v")
         quantise_t("s", 1, 0)
-        finish_quarter(0, 0, "s")
         quantise_t("s", 1, 1)
-        finish_quarter(1, 0, "s")
+        weave_s(0, 3, "s")
         quantise_t("x", 1, 1)
+        bias(6, (1,))
+        bias(7, (1,))
+        finish(0, WIDE, 0, "s", 0, 1)
         quantise_t("x", 1, 2)
-        finish(0, 2)
-        finish(0, 3)
-        bias(3, 2)
-        times(2, 3)
+        times(3, (2,))
+        finish(0, WIDE, 1, "s", 1, 2)
+        finish(0, WIDE, 2, "s", 1, 2)
         quantise_t("x", 1, 3)
-        times(3, 2)
-        weave_s(0, 2, "v")
-        bias(3, 3)
-        for r in range(4, 8):
-            finish(0, r)
         weave_s(1, 2, "v")
+        times(3, (3,))
         quantise_t("s", 0, 2)
         quantise_t("s", 1, 2)
-        times(3, 3)
-        weave_s(0, 3, "v")
         weave_s(1, 3, "v")
         quantise_t("s", 0, 3)
         quantise_t("s", 1, 3)
-        for q in (2, 3):
-            for rp in range(4):
-                finish_quarter(q, rp, "v" if q == 3 and rp % 2 == 0 else "s")
+        for r in range(3, 7):
+            finish(0, WIDE, r, "s", r - (r + 1) % 2, 2)
+        finish(0, WIDE, 7, "s", 7, 1)
+        for r in range(8):
+            finish(WIDE, WIDE, r, "v" if r % 2 else "s", r - r % 2 if r < 6 else r, 2 if r < 6 else 1)

@@ -149,10 +149,12 @@ def tile_focalmodulationqueryweightgrad_w4_kernel(
         w_sb = {}
         w_in = {"h": (wh_words, wh_scales, 0), "p": (wp_words, wp_scales, 1)}
 
-        def load_w(key):
-            t = keep.tile([P, A, 2 * D], U8, name=f"w_{key}", align_bytes=64)
-            nc.sync.dma_start(out=t[:].bitcast(I32), in_=w_in[key][0].bitcast(I32).rearrange("a p n -> p a n"))
-            w_sb[key] = t
+        def load_w(key, first=0, width=D):
+            t = keep.tile([P, A, 2 * width], U8, name=f"w_{key}{first}", align_bytes=64)
+            words = w_in[key][0].bitcast(I32).rearrange("a p n -> p a n")
+            nc.sync.dma_start(out=t[:].bitcast(I32), in_=words[:, :, first // 2 : (first + width) // 2])
+            for col in range(0, width, QW):
+                w_sb[key, first + col] = (t, col)
 
         def load_w_scales(key, queue, rows=range(4)):
             sv = w_in[key][1].bitcast(I32).rearrange("a (q r) n -> r q a n", r=4)
@@ -163,28 +165,29 @@ def tile_focalmodulationqueryweightgrad_w4_kernel(
         kin = {}
         cg = {}
 
-        def turn(t, a):
+        def turn(t, a, first_u=0, count=U):
             h, j = divmod(t, J)
             tile, first = zg[t, WIDE * a]
-            b = bank(f"gt{t}{a}", [P, U * 4, 2, NT], BF16)
+            b = bank(f"gt{t}{a}{first_u}", [P, count * 4, 2, NT], BF16)
             last = H * U * J
-            for u in range(U):
-                i = U * J * h + J * u + j
+            for u in range(count):
+                i = U * J * h + J * (first_u + u) + j
                 for k in range(4):
                     nc.tensor.matmul(
                         b[:, 4 * u + k, :, :],
-                        lhsT=tile[:, u, first + k : first + WIDE : 4],
+                        lhsT=tile[:, first_u + u, first + k : first + WIDE : 4],
                         rhs=table[:, i : last + 1 : last - i, :],
                         start=True,
                         stop=True,
                     )
-            turned[t, a] = b
+            turned[t, a, first_u] = (b, count)
 
-        def take(t, a, engine):
+        def take(t, a, engine, first_u=0):
             if t not in kin:
                 kin[t] = work.tile([P, A, 2 * NT, U * 4], BF16, name=f"kin{t}", tag="kin", bufs=3, align_bytes=64)
-            copy(engine, kin[t][:, a, :, :], turned[t, a][:].rearrange("p s c n -> p (c n) s"))
-            emptied(f"gt{t}{a}")
+            b, count = turned[t, a, first_u]
+            copy(engine, kin[t][:, a, :, 4 * first_u : 4 * (first_u + count)], b[:].rearrange("p s c n -> p (c n) s"))
+            emptied(f"gt{t}{a}{first_u}")
 
         def turn_take(t, e0="s", e1="s"):
             turn(t, 0)
@@ -212,22 +215,22 @@ def tile_focalmodulationqueryweightgrad_w4_kernel(
 
         def passes(dst, key, t, first, width):
             codes, scales = cg[t]
+            words, at = w_sb[key, first]
             for a in range(A):
                 col = P * (2 * a + w_in[key][2])
                 nc.tensor.matmul_mx(
                     dst,
                     lhsT=codes[:, col : col + P].bitcast(FP8X4),
                     lhsT_scale=scales[:, col : col + P],
-                    rhs=w_sb[key][:, a, 2 * first : 2 * (first + width)].bitcast(FP4X4),
+                    rhs=words[:, a, 2 * at : 2 * (at + width)].bitcast(FP4X4),
                     rhs_scale=w_sc[key][:, a, first : first + width],
                     start=(a == 0),
                     stop=(a == A - 1),
                 )
 
-        def product_m(t, halves=range(2)):
-            for c in halves:
-                mp["m", t, c] = bank(f"m{t}{c}", [P, WIDE], F32)
-                passes(mp["m", t, c][:], "h", t, WIDE * c, WIDE)
+        def product_m(t, first, width=WIDE):
+            mp["m", t, first] = bank(f"m{t}_{first}", [P, width], F32)
+            passes(mp["m", t, first][:], "h", t, first, width)
 
         def product_p(t, qs=range(NQ)):
             k, i = divmod(t, 2)
@@ -236,15 +239,18 @@ def tile_focalmodulationqueryweightgrad_w4_kernel(
                     mp["p", k, q] = bank(f"p{k}{q}", [P, 2, QW], F32)
                 passes(mp["p", k, q][:, i, :], "p", t, QW * q, QW)
 
-        def bias(t, halves=range(2)):
+        def bias(t, first, width=WIDE):
             k, i = divmod(t, 2)
-            for c in halves:
-                if i == 0:
-                    mb[k, c] = work.tile([P, 2, WIDE], F32, name=f"mb{k}{c}", tag="mb", bufs=4)
-                nc.vector.tensor_tensor(
-                    out=mb[k, c][:, i, :], in0=mp["m", t, c][:], in1=bh_bc[:, WIDE * c : WIDE * (c + 1)], op=ADD
-                )
-                emptied(f"m{t}{c}")
+            c, at = divmod(first, WIDE)
+            if (k, c) not in mb:
+                mb[k, c] = work.tile([P, 2, WIDE], F32, name=f"mb{k}{c}", tag="mb", bufs=5)
+            nc.vector.tensor_tensor(
+                out=mb[k, c][:, i, at : at + width],
+                in0=mp["m", t, first][:],
+                in1=bh_bc[:, first : first + width],
+                op=ADD,
+            )
+            emptied(f"m{t}_{first}")
 
         def times(k, qs=range(NQ)):
             h, r = divmod(k, 2)
@@ -270,13 +276,13 @@ def tile_focalmodulationqueryweightgrad_w4_kernel(
 
         x_slots = {}
 
-        def widen(h, c, engine, slots=range(J)):
+        def widen(h, c, engine, slots=range(J), at=0, width=WIDE):
             if (h, c) not in x_slots:
                 x_slots[h, c] = keep.tile([P, J, WIDE], BF16, name=f"xw{h}{c}")
             for j in slots:
-                dst = x_slots[h, c][:, j, :]
+                dst = x_slots[h, c][:, j, at : at + width]
                 t, first = x_sb[h, j]
-                src = t[:, first + WIDE * c : first + WIDE * (c + 1)].bitcast(FP8)
+                src = t[:, first + WIDE * c + at : first + WIDE * c + at + width].bitcast(FP8)
                 scale = xs_sb[:, h, j : j + 1]
                 if engine == "s":
                     nc.scalar.activation(out=dst, in_=src, func=COPY, scale=scale)
@@ -352,10 +358,11 @@ def tile_focalmodulationqueryweightgrad_w4_kernel(
         load_zg(1, (2, 3))
         load_w_scales("h", nc.sync, (2, 3))
         load_w("h")
+        load_zg(2)
         load_w("p")
         load_x(0)
-        for t in (2, 3, 4):
-            load_zg(t)
+        load_zg(3)
+        load_zg(4)
         load_x(1)
         for t in (5, 6, 7):
             load_zg(t)
@@ -370,124 +377,153 @@ def tile_focalmodulationqueryweightgrad_w4_kernel(
                 for i in range(2):
                     product_p(2 * k + i, (q,))
 
+        def both_m(t):
+            for first in (0, WIDE):
+                product_m(t, first)
+
+        def both_bias(t):
+            for first in (0, WIDE):
+                bias(t, first)
+
+        def turn_take_halves(t):
+            for a in range(A):
+                for first_u in (0, 2):
+                    turn(t, a, first_u, 2)
+            for a in range(A):
+                take(t, a, "s", 0)
+                take(t, a, "v", 2)
+
+        turn_take_halves(0)
         spread_bias()
-        turn_take(0, "s", "v")
         quantise_cg(0)
-        turn_take(1, "s", "v")
-        product_m(0)
-        product_p(0)
+        turn_take_halves(1)
+        both_m(0)
         quantise_cg(1)
-        bias(0)
+        both_bias(0)
+        both_m(1)
+        both_bias(1)
+        turn_take_halves(2)
+        pair_p(0, range(NQ))
         widen(0, 0, "s")
-        weave_x(0, 0, "g", "ga")
-        weave_x(0, 1, "g", "gb")
-        widen(0, 1, "s", (0, 1))
-        product_m(1)
-        product_p(1)
-        bias(1)
-        times(0)
-        turn_take(2, "s", "v")
-        widen(0, 1, "s", (2, 3))
+        widen(0, 1, "s", (0,))
+        times(0, (0,))
         quantise_cg(2)
-        quantise_t("x", 0, 1)
-        quantise_t("x", 0, 0)
-        weave_x(0, 2, "g", "ga")
-        turn_both(3)
-        product_m(2)
-        product_p(2, (0, 1))
-        take(3, 0, "s")
-        bias(2, (0,))
-        take(3, 1, "s")
-        bias(2, (1,))
-        turn_both(4)
+        times(0, (1, 2, 3))
+        both_m(2)
+        weave_x(0, 0, "v")
+        bias(2, 0)
+        turn_take_halves(3)
+        product_p(2)
+        widen(0, 1, "s", (1, 2, 3))
+        bias(2, WIDE)
         quantise_cg(3)
+        turn_both(4)
+        weave_x(0, 1, "v", "ga")
+        quantise_t("x", 0, 0)
+        quantise_t("x", 0, 1)
+        weave_x(0, 2, "g", "ga")
+        take(4, 0, "s")
+        both_m(3)
+        take(4, 1, "s")
+        product_p(3)
+        both_bias(3)
+        widen(1, 0, "s", (0, 1))
+        times(1, (0,))
+        turn_both(5)
+        times(1, (1,))
+        quantise_cg(4)
         quantise_t("x", 0, 2)
         weave_x(0, 3, "g", "ga")
-        product_m(3)
-        product_p(3, (0, 1))
-        take(4, 0, "s")
-        bias(3, (0,))
-        take(4, 1, "s")
-        bias(3, (1,))
-        widen(1, 0, "s", (0, 1, 2))
-        pair_p(1, (2, 3))
-        times(1, (0, 1))
-        turn_both(5)
-        quantise_cg(4)
-        quantise_t("x", 0, 3)
         times(1, (2,))
-        product_m(4)
+        both_m(4)
         take(5, 0, "s")
         times(1, (3,))
-        turn_both(6)
-        bias(4, (0,))
-        take(5, 1, "s")
-        widen(1, 0, "s", (3,))
         product_p(4, (0, 1))
+        bias(4, 0)
+        take(5, 1, "s")
+        turn_both(6)
+        widen(1, 0, "s", (2, 3))
         weave_s(0, 0, "v")
-        weave_s(0, 1, "v", "ga")
+        weave_s(0, 1, "v")
         quantise_cg(5)
         take(6, 0, "s")
-        product_m(5, (0,))
+        product_m(5, 0)
         product_p(5, (0, 1))
         quantise_t("s", 0, 0)
         quantise_t("s", 0, 1)
+        quantise_t("x", 0, 3)
         weave_x(1, 0, "g", "ga")
-        bias(4, (1,))
         take(6, 1, "s")
-        bias(5, (0,))
-        turn_both(7)
-        product_m(5, (1,))
+        bias(4, WIDE)
+        bias(5, 0)
+        turn(7, 0, 0, 2)
+        turn(7, 0, 2, 2)
         times(2, (0,))
+        turn(7, 1, 0, 2)
+        turn(7, 1, 2, 2)
+        take(7, 0, "s", 0)
         quantise_cg(6)
-        times(2, (1,))
-        take(7, 0, "s")
-        product_m(6, (0,))
+        take(7, 1, "s", 0)
+        take(7, 0, "v", 2)
+        product_m(5, WIDE)
+        take(7, 1, "v", 2)
+        product_m(6, 0)
         product_p(6, (0, 1))
-        take(7, 1, "s")
-        bias(5, (1,))
-        pair_p(2, (2,))
-        bias(6, (0,))
         widen(1, 1, "s")
-        pair_p(2, (3,))
         quantise_cg(7)
         quantise_t("x", 1, 0)
         weave_x(1, 1, "g", "ga")
-        product_m(7, (0,))
-        product_p(7, (0, 1))
-        times(2, (2,))
-        bias(7, (0,))
-        weave_s(0, 2, "s")
         weave_x(1, 2, "s")
         weave_x(1, 3, "s")
-        product_m(6, (1,))
-        times(2, (3,))
-        product_m(7, (1,))
-        times(3, (0, 1))
-        pair_p(3, (2, 3))
+        product_m(7, 0, QW)
+        product_p(7, (0,))
+        bias(6, 0)
+        product_m(7, QW, QW)
+        product_p(7, (1,))
+        bias(7, 0, QW)
+        times(2, (1,))
+        pair_p(2, (2,))
+        times(3, (0,))
+        product_m(6, WIDE)
+        bias(7, QW, QW)
         weave_s(1, 0, "v")
-        weave_s(1, 1, "v")
-        quantise_t("s", 1, 0)
-        quantise_t("s", 1, 1)
-        weave_s(0, 3, "s")
         quantise_t("x", 1, 1)
-        bias(6, (1,))
-        bias(7, (1,))
-        finish(0, WIDE, 0, "s", 0, 1)
+        quantise_t("s", 1, 0)
+        product_m(7, WIDE)
+        times(3, (1,))
+        finish(0, QW, 0, "s", 0, 1)
         quantise_t("x", 1, 2)
-        times(3, (2,))
-        finish(0, WIDE, 1, "s", 1, 2)
-        finish(0, WIDE, 2, "s", 1, 2)
+        weave_s(1, 1, "v")
         quantise_t("x", 1, 3)
-        weave_s(1, 2, "v")
-        times(3, (3,))
+        finish(0, QW, 1, "s", 1, 1)
+        quantise_t("s", 1, 1)
+        weave_s(0, 2, "v")
+        finish(0, QW, 2, "s", 2, 1)
+        bias(5, WIDE)
+        finish(0, QW, 3, "s", 3, 1)
+        weave_s(0, 3, "v")
+        bias(6, WIDE)
+        pair_p(3, (2,))
+        bias(7, WIDE)
+        finish(QW, QW, 0, "s", 0, 1)
+        times(2, (2,))
+        finish(QW, QW, 1, "s", 1, 1)
+        times(3, (2,))
+        finish(QW, QW, 2, "s", 2, 1)
+        pair_p(2, (3,))
         quantise_t("s", 0, 2)
-        quantise_t("s", 1, 2)
-        weave_s(1, 3, "v")
+        weave_s(1, 2, "v")
+        finish(QW, QW, 3, "s", 3, 1)
+        pair_p(3, (3,))
         quantise_t("s", 0, 3)
+        quantise_t("s", 1, 2)
+        times(2, (3,))
+        times(3, (3,))
+        finish(2 * QW, QW, 0, "s", 0, 1)
+        weave_s(1, 3, "v")
+        finish(2 * QW, QW, 1, "s", 1, 1)
         quantise_t("s", 1, 3)
-        for r in range(3, 7):
-            finish(0, WIDE, r, "s", r - (r + 1) % 2, 2)
-        finish(0, WIDE, 7, "s", 7, 1)
-        for r in range(8):
-            finish(WIDE, WIDE, r, "v" if r % 2 else "s", r - r % 2 if r < 6 else r, 2 if r < 6 else 1)
+        for rp in range(2, 4):
+            finish(2 * QW, QW, rp, "s", rp, 1)
+        for rp in range(4):
+            finish(3 * QW, QW, rp, "s" if rp % 2 else "v", rp, 1)

@@ -436,6 +436,7 @@ def tile_focalmodulationqueryweightgrad_w4_kernel(
         weave_x(0, 3, "g", "ga")
         times(1, (2,))
         both_m(4)
+        weave_s(0, 0, "s")
         take(5, 0, "s")
         times(1, (3,))
         product_p(4, (0, 1))
@@ -443,7 +444,6 @@ def tile_focalmodulationqueryweightgrad_w4_kernel(
         take(5, 1, "s")
         turn_both(6)
         widen(1, 0, "s", (2, 3))
-        weave_s(0, 0, "v")
         weave_s(0, 1, "v")
         quantise_cg(5)
         take(6, 0, "s")
@@ -470,11 +470,13 @@ def tile_focalmodulationqueryweightgrad_w4_kernel(
         product_m(6, 0)
         product_p(6, (0, 1))
         widen(1, 1, "s")
+        pair_p(2, (2,))
         quantise_cg(7)
         quantise_t("x", 1, 0)
         weave_x(1, 1, "g", "ga")
         weave_x(1, 2, "s")
         weave_x(1, 3, "s")
+        weave_s(0, 2, "s")
         product_m(7, 0, QW)
         product_p(7, (0,))
         bias(6, 0)
@@ -482,14 +484,14 @@ def tile_focalmodulationqueryweightgrad_w4_kernel(
         product_p(7, (1,))
         bias(7, 0, QW)
         times(2, (1,))
-        pair_p(2, (2,))
         times(3, (0,))
         product_m(6, WIDE)
         bias(7, QW, QW)
         weave_s(1, 0, "v")
+        product_m(7, WIDE)
         quantise_t("x", 1, 1)
         quantise_t("s", 1, 0)
-        product_m(7, WIDE)
+        pair_p(3, (2,))
         times(3, (1,))
         finish(0, QW, 0, "s", 0, 1)
         quantise_t("x", 1, 2)
@@ -497,33 +499,30 @@ def tile_focalmodulationqueryweightgrad_w4_kernel(
         quantise_t("x", 1, 3)
         finish(0, QW, 1, "s", 1, 1)
         quantise_t("s", 1, 1)
-        weave_s(0, 2, "v")
-        finish(0, QW, 2, "s", 2, 1)
         bias(5, WIDE)
-        finish(0, QW, 3, "s", 3, 1)
-        weave_s(0, 3, "v")
+        finish(0, QW, 2, "s", 2, 1)
         bias(6, WIDE)
-        pair_p(3, (2,))
-        bias(7, WIDE)
-        finish(QW, QW, 0, "s", 0, 1)
-        times(2, (2,))
-        finish(QW, QW, 1, "s", 1, 1)
-        times(3, (2,))
-        finish(QW, QW, 2, "s", 2, 1)
+        finish(0, QW, 3, "s", 3, 1)
         pair_p(2, (3,))
+        bias(7, WIDE)
+        weave_s(0, 3, "s")
+        times(2, (2,))
+        finish(QW, QW, 0, "s", 0, 1)
+        times(3, (2,))
+        finish(QW, QW, 1, "s", 1, 1)
+        pair_p(3, (3,))
         quantise_t("s", 0, 2)
         weave_s(1, 2, "v")
-        finish(QW, QW, 3, "s", 3, 1)
-        pair_p(3, (3,))
-        quantise_t("s", 0, 3)
-        quantise_t("s", 1, 2)
         times(2, (3,))
+        finish(QW, QW, 2, "s", 2, 1)
+        quantise_t("s", 1, 2)
         times(3, (3,))
-        finish(2 * QW, QW, 0, "s", 0, 1)
+        finish(QW, QW, 3, "s", 3, 1)
+        quantise_t("s", 0, 3)
         weave_s(1, 3, "v")
-        finish(2 * QW, QW, 1, "s", 1, 1)
+        finish(2 * QW, QW, 0, "s", 0, 1)
         quantise_t("s", 1, 3)
-        for rp in range(2, 4):
-            finish(2 * QW, QW, rp, "s", rp, 1)
+        for rp in range(1, 4):
+            finish(2 * QW, QW, rp, "s" if rp % 2 else "v", rp, 1)
         for rp in range(4):
             finish(3 * QW, QW, rp, "s" if rp % 2 else "v", rp, 1)

@@ -351,11 +351,10 @@ def tile_focalmodulationqueryweightgrad_w4_kernel(
         load_zg(0, (0, 1))
         load_bias()
         load_zg(0, (2, 3))
+        load_w_scales("h", nc.gpsimd, (0, 1))
         load_w_scales("p", nc.gpsimd)
         load_xs()
-        load_zg(1, (0, 1))
-        load_w_scales("h", nc.sync, (0, 1))
-        load_zg(1, (2, 3))
+        load_zg(1)
         load_w_scales("h", nc.sync, (2, 3))
         load_w("h")
         load_zg(2)
@@ -464,8 +463,9 @@ def tile_focalmodulationqueryweightgrad_w4_kernel(
         take(7, 0, "s", 0)
         quantise_cg(6)
         take(7, 1, "s", 0)
-        take(7, 0, "v", 2)
+        take(7, 0, "s", 2)
         product_m(5, WIDE)
+        times(2, (1,))
         take(7, 1, "v", 2)
         product_m(6, 0)
         product_p(6, (0, 1))
@@ -483,7 +483,6 @@ def tile_focalmodulationqueryweightgrad_w4_kernel(
         product_m(7, QW, QW)
         product_p(7, (1,))
         bias(7, 0, QW)
-        times(2, (1,))
         times(3, (0,))
         product_m(6, WIDE)
         bias(7, QW, QW)

@@ -27,7 +27,16 @@ NT = 32
 QW = 256
 NQ = D // QW
 WIDE = 512
+LEFT, RIGHT = 0, WIDE
 BANKS = 8
+GATE_ROWS = H * U * J
+OUT_SCALE = 1.0 / 32.0
+CHAIN = "chain"
+BIG_BUFS = H * J
+TAKE_BUFS = 3
+M_BUFS = 5
+S_BUFS = 5
+X_BUFS = 4
 
 FLOPS = 3 * 2 * T * D * D + 2 * L * T * D + 2 * T * D
 
@@ -42,14 +51,14 @@ def tile_focalmodulationqueryweightgrad_w4_kernel(
         psum = ctx.enter_context(tc.psum_pool(name="psum", bufs=1))
         ctx.enter_context(tc.manual_schedule())
 
-        raw_gates = keep.tile([P, H * U * J, L], BF16, name="raw_gates")
+        raw_gates = keep.tile([P, GATE_ROWS, L], BF16, name="raw_gates")
         bh_row = keep.tile([P, D], BF16, name="bh_row")
-        w_sc = {key: keep.tile([P, A, D], U8, name=f"w_sc{key}", align_bytes=64) for key in "hp"}
+        w_sc = {key: keep.tile([P, A, D], U8, name=f"scales_{key}", align_bytes=64) for key in ("wh", "wp")}
         padded = keep.tile([P, P + L + 1], BF16, name="padded")
         ident = padded[:, 0:P]
         ones = keep.tile([P, P], BF16, name="ones")
         block = keep.tile([P, NT], F32, name="block")
-        table = keep.tile([P, H * U * J + 1, NT], BF16, name="table")
+        table = keep.tile([P, GATE_ROWS + 1, NT], BF16, name="table")
         xs_sb = keep.tile([P, H, J], F32, name="xs_sb")
         bh_bc = keep.tile([P, D], BF16, name="bh_bc")
 
@@ -57,8 +66,7 @@ def tile_focalmodulationqueryweightgrad_w4_kernel(
         held = {}
 
         def bank(name, shape, dtype):
-            n = empty[0]
-            empty.remove(n)
+            n = empty.pop(0)
             held[name] = n
             return psum.tile(shape, dtype, name=name, tag=f"bank{n}")
 
@@ -69,14 +77,14 @@ def tile_focalmodulationqueryweightgrad_w4_kernel(
             nc.gpsimd.memset(raw_gates[:], 0.0)
             nc.vector.memset(bh_row[:], 0.0)
             nc.vector.memset(ones[:], 1.0)
-            for key in "hp":
+            for key in w_sc:
                 nc.vector.memset(w_sc[key][:].rearrange("p s n -> p (s n)").bitcast(I32), 0)
             nc.gpsimd.memset(padded[:, P:], 0.0)
             make_identity(nc, ident)
             nc.vector.tensor_reduce(
                 out=block[:], in_=ident.rearrange("p (n l) -> p n l", l=L + 1), axis=mybir.AxisListType.X, op=ADD
             )
-            nc.vector.tensor_copy(out=table[:, H * U * J, :], in_=ident[:, L : P : L + 1])
+            nc.vector.tensor_copy(out=table[:, GATE_ROWS, :], in_=ident[:, L : P : L + 1])
 
         def load_gates():
             nc.sync.dma_start(
@@ -88,10 +96,10 @@ def tile_focalmodulationqueryweightgrad_w4_kernel(
             nc.sync.dma_start(out=bh_row[0:1, :], in_=bh.rearrange("(o n) -> o n", o=1))
 
         def load_xs():
-            nc.gpsimd.dma_start(out=xs_sb[:], in_=x_scale.rearrange("(h m j) o -> m h (j o)", h=H, j=J))
+            nc.gpsimd.dma_start(out=xs_sb[:], in_=x_scale.rearrange("(h r j) o -> r h (j o)", h=H, j=J))
 
-        def make_tables():
-            b = bank("gates", [P, H * U * J], F32)
+        def make_table():
+            b = bank("gates", [P, GATE_ROWS], F32)
             for l in range(L):
                 nc.tensor.matmul(
                     b[:], lhsT=padded[:, L - l : P + L - l], rhs=raw_gates[:, :, l], start=(l == 0), stop=(l == L - 1)
@@ -116,8 +124,8 @@ def tile_focalmodulationqueryweightgrad_w4_kernel(
 
         def spread_bias():
             b = bank("bias", [P, D], BF16)
-            for e in range(2):
-                cols = slice(WIDE * e, WIDE * (e + 1))
+            for first in (LEFT, RIGHT):
+                cols = slice(first, first + WIDE)
                 nc.tensor.matmul(b[:, cols], lhsT=ones[:], rhs=bh_row[:, cols], start=True, stop=True)
             copy("s", bh_bc[:], b[:])
             emptied("bias")
@@ -126,250 +134,206 @@ def tile_focalmodulationqueryweightgrad_w4_kernel(
         rows_of.append(g.rearrange("(h n u j) d -> h n u (j d)", h=H, u=U, j=J))
         zg = {}
 
-        def load_zg(t, levels=range(L + 1), a=None):
+        def load_zg(t, levels=range(L + 1)):
             h, j = divmod(t, J)
-            first, width = (0, D) if a is None else (WIDE * a, WIDE)
-            if (t, first) not in zg:
-                tile = work.tile([P, U, width], BF16, name=f"zg{t}_{first}", tag="big", bufs=8, align_bytes=64)
-                for k in range(0, width, WIDE):
-                    zg[t, first + k] = (tile, k)
+            if t not in zg:
+                zg[t] = work.tile([P, U, D], BF16, name=f"zg{t}", tag="big", bufs=BIG_BUFS, align_bytes=64)
             for l in levels:
-                src = rows_of[l][h][:, :, D * j + first : D * j + first + width]
-                nc.sync.dma_start(out=zg[t, first][0][l : P : L + 1, :, :], in_=src)
+                nc.sync.dma_start(out=zg[t][l : P : L + 1, :, :], in_=rows_of[l][h][:, :, D * j : D * (j + 1)])
 
-        x_view = x_bytes.rearrange("(h m j) n -> h m (j n)", h=H, j=J)
+        x_view = x_bytes.rearrange("(h r j) n -> h r (j n)", h=H, j=J)
         x_sb = {}
 
-        def load_x(h, first=0, count=J):
-            t = keep.tile([P, count * D], U8, name=f"x_sb{h}{first}", align_bytes=64)
-            nc.sync.dma_start(out=t[:], in_=x_view[h][:, D * first : D * (first + count)])
-            for j in range(count):
-                x_sb[h, first + j] = (t, D * j)
+        def load_x(h):
+            x_sb[h] = keep.tile([P, J * D], U8, name=f"x_sb{h}", align_bytes=64)
+            nc.sync.dma_start(out=x_sb[h][:], in_=x_view[h])
 
+        w_in = {"wh": (wh_words, wh_scales, 0), "wp": (wp_words, wp_scales, 1)}
         w_sb = {}
-        w_in = {"h": (wh_words, wh_scales, 0), "p": (wp_words, wp_scales, 1)}
 
-        def load_w(key, first=0, width=D):
-            t = keep.tile([P, A, 2 * width], U8, name=f"w_{key}{first}", align_bytes=64)
-            words = w_in[key][0].bitcast(I32).rearrange("a p n -> p a n")
-            nc.sync.dma_start(out=t[:].bitcast(I32), in_=words[:, :, first // 2 : (first + width) // 2])
-            for col in range(0, width, QW):
-                w_sb[key, first + col] = (t, col)
+        def load_w(key):
+            w_sb[key] = keep.tile([P, A, 2 * D], U8, name=f"words_{key}", align_bytes=64)
+            nc.sync.dma_start(out=w_sb[key][:].bitcast(I32), in_=w_in[key][0].bitcast(I32).rearrange("a p n -> p a n"))
 
         def load_w_scales(key, queue, rows=range(4)):
-            sv = w_in[key][1].bitcast(I32).rearrange("a (q r) n -> r q a n", r=4)
-            for r in rows:
-                queue.dma_start(out=w_sc[key][r:P:32, :, :].bitcast(I32), in_=sv[r])
+            sv = w_in[key][1].bitcast(I32).rearrange("a (q i) n -> i q a n", i=4)
+            for i in rows:
+                queue.dma_start(out=w_sc[key][i:P:32, :, :].bitcast(I32), in_=sv[i])
 
         turned = {}
-        kin = {}
+        taken = {}
         cg = {}
 
         def turn(t, a, first_u=0, count=U):
             h, j = divmod(t, J)
-            tile, first = zg[t, WIDE * a]
-            b = bank(f"gt{t}{a}{first_u}", [P, count * 4, 2, NT], BF16)
-            last = H * U * J
+            b = bank(f"gt{t}{a}{first_u}", [P, count * J, 2, NT], BF16)
             for u in range(count):
-                i = U * J * h + J * (first_u + u) + j
-                for k in range(4):
+                row = U * J * h + J * (first_u + u) + j
+                for i in range(J):
                     nc.tensor.matmul(
-                        b[:, 4 * u + k, :, :],
-                        lhsT=tile[:, first_u + u, first + k : first + WIDE : 4],
-                        rhs=table[:, i : last + 1 : last - i, :],
+                        b[:, J * u + i, :, :],
+                        lhsT=zg[t][:, first_u + u, WIDE * a + i : WIDE * (a + 1) : J],
+                        rhs=table[:, row : GATE_ROWS + 1 : GATE_ROWS - row, :],
                         start=True,
                         stop=True,
                     )
             turned[t, a, first_u] = (b, count)
 
         def take(t, a, engine, first_u=0):
-            if t not in kin:
-                kin[t] = work.tile([P, A, 2 * NT, U * 4], BF16, name=f"kin{t}", tag="kin", bufs=3, align_bytes=64)
+            if t not in taken:
+                taken[t] = work.tile([P, A, 2 * NT, U * J], BF16, name=f"taken{t}", tag="taken", bufs=TAKE_BUFS, align_bytes=64)
             b, count = turned[t, a, first_u]
-            copy(engine, kin[t][:, a, :, 4 * first_u : 4 * (first_u + count)], b[:].rearrange("p s c n -> p (c n) s"))
+            copy(engine, taken[t][:, a, :, J * first_u : J * (first_u + count)], b[:].rearrange("p s c n -> p (c n) s"))
             emptied(f"gt{t}{a}{first_u}")
-
-        def turn_take(t, e0="s", e1="s"):
-            turn(t, 0)
-            take(t, 0, e0)
-            turn(t, 1)
-            take(t, 1, e1)
 
         def quantise(dst, scales, src):
             nc.vector.quantize_mx(out=dst.bitcast(FP8X4), scales=scales, in_=src)
 
-        def quantise_cg(t, first=0, count=A):
-            if t not in cg:
-                q = keep.tile([P, A * 2 * P], U32, name=f"cgq{t}", align_bytes=64)
-                s = keep.tile([P, A * 2 * P], U8, name=f"cgs{t}", align_bytes=64)
-                cg[t] = (q, s)
-            q, s = cg[t]
-            cols = slice(2 * P * first, 2 * P * (first + count))
-            src = kin[t][:, first : first + count, :, :]
-            quantise(q[:, cols], s[:, cols], src.rearrange("p a n s -> p (a n s)"))
+        def quantise_cg(t):
+            codes = keep.tile([P, A * 2 * P], U32, name=f"cgq{t}", align_bytes=64)
+            scales = keep.tile([P, A * 2 * P], U8, name=f"cgs{t}", align_bytes=64)
+            cg[t] = (codes, scales)
+            quantise(codes[:], scales[:], taken[t][:].rearrange("p a n s -> p (a n s)"))
 
-        mp = {}
+        m_bank = {}
+        p_bank = {}
         mb = {}
         paired = {}
         woven = {}
 
         def passes(dst, key, t, first, width):
             codes, scales = cg[t]
-            words, at = w_sb[key, first]
             for a in range(A):
                 col = P * (2 * a + w_in[key][2])
                 nc.tensor.matmul_mx(
                     dst,
                     lhsT=codes[:, col : col + P].bitcast(FP8X4),
                     lhsT_scale=scales[:, col : col + P],
-                    rhs=words[:, a, 2 * at : 2 * (at + width)].bitcast(FP4X4),
+                    rhs=w_sb[key][:, a, 2 * first : 2 * (first + width)].bitcast(FP4X4),
                     rhs_scale=w_sc[key][:, a, first : first + width],
                     start=(a == 0),
                     stop=(a == A - 1),
                 )
 
         def product_m(t, first, width=WIDE):
-            mp["m", t, first] = bank(f"m{t}_{first}", [P, width], F32)
-            passes(mp["m", t, first][:], "h", t, first, width)
+            m_bank[t, first] = bank(f"m{t}_{first}", [P, width], F32)
+            passes(m_bank[t, first][:], "wh", t, first, width)
 
         def product_p(t, qs=range(NQ)):
             k, i = divmod(t, 2)
             for q in qs:
-                if ("p", k, q) not in mp:
-                    mp["p", k, q] = bank(f"p{k}{q}", [P, 2, QW], F32)
-                passes(mp["p", k, q][:, i, :], "p", t, QW * q, QW)
+                if i == 0:
+                    p_bank[k, q] = bank(f"p{k}{q}", [P, 2, QW], F32)
+                passes(p_bank[k, q][:, i, :], "wp", t, QW * q, QW)
 
         def bias(t, first, width=WIDE):
             k, i = divmod(t, 2)
             c, at = divmod(first, WIDE)
             if (k, c) not in mb:
-                mb[k, c] = work.tile([P, 2, WIDE], F32, name=f"mb{k}{c}", tag="mb", bufs=5)
+                mb[k, c] = work.tile([P, 2, WIDE], F32, name=f"mb{k}{c}", tag="mb", bufs=M_BUFS)
             nc.vector.tensor_tensor(
                 out=mb[k, c][:, i, at : at + width],
-                in0=mp["m", t, first][:],
+                in0=m_bank[t, first][:],
                 in1=bh_bc[:, first : first + width],
                 op=ADD,
             )
             emptied(f"m{t}_{first}")
 
         def times(k, qs=range(NQ)):
-            h, r = divmod(k, 2)
+            h, second = divmod(k, 2)
             for q in qs:
-                if r == 0:
+                if not second:
                     paired[h, q] = keep.tile([P, 2, QW, 2], BF16, name=f"sp{h}{q}", align_bytes=64)
                 c, e = divmod(q, 2)
                 nc.vector.tensor_tensor(
-                    out=paired[h, q][:, r, :, :],
-                    in0=mp["p", k, q][:].rearrange("p i n -> p n i"),
+                    out=paired[h, q][:, second, :, :],
+                    in0=p_bank[k, q][:].rearrange("p i n -> p n i"),
                     in1=mb[k, c][:, :, QW * e : QW * (e + 1)].rearrange("p i n -> p n i"),
                     op=MULT,
                 )
                 emptied(f"p{k}{q}")
 
-        def weave_s(h, q, engine="s", chain=None):
-            tag, bufs = (chain, 1) if chain else ("sw", 5)
-            t = work.tile([P, QW, J], BF16, name=f"s{h}_{q}", tag=tag, bufs=bufs, align_bytes=64)
+        def weave_s(h, q, engine):
+            t = work.tile([P, QW, J], BF16, name=f"s{h}_{q}", tag="sw", bufs=S_BUFS, align_bytes=64)
             word = U32 if engine == "s" else I32
-            words = paired[h, q][:].rearrange("p r n i -> p r (n i)").bitcast(word)
-            copy(engine, t[:].bitcast(word), words.rearrange("p r n -> p n r"))
+            words = paired[h, q][:].rearrange("p k n i -> p k (n i)").bitcast(word)
+            copy(engine, t[:].bitcast(word), words.rearrange("p k n -> p n k"))
             woven["s", h, q] = t
 
         x_slots = {}
 
-        def widen(h, c, engine, slots=range(J), at=0, width=WIDE):
-            if (h, c) not in x_slots:
-                x_slots[h, c] = keep.tile([P, J, WIDE], BF16, name=f"xw{h}{c}")
+        def widen(h, first, slots=range(J)):
+            if (h, first) not in x_slots:
+                x_slots[h, first] = keep.tile([P, J, WIDE], BF16, name=f"xw{h}{first // WIDE}")
             for j in slots:
-                dst = x_slots[h, c][:, j, at : at + width]
-                t, first = x_sb[h, j]
-                src = t[:, first + WIDE * c + at : first + WIDE * c + at + width].bitcast(FP8)
-                scale = xs_sb[:, h, j : j + 1]
-                if engine == "s":
-                    nc.scalar.activation(out=dst, in_=src, func=COPY, scale=scale)
-                else:
-                    nc.vector.tensor_scalar(out=dst, in0=src, scalar1=scale, scalar2=None, op0=MULT)
+                nc.scalar.activation(
+                    out=x_slots[h, first][:, j, :],
+                    in_=x_sb[h][:, D * j + first : D * j + first + WIDE].bitcast(FP8),
+                    func=COPY,
+                    scale=xs_sb[:, h, j : j + 1],
+                )
 
-        def weave_x(h, q, engine, chain=None):
-            src = x_slots[h, q // 2][:, :, QW * (q % 2) : QW * (q % 2 + 1)]
-            tag, bufs = (chain, 1) if chain else ("xw", 4)
+        def weave_x(h, q, engine, tag="xw"):
+            c, e = divmod(q, 2)
+            src = x_slots[h, WIDE * c][:, :, QW * e : QW * (e + 1)]
+            bufs = 1 if tag == CHAIN else X_BUFS
             t = work.tile([P, QW, J], BF16, name=f"x{h}_{q}", tag=tag, bufs=bufs, align_bytes=64)
             if engine == "g":
                 copy(engine, t[:], src.rearrange("p j n -> p n j"))
             else:
-                copy(engine, t[:].rearrange("p (c i) j -> p c j i", i=4), src.rearrange("p j (c i) -> p c j i", i=4))
+                copy(engine, t[:].rearrange("p (b n) j -> p b j n", n=4), src.rearrange("p j (b n) -> p b j n", n=4))
             woven["x", h, q] = t
 
         codes_t = {}
         for key in ("x", "s"):
             for h in range(H):
-                cq = keep.tile([P, D], U32, name=f"{key}q{h}", align_bytes=64)
-                cs = keep.tile([P, D], U8, name=f"{key}s{h}", align_bytes=64)
-                codes_t[key, h] = (cq, cs)
+                codes_t[key, h] = (
+                    keep.tile([P, D], U32, name=f"{key}q{h}", align_bytes=64),
+                    keep.tile([P, D], U8, name=f"{key}s{h}", align_bytes=64),
+                )
 
         def quantise_t(key, h, q):
-            cq, cs = codes_t[key, h]
+            codes, scales = codes_t[key, h]
             cols = slice(QW * q, QW * (q + 1))
-            quantise(cq[:, cols], cs[:, cols], woven[key, h, q][:].rearrange("p n t -> p (n t)"))
+            quantise(codes[:, cols], scales[:, cols], woven[key, h, q][:].rearrange("p n j -> p (n j)"))
 
-        staged = {}
-
-        def finish(first, width, r, engine, g0, group):
-            count = WIDE // width
-            name = f"o{first}_{r}"
-            b = bank(name, [P, count, width], F32)
-            cols = slice(first, first + width)
-            for i in range(count):
-                rows = slice(P * (count * r + i), P * (count * r + i + 1))
+        def finish(q, v, engine):
+            name = f"o{QW * q}_{v}"
+            b = bank(name, [P, 2, QW], F32)
+            cols = slice(QW * q, QW * (q + 1))
+            for i in range(2):
+                rows = slice(QW * v + P * i, QW * v + P * (i + 1))
                 for h in range(H):
-                    xq, xs = codes_t["x", h]
-                    sq, ss = codes_t["s", h]
+                    x_codes, x_scales = codes_t["x", h]
+                    s_codes, s_scales = codes_t["s", h]
                     nc.tensor.matmul_mx(
                         b[:, i, :],
-                        lhsT=xq[:, rows].bitcast(FP8X4),
-                        lhsT_scale=xs[:, rows],
-                        rhs=sq[:, cols].bitcast(FP8X4),
-                        rhs_scale=ss[:, cols],
+                        lhsT=x_codes[:, rows].bitcast(FP8X4),
+                        lhsT_scale=x_scales[:, rows],
+                        rhs=s_codes[:, cols].bitcast(FP8X4),
+                        rhs_scale=s_scales[:, cols],
                         start=(h == 0),
                         stop=(h == H - 1),
                     )
-            i = r - g0
-            if i == 0:
-                staged[first, g0] = work.tile([P, group * count, width], F32, name=f"ob{first}_{g0}", tag="big", bufs=8, align_bytes=64)
-            t = staged[first, g0]
-            dst = t[:, count * i : count * (i + 1), :]
+            t = work.tile([P, 2, QW], F32, name=f"ob{QW * q}_{v}", tag="big", bufs=BIG_BUFS, align_bytes=64)
             if engine == "s":
-                nc.scalar.activation(out=dst, in_=b[:], func=COPY, scale=1.0 / 32.0)
+                nc.scalar.activation(out=t[:], in_=b[:], func=COPY, scale=OUT_SCALE)
             else:
-                nc.vector.tensor_scalar(out=dst, in0=b[:], scalar1=1.0 / 32.0, scalar2=None, op0=MULT)
+                nc.vector.tensor_scalar(out=t[:], in0=b[:], scalar1=OUT_SCALE, scalar2=None, op0=MULT)
             emptied(name)
-            if i == group - 1:
-                rows = out[P * count * g0 : P * count * (g0 + group), cols]
-                nc.sync.dma_start(out=rows.rearrange("(i p) n -> p i n", p=P), in_=t[:])
-
-        constants()
-        load_gates()
-        load_zg(0, (0, 1))
-        load_bias()
-        load_zg(0, (2, 3))
-        load_w_scales("h", nc.gpsimd, (0, 1))
-        load_w_scales("p", nc.gpsimd)
-        load_xs()
-        load_zg(1)
-        load_w_scales("h", nc.sync, (2, 3))
-        load_w("h")
-        load_zg(2)
-        load_w("p")
-        load_x(0)
-        load_zg(3)
-        load_zg(4)
-        load_x(1)
-        for t in (5, 6, 7):
-            load_zg(t)
-        make_tables()
+            nc.sync.dma_start(out=out[QW * v : QW * (v + 1), cols].rearrange("(i p) n -> p i n", p=P), in_=t[:])
 
         def turn_both(t):
             for a in range(A):
                 turn(t, a)
+
+        def turn_take_halves(t):
+            for a in range(A):
+                for first_u in (0, U // 2):
+                    turn(t, a, first_u, U // 2)
+            for a in range(A):
+                take(t, a, "s", 0)
+                take(t, a, "v", U // 2)
 
         def pair_p(k, qs):
             for q in qs:
@@ -377,20 +341,33 @@ def tile_focalmodulationqueryweightgrad_w4_kernel(
                     product_p(2 * k + i, (q,))
 
         def both_m(t):
-            for first in (0, WIDE):
+            for first in (LEFT, RIGHT):
                 product_m(t, first)
 
         def both_bias(t):
-            for first in (0, WIDE):
+            for first in (LEFT, RIGHT):
                 bias(t, first)
 
-        def turn_take_halves(t):
-            for a in range(A):
-                for first_u in (0, 2):
-                    turn(t, a, first_u, 2)
-            for a in range(A):
-                take(t, a, "s", 0)
-                take(t, a, "v", 2)
+        constants()
+        load_gates()
+        load_zg(0, (0, 1))
+        load_bias()
+        load_zg(0, (2, 3))
+        load_w_scales("wh", nc.gpsimd, (0, 1))
+        load_w_scales("wp", nc.gpsimd)
+        load_xs()
+        load_zg(1)
+        load_w_scales("wh", nc.sync, (2, 3))
+        load_w("wh")
+        load_zg(2)
+        load_w("wp")
+        load_x(0)
+        load_zg(3)
+        load_zg(4)
+        load_x(1)
+        for t in range(5, H * J):
+            load_zg(t)
+        make_table()
 
         turn_take_halves(0)
         spread_bias()
@@ -403,125 +380,131 @@ def tile_focalmodulationqueryweightgrad_w4_kernel(
         both_bias(1)
         turn_take_halves(2)
         pair_p(0, range(NQ))
-        widen(0, 0, "s")
-        widen(0, 1, "s", (0,))
+        widen(0, LEFT)
+        widen(0, RIGHT, (0,))
         times(0, (0,))
         quantise_cg(2)
         times(0, (1, 2, 3))
+
         both_m(2)
-        weave_x(0, 0, "v")
-        bias(2, 0)
+        weave_x(0, 0, "g")
+        bias(2, LEFT)
         turn_take_halves(3)
         product_p(2)
-        widen(0, 1, "s", (1, 2, 3))
-        bias(2, WIDE)
+        widen(0, RIGHT, (1, 2, 3))
+        bias(2, RIGHT)
         quantise_cg(3)
         turn_both(4)
-        weave_x(0, 1, "v", "ga")
+        weave_x(0, 1, "v", CHAIN)
         quantise_t("x", 0, 0)
         quantise_t("x", 0, 1)
-        weave_x(0, 2, "g", "ga")
+        weave_x(0, 2, "g", CHAIN)
         take(4, 0, "s")
         both_m(3)
         take(4, 1, "s")
         product_p(3)
         both_bias(3)
-        widen(1, 0, "s", (0, 1))
+        widen(1, LEFT, (0, 1))
         times(1, (0,))
         turn_both(5)
-        times(1, (1,))
         quantise_cg(4)
         quantise_t("x", 0, 2)
-        weave_x(0, 3, "g", "ga")
+        weave_x(0, 3, "g", CHAIN)
+        times(1, (1,))
         times(1, (2,))
+
         both_m(4)
         weave_s(0, 0, "s")
         take(5, 0, "s")
         times(1, (3,))
         product_p(4, (0, 1))
-        bias(4, 0)
+        bias(4, LEFT)
         take(5, 1, "s")
         turn_both(6)
-        widen(1, 0, "s", (2, 3))
+        widen(1, LEFT, (2, 3))
         weave_s(0, 1, "v")
         quantise_cg(5)
         take(6, 0, "s")
-        product_m(5, 0)
+        product_m(5, LEFT)
         product_p(5, (0, 1))
         quantise_t("s", 0, 0)
-        quantise_t("s", 0, 1)
         quantise_t("x", 0, 3)
-        weave_x(1, 0, "g", "ga")
+        weave_x(1, 0, "g", CHAIN)
         take(6, 1, "s")
-        bias(4, WIDE)
-        bias(5, 0)
-        turn(7, 0, 0, 2)
-        turn(7, 0, 2, 2)
+        bias(4, RIGHT)
+        bias(5, LEFT)
+
+        turn(7, 0, 0, U // 2)
+        turn(7, 0, U // 2, U // 2)
         times(2, (0,))
-        turn(7, 1, 0, 2)
-        turn(7, 1, 2, 2)
+        turn(7, 1, 0, U // 2)
+        turn(7, 1, U // 2, U // 2)
         take(7, 0, "s", 0)
         quantise_cg(6)
         take(7, 1, "s", 0)
-        take(7, 0, "s", 2)
-        product_m(5, WIDE)
+        take(7, 0, "s", U // 2)
+        product_m(5, RIGHT)
         times(2, (1,))
-        take(7, 1, "v", 2)
-        product_m(6, 0)
+        take(7, 1, "v", U // 2)
+        quantise_t("s", 0, 1)
+        product_m(6, LEFT)
         product_p(6, (0, 1))
-        widen(1, 1, "s")
+        widen(1, RIGHT)
         pair_p(2, (2,))
         quantise_cg(7)
         quantise_t("x", 1, 0)
-        weave_x(1, 1, "g", "ga")
+        weave_x(1, 1, "g", CHAIN)
         weave_x(1, 2, "s")
         weave_x(1, 3, "s")
         weave_s(0, 2, "s")
-        product_m(7, 0, QW)
+
+        product_m(7, LEFT, QW)
         product_p(7, (0,))
-        bias(6, 0)
+        bias(6, LEFT)
         product_m(7, QW, QW)
         product_p(7, (1,))
-        bias(7, 0, QW)
+        bias(7, LEFT, QW)
         times(3, (0,))
-        product_m(6, WIDE)
+        product_m(6, RIGHT)
         bias(7, QW, QW)
         weave_s(1, 0, "v")
-        product_m(7, WIDE)
+        product_m(7, RIGHT)
         quantise_t("x", 1, 1)
         quantise_t("s", 1, 0)
         pair_p(3, (2,))
         times(3, (1,))
-        finish(0, QW, 0, "s", 0, 1)
+
+        finish(0, 0, "s")
         quantise_t("x", 1, 2)
         weave_s(1, 1, "v")
         quantise_t("x", 1, 3)
-        finish(0, QW, 1, "s", 1, 1)
+        finish(0, 1, "s")
         quantise_t("s", 1, 1)
-        bias(5, WIDE)
-        finish(0, QW, 2, "s", 2, 1)
-        bias(6, WIDE)
-        finish(0, QW, 3, "s", 3, 1)
+        bias(5, RIGHT)
+        finish(0, 2, "s")
+        bias(6, RIGHT)
+        finish(0, 3, "s")
         pair_p(2, (3,))
-        bias(7, WIDE)
+        bias(7, RIGHT)
         weave_s(0, 3, "s")
         times(2, (2,))
-        finish(QW, QW, 0, "s", 0, 1)
+        finish(1, 0, "s")
         times(3, (2,))
-        finish(QW, QW, 1, "s", 1, 1)
+        finish(1, 1, "s")
         pair_p(3, (3,))
         quantise_t("s", 0, 2)
         weave_s(1, 2, "v")
-        times(2, (3,))
-        finish(QW, QW, 2, "s", 2, 1)
-        quantise_t("s", 1, 2)
-        times(3, (3,))
-        finish(QW, QW, 3, "s", 3, 1)
         quantise_t("s", 0, 3)
+        quantise_t("s", 1, 2)
+        finish(1, 2, "s")
+        times(2, (3,))
+        times(3, (3,))
+        finish(1, 3, "s")
         weave_s(1, 3, "v")
-        finish(2 * QW, QW, 0, "s", 0, 1)
+        finish(2, 0, "s")
         quantise_t("s", 1, 3)
-        for rp in range(1, 4):
-            finish(2 * QW, QW, rp, "s" if rp % 2 else "v", rp, 1)
-        for rp in range(4):
-            finish(3 * QW, QW, rp, "s" if rp % 2 else "v", rp, 1)
+
+        for v in range(1, NQ):
+            finish(2, v, "s" if v % 2 else "v")
+        for v in range(NQ):
+            finish(3, v, "s" if v % 2 else "v")

from contextlib import ExitStack

import concourse.mybir as mybir
from concourse.masks import make_identity

F32 = mybir.dt.float32
BF16 = mybir.dt.bfloat16
U32 = mybir.dt.uint32
I32 = mybir.dt.int32
U8 = mybir.dt.uint8
FP8 = mybir.dt.float8_e4m3fn
FP8X4 = mybir.dt.float8_e4m3fn_x4
FP4X4 = mybir.dt.float4_e2m1fn_x4
MULT = mybir.AluOpType.mult
ADD = mybir.AluOpType.add
COPY = mybir.ActivationFunctionType.Copy

T = 1024
D = 1024
L = 3
P = 128
J = 4
H = 2
A = 2
U = 4
NT = 32
QW = 256
NQ = D // QW
WIDE = 512
LEFT, RIGHT = 0, WIDE
BANKS = 8
GATE_ROWS = H * U * J
OUT_SCALE = 1.0 / 32.0
CHAIN = "chain"
BIG_BUFS = H * J
TAKE_BUFS = 3
M_BUFS = 5
S_BUFS = 5
X_BUFS = 4

FLOPS = 3 * 2 * T * D * D + 2 * L * T * D + 2 * T * D


def tile_focalmodulationqueryweightgrad_w4_kernel(
    tc, x_bytes, x_scale, z, gates, wh_words, wh_scales, bh, wp_words, wp_scales, g, out
):
    nc = tc.nc
    with ExitStack() as ctx:
        keep = ctx.enter_context(tc.tile_pool(name="keep", bufs=1))
        work = ctx.enter_context(tc.tile_pool(name="work", bufs=2))
        psum = ctx.enter_context(tc.psum_pool(name="psum", bufs=1))
        ctx.enter_context(tc.manual_schedule())

        raw_gates = keep.tile([P, GATE_ROWS, L], BF16, name="raw_gates")
        bh_row = keep.tile([P, D], BF16, name="bh_row")
        w_sc = {key: keep.tile([P, A, D], U8, name=f"scales_{key}", align_bytes=64) for key in ("wh", "wp")}
        padded = keep.tile([P, P + L + 1], BF16, name="padded")
        ident = padded[:, 0:P]
        ones = keep.tile([P, P], BF16, name="ones")
        block = keep.tile([P, NT], F32, name="block")
        table = keep.tile([P, GATE_ROWS + 1, NT], BF16, name="table")
        xs_sb = keep.tile([P, H, J], F32, name="xs_sb")
        bh_bc = keep.tile([P, D], BF16, name="bh_bc")

        empty = list(range(BANKS))
        held = {}

        def bank(name, shape, dtype):
            n = empty.pop(0)
            held[name] = n
            return psum.tile(shape, dtype, name=name, tag=f"bank{n}")

        def emptied(name):
            empty.append(held[name])

        def constants():
            nc.gpsimd.memset(raw_gates[:], 0.0)
            nc.vector.memset(bh_row[:], 0.0)
            nc.vector.memset(ones[:], 1.0)
            for key in w_sc:
                nc.vector.memset(w_sc[key][:].rearrange("p s n -> p (s n)").bitcast(I32), 0)
            nc.gpsimd.memset(padded[:, P:], 0.0)
            make_identity(nc, ident)
            nc.vector.tensor_reduce(
                out=block[:], in_=ident.rearrange("p (n l) -> p n l", l=L + 1), axis=mybir.AxisListType.X, op=ADD
            )
            nc.vector.tensor_copy(out=table[:, GATE_ROWS, :], in_=ident[:, L : P : L + 1])

        def load_gates():
            nc.sync.dma_start(
                out=raw_gates[L : P : L + 1, :, :].rearrange("n (h r) l -> n h (r l)", h=H),
                in_=gates.rearrange("(h n r) l -> n h (r l)", h=H, r=U * J),
            )

        def load_bias():
            nc.sync.dma_start(out=bh_row[0:1, :], in_=bh.rearrange("(o n) -> o n", o=1))

        def load_xs():
            nc.gpsimd.dma_start(out=xs_sb[:], in_=x_scale.rearrange("(h r j) o -> r h (j o)", h=H, j=J))

        def make_table():
            b = bank("gates", [P, GATE_ROWS], F32)
            for l in range(L):
                nc.tensor.matmul(
                    b[:], lhsT=padded[:, L - l : P + L - l], rhs=raw_gates[:, :, l], start=(l == 0), stop=(l == L - 1)
                )
            for h in range(H):
                rows = slice(U * J * h, U * J * (h + 1))
                nc.vector.tensor_tensor(
                    out=table[:, rows, :],
                    in0=b[:, rows].unsqueeze(2).to_broadcast([P, U * J, NT]),
                    in1=block[:].unsqueeze(1).to_broadcast([P, U * J, NT]),
                    op=MULT,
                )
            emptied("gates")

        def copy(engine, dst, src):
            if engine == "s":
                nc.scalar.copy(out=dst, in_=src)
            elif engine == "v":
                nc.vector.tensor_copy(out=dst, in_=src)
            else:
                nc.gpsimd.tensor_scalar(out=dst, in0=src, scalar1=1.0, scalar2=0.0, op0=MULT, op1=ADD)

        def spread_bias():
            b = bank("bias", [P, D], BF16)
            for first in (LEFT, RIGHT):
                cols = slice(first, first + WIDE)
                nc.tensor.matmul(b[:, cols], lhsT=ones[:], rhs=bh_row[:, cols], start=True, stop=True)
            copy("s", bh_bc[:], b[:])
            emptied("bias")

        rows_of = [z[l].rearrange("(h n u j) d -> h n u (j d)", h=H, u=U, j=J) for l in range(L)]
        rows_of.append(g.rearrange("(h n u j) d -> h n u (j d)", h=H, u=U, j=J))
        zg = {}

        def load_zg(t, levels=range(L + 1)):
            h, j = divmod(t, J)
            if t not in zg:
                zg[t] = work.tile([P, U, D], BF16, name=f"zg{t}", tag="big", bufs=BIG_BUFS, align_bytes=64)
            for l in levels:
                nc.sync.dma_start(out=zg[t][l : P : L + 1, :, :], in_=rows_of[l][h][:, :, D * j : D * (j + 1)])

        x_view = x_bytes.rearrange("(h r j) n -> h r (j n)", h=H, j=J)
        x_sb = {}

        def load_x(h):
            x_sb[h] = keep.tile([P, J * D], U8, name=f"x_sb{h}", align_bytes=64)
            nc.sync.dma_start(out=x_sb[h][:], in_=x_view[h])

        w_in = {"wh": (wh_words, wh_scales, 0), "wp": (wp_words, wp_scales, 1)}
        w_sb = {}

        def load_w(key):
            w_sb[key] = keep.tile([P, A, 2 * D], U8, name=f"words_{key}", align_bytes=64)
            nc.sync.dma_start(out=w_sb[key][:].bitcast(I32), in_=w_in[key][0].bitcast(I32).rearrange("a p n -> p a n"))

        def load_w_scales(key, queue, rows=range(4)):
            sv = w_in[key][1].bitcast(I32).rearrange("a (q i) n -> i q a n", i=4)
            for i in rows:
                queue.dma_start(out=w_sc[key][i:P:32, :, :].bitcast(I32), in_=sv[i])

        turned = {}
        taken = {}
        cg = {}

        def turn(t, a, first_u=0, count=U):
            h, j = divmod(t, J)
            b = bank(f"gt{t}{a}{first_u}", [P, count * J, 2, NT], BF16)
            for u in range(count):
                row = U * J * h + J * (first_u + u) + j
                for i in range(J):
                    nc.tensor.matmul(
                        b[:, J * u + i, :, :],
                        lhsT=zg[t][:, first_u + u, WIDE * a + i : WIDE * (a + 1) : J],
                        rhs=table[:, row : GATE_ROWS + 1 : GATE_ROWS - row, :],
                        start=True,
                        stop=True,
                    )
            turned[t, a, first_u] = (b, count)

        def take(t, a, engine, first_u=0):
            if t not in taken:
                taken[t] = work.tile([P, A, 2 * NT, U * J], BF16, name=f"taken{t}", tag="taken", bufs=TAKE_BUFS, align_bytes=64)
            b, count = turned[t, a, first_u]
            copy(engine, taken[t][:, a, :, J * first_u : J * (first_u + count)], b[:].rearrange("p s c n -> p (c n) s"))
            emptied(f"gt{t}{a}{first_u}")

        def quantise(dst, scales, src):
            nc.vector.quantize_mx(out=dst.bitcast(FP8X4), scales=scales, in_=src)

        def quantise_cg(t):
            codes = keep.tile([P, A * 2 * P], U32, name=f"cgq{t}", align_bytes=64)
            scales = keep.tile([P, A * 2 * P], U8, name=f"cgs{t}", align_bytes=64)
            cg[t] = (codes, scales)
            quantise(codes[:], scales[:], taken[t][:].rearrange("p a n s -> p (a n s)"))

        m_bank = {}
        p_bank = {}
        mb = {}
        paired = {}
        woven = {}

        def passes(dst, key, t, first, width):
            codes, scales = cg[t]
            for a in range(A):
                col = P * (2 * a + w_in[key][2])
                nc.tensor.matmul_mx(
                    dst,
                    lhsT=codes[:, col : col + P].bitcast(FP8X4),
                    lhsT_scale=scales[:, col : col + P],
                    rhs=w_sb[key][:, a, 2 * first : 2 * (first + width)].bitcast(FP4X4),
                    rhs_scale=w_sc[key][:, a, first : first + width],
                    start=(a == 0),
                    stop=(a == A - 1),
                )

        def product_m(t, first, width=WIDE):
            m_bank[t, first] = bank(f"m{t}_{first}", [P, width], F32)
            passes(m_bank[t, first][:], "wh", t, first, width)

        def product_p(t, qs=range(NQ)):
            k, i = divmod(t, 2)
            for q in qs:
                if i == 0:
                    p_bank[k, q] = bank(f"p{k}{q}", [P, 2, QW], F32)
                passes(p_bank[k, q][:, i, :], "wp", t, QW * q, QW)

        def bias(t, first, width=WIDE):
            k, i = divmod(t, 2)
            c, at = divmod(first, WIDE)
            if (k, c) not in mb:
                mb[k, c] = work.tile([P, 2, WIDE], F32, name=f"mb{k}{c}", tag="mb", bufs=M_BUFS)
            nc.vector.tensor_tensor(
                out=mb[k, c][:, i, at : at + width],
                in0=m_bank[t, first][:],
                in1=bh_bc[:, first : first + width],
                op=ADD,
            )
            emptied(f"m{t}_{first}")

        def times(k, qs=range(NQ)):
            h, second = divmod(k, 2)
            for q in qs:
                if not second:
                    paired[h, q] = keep.tile([P, 2, QW, 2], BF16, name=f"sp{h}{q}", align_bytes=64)
                c, e = divmod(q, 2)
                nc.vector.tensor_tensor(
                    out=paired[h, q][:, second, :, :],
                    in0=p_bank[k, q][:].rearrange("p i n -> p n i"),
                    in1=mb[k, c][:, :, QW * e : QW * (e + 1)].rearrange("p i n -> p n i"),
                    op=MULT,
                )
                emptied(f"p{k}{q}")

        def weave_s(h, q, engine):
            t = work.tile([P, QW, J], BF16, name=f"s{h}_{q}", tag="sw", bufs=S_BUFS, align_bytes=64)
            word = U32 if engine == "s" else I32
            words = paired[h, q][:].rearrange("p k n i -> p k (n i)").bitcast(word)
            copy(engine, t[:].bitcast(word), words.rearrange("p k n -> p n k"))
            woven["s", h, q] = t

        x_slots = {}

        def widen(h, first, slots=range(J)):
            if (h, first) not in x_slots:
                x_slots[h, first] = keep.tile([P, J, WIDE], BF16, name=f"xw{h}{first // WIDE}")
            for j in slots:
                nc.scalar.activation(
                    out=x_slots[h, first][:, j, :],
                    in_=x_sb[h][:, D * j + first : D * j + first + WIDE].bitcast(FP8),
                    func=COPY,
                    scale=xs_sb[:, h, j : j + 1],
                )

        def weave_x(h, q, engine, tag="xw"):
            c, e = divmod(q, 2)
            src = x_slots[h, WIDE * c][:, :, QW * e : QW * (e + 1)]
            bufs = 1 if tag == CHAIN else X_BUFS
            t = work.tile([P, QW, J], BF16, name=f"x{h}_{q}", tag=tag, bufs=bufs, align_bytes=64)
            if engine == "g":
                copy(engine, t[:], src.rearrange("p j n -> p n j"))
            else:
                copy(engine, t[:].rearrange("p (b n) j -> p b j n", n=4), src.rearrange("p j (b n) -> p b j n", n=4))
            woven["x", h, q] = t

        codes_t = {}
        for key in ("x", "s"):
            for h in range(H):
                codes_t[key, h] = (
                    keep.tile([P, D], U32, name=f"{key}q{h}", align_bytes=64),
                    keep.tile([P, D], U8, name=f"{key}s{h}", align_bytes=64),
                )

        def quantise_t(key, h, q):
            codes, scales = codes_t[key, h]
            cols = slice(QW * q, QW * (q + 1))
            quantise(codes[:, cols], scales[:, cols], woven[key, h, q][:].rearrange("p n j -> p (n j)"))

        def finish(q, v, engine):
            name = f"o{QW * q}_{v}"
            b = bank(name, [P, 2, QW], F32)
            cols = slice(QW * q, QW * (q + 1))
            for i in range(2):
                rows = slice(QW * v + P * i, QW * v + P * (i + 1))
                for h in range(H):
                    x_codes, x_scales = codes_t["x", h]
                    s_codes, s_scales = codes_t["s", h]
                    nc.tensor.matmul_mx(
                        b[:, i, :],
                        lhsT=x_codes[:, rows].bitcast(FP8X4),
                        lhsT_scale=x_scales[:, rows],
                        rhs=s_codes[:, cols].bitcast(FP8X4),
                        rhs_scale=s_scales[:, cols],
                        start=(h == 0),
                        stop=(h == H - 1),
                    )
            t = work.tile([P, 2, QW], F32, name=f"ob{QW * q}_{v}", tag="big", bufs=BIG_BUFS, align_bytes=64)
            if engine == "s":
                nc.scalar.activation(out=t[:], in_=b[:], func=COPY, scale=OUT_SCALE)
            else:
                nc.vector.tensor_scalar(out=t[:], in0=b[:], scalar1=OUT_SCALE, scalar2=None, op0=MULT)
            emptied(name)
            nc.sync.dma_start(out=out[QW * v : QW * (v + 1), cols].rearrange("(i p) n -> p i n", p=P), in_=t[:])

        def turn_both(t):
            for a in range(A):
                turn(t, a)

        def turn_take_halves(t):
            for a in range(A):
                for first_u in (0, U // 2):
                    turn(t, a, first_u, U // 2)
            for a in range(A):
                take(t, a, "s", 0)
                take(t, a, "v", U // 2)

        def pair_p(k, qs):
            for q in qs:
                for i in range(2):
                    product_p(2 * k + i, (q,))

        def both_m(t):
            for first in (LEFT, RIGHT):
                product_m(t, first)

        def both_bias(t):
            for first in (LEFT, RIGHT):
                bias(t, first)

        constants()
        load_gates()
        load_zg(0, (0, 1))
        load_bias()
        load_zg(0, (2, 3))
        load_w_scales("wh", nc.gpsimd, (0, 1))
        load_w_scales("wp", nc.gpsimd)
        load_xs()
        load_zg(1)
        load_w_scales("wh", nc.sync, (2, 3))
        load_w("wh")
        load_zg(2)
        load_w("wp")
        load_x(0)
        load_zg(3)
        load_zg(4)
        load_x(1)
        for t in range(5, H * J):
            load_zg(t)
        make_table()

        turn_take_halves(0)
        spread_bias()
        quantise_cg(0)
        turn_take_halves(1)
        both_m(0)
        quantise_cg(1)
        both_bias(0)
        both_m(1)
        both_bias(1)
        turn_take_halves(2)
        pair_p(0, range(NQ))
        widen(0, LEFT)
        widen(0, RIGHT, (0,))
        times(0, (0,))
        quantise_cg(2)
        times(0, (1, 2, 3))

        both_m(2)
        weave_x(0, 0, "g")
        bias(2, LEFT)
        turn_take_halves(3)
        product_p(2)
        widen(0, RIGHT, (1, 2, 3))
        bias(2, RIGHT)
        quantise_cg(3)
        turn_both(4)
        weave_x(0, 1, "v", CHAIN)
        quantise_t("x", 0, 0)
        quantise_t("x", 0, 1)
        weave_x(0, 2, "g", CHAIN)
        take(4, 0, "s")
        both_m(3)
        take(4, 1, "s")
        product_p(3)
        both_bias(3)
        widen(1, LEFT, (0, 1))
        times(1, (0,))
        turn_both(5)
        quantise_cg(4)
        quantise_t("x", 0, 2)
        weave_x(0, 3, "g", CHAIN)
        times(1, (1,))
        times(1, (2,))

        both_m(4)
        weave_s(0, 0, "s")
        take(5, 0, "s")
        times(1, (3,))
        product_p(4, (0, 1))
        bias(4, LEFT)
        take(5, 1, "s")
        turn_both(6)
        widen(1, LEFT, (2, 3))
        weave_s(0, 1, "v")
        quantise_cg(5)
        take(6, 0, "s")
        product_m(5, LEFT)
        product_p(5, (0, 1))
        quantise_t("s", 0, 0)
        quantise_t("x", 0, 3)
        weave_x(1, 0, "g", CHAIN)
        take(6, 1, "s")
        bias(4, RIGHT)
        bias(5, LEFT)

        turn(7, 0, 0, U // 2)
        turn(7, 0, U // 2, U // 2)
        times(2, (0,))
        turn(7, 1, 0, U // 2)
        turn(7, 1, U // 2, U // 2)
        take(7, 0, "s", 0)
        quantise_cg(6)
        take(7, 1, "s", 0)
        take(7, 0, "s", U // 2)
        product_m(5, RIGHT)
        times(2, (1,))
        take(7, 1, "v", U // 2)
        quantise_t("s", 0, 1)
        product_m(6, LEFT)
        product_p(6, (0, 1))
        widen(1, RIGHT)
        pair_p(2, (2,))
        quantise_cg(7)
        quantise_t("x", 1, 0)
        weave_x(1, 1, "g", CHAIN)
        weave_x(1, 2, "s")
        weave_x(1, 3, "s")
        weave_s(0, 2, "s")

        product_m(7, LEFT, QW)
        product_p(7, (0,))
        bias(6, LEFT)
        product_m(7, QW, QW)
        product_p(7, (1,))
        bias(7, LEFT, QW)
        times(3, (0,))
        product_m(6, RIGHT)
        bias(7, QW, QW)
        weave_s(1, 0, "v")
        product_m(7, RIGHT)
        quantise_t("x", 1, 1)
        quantise_t("s", 1, 0)
        pair_p(3, (2,))
        times(3, (1,))

        finish(0, 0, "s")
        quantise_t("x", 1, 2)
        weave_s(1, 1, "v")
        quantise_t("x", 1, 3)
        finish(0, 1, "s")
        quantise_t("s", 1, 1)
        bias(5, RIGHT)
        finish(0, 2, "s")
        bias(6, RIGHT)
        finish(0, 3, "s")
        pair_p(2, (3,))
        bias(7, RIGHT)
        weave_s(0, 3, "s")
        times(2, (2,))
        finish(1, 0, "s")
        times(3, (2,))
        finish(1, 1, "s")
        pair_p(3, (3,))
        quantise_t("s", 0, 2)
        weave_s(1, 2, "v")
        quantise_t("s", 0, 3)
        quantise_t("s", 1, 2)
        finish(1, 2, "s")
        times(2, (3,))
        times(3, (3,))
        finish(1, 3, "s")
        weave_s(1, 3, "v")
        finish(2, 0, "s")
        quantise_t("s", 1, 3)

        for v in range(1, NQ):
            finish(2, v, "s" if v % 2 else "v")
        for v in range(NQ):
            finish(3, v, "s" if v % 2 else "v")
